import numpy as np, ml_dtypes
CORES = [83,85,87,115,117,119]
N = 6
BF = ml_dtypes.bfloat16
def gentries(a):
    return np.ascontiguousarray(a.reshape(8, 16, -1).transpose(0, 2, 1)).reshape(8, -1)
def gtable(e):
    e = np.asarray(e); return np.ascontiguousarray(e.reshape(8, -1, 16).transpose(0, 2, 1)).reshape(128, -1).astype(np.int32)
C, NV, LN, RO, LV = 3072, 1024, 96, 4, 2
H, L, B, S = NV // 2, 2 * LN, C - LN * RO, LN // N
def parts(rng):
    o = np.argsort(rng.random((N, 8, C)), axis=-1); h = np.zeros((N, 8, C), np.int64)
    np.put_along_axis(h, o, np.broadcast_to(np.arange(C) * 256 // C, (N, 8, C)), 2)
    x = np.clip(h[:, :, None] + rng.integers(-60, 61, (N, 8, 16, C)), 0, 255)
    cen = rng.random((N, 8, NV, 1)); wd = rng.choice(np.array([0.02, 0.1, 0.3, 1.0]), (N, 8, NV, 1))
    pos = np.clip(((cen + wd * (rng.random((N, 8, NV, 16)) - 0.5)) * C).astype(np.int64), 0, C - 1)
    ring = np.take_along_axis(o, pos.reshape(N, 8, -1), 2).reshape(N, 8, NV, 16)
    ring = np.where(rng.random(ring.shape) < 0.04, C, ring)
    kid = rng.integers(0, NV, (N, 8, 2, NV)); rt = rng.integers(0, NV, (N, 8, L)); fn = rng.integers(0, C, (N, 8, LN))
    xl = np.clip(rng.integers(0, 256, (N, 8, 1, LN)) + rng.integers(-60, 61, (N, 8, 16, LN)), 0, 255)
    snd = np.argsort(rng.random((N, 8, LN)), axis=-1)
    return x, ring, kid, rt, xl, fn, snd
def plant(rng, ring, rt, fn):
    n, g, i = np.indices((N, 8, LN)); v = rt[..., LN:]; k = rng.integers(0, 16, (N, 8, LN))
    m = rng.random((N, 8, LN)) < 0.7; ring[n[m], g[m], v[m], k[m]] = fn[m]
    m = rng.random((N, 8, LN)) < 0.4; ring[n[m], g[m], v[m] ^ H, 15 - k[m]] = fn[m]
def pack(x, ring, kid, rt, xl, fn, snd):
    return {"x": np.ascontiguousarray(np.reshape(x, (N, 128, C))).astype(np.float32).astype(BF), "ring": np.ascontiguousarray(ring.transpose(0, 1, 3, 2)).reshape(N, 128, NV).astype(np.int32),
            "kid": np.ascontiguousarray(kid).reshape(N, 16, NV).astype(np.int32), "rt": np.stack([gtable(a) for a in rt]), "xl": np.reshape(xl, (N, 128, LN)).astype(np.float32).astype(BF),
            "fn": np.stack([gtable(a) for a in fn]), "snd": np.stack([gtable(a) for a in snd])}
def edge(rng, shape, top, share):
    r = rng.random(shape)
    return np.where(r < share * 0.5, 0, np.where(r < share, top, rng.integers(0, top + 1, shape)))
def halves(rng, *shape):
    k = shape[:-2] + (1, shape[-1])
    return 255 * np.where(rng.random(k) < 0.5, rng.integers(0, 2, k), rng.integers(0, 2, shape))
def swaps(rng, n, g, x, ring, rt, xl, fn, but):
    p = np.concatenate([np.array([0]), rng.permutation(np.arange(1, H - 1))[:L - 2], np.array([H - 1])])
    r = p + H * rng.integers(0, 2, L); r[0] = 0; r[L - 1] = NV - 1; rt[n, g] = r
    x[n, g, :, 0] = 255; x[n, g, :, C - 1] = 0
    hi = rng.integers(0, 2, L); xl[n, g] = 255 * hi[:LN]; fn[n, g] = np.where(hi[LN:] == 1, 0, C - 1)
    ring[n, g, r] = np.where(hi == 1, C, 0)[:, None]; ring[n, g, r ^ H] = np.where(hi == 1, 0, C)[:, None]
    if but: ring[n, g, r[L // 2] ^ H] = ring[n, g, r[L // 2]].copy()
def again(rng, n, g, x, ring, kid, rt, xl, fn, snd):
    o = rng.permutation(H); r = o[:L] + H * rng.integers(0, 2, L); rt[n, g] = r; i = np.arange(LN); h = LN // 2
    gap = np.array([2, L - 2, L, L, L + 2, 2 * L])
    x[n, g, :, 0] = 255; x[n, g, :, 1:7] = (2040 + gap[None, :] // 2 + np.arange(16)[:, None]) // 16
    xl[n, g] = 255; fn[n, g] = np.where(i < h, 0, 1 + i % 6); snd[n, g, :S] = h + np.arange(S)
    good = np.concatenate([np.zeros(LN, np.int64), fn[n, g]])[:, None]
    ring[n, g, r] = C; ring[n, g, r ^ H] = good
    if LV == 2: kid[n, g][:, r] = r ^ H
    else:
        q = o[L:2 * L] + H * rng.integers(0, 2, L); ring[n, g, q] = C; ring[n, g, q ^ H] = good
        kid[n, g][:, r] = q; kid[n, g][:, q] = r ^ H
def setup_inputs(rng):
    x, ring, kid, rt, xl, fn, snd = parts(rng); plant(rng, ring, rt, fn)
    return pack(x, ring, kid, rt, xl, fn, snd)
def setup_inputs_spread(rng):
    x, ring, kid, rt, xl, fn, snd = parts(rng)
    x = np.minimum(np.exp2(8 * rng.random((N, 8, 1, C))) * rng.random((N, 8, 16, C)), 255).astype(np.int64)
    xl = np.minimum(np.exp2(8 * rng.random((N, 8, 1, LN))) * rng.random((N, 8, 16, LN)), 255).astype(np.int64)
    ring = rng.integers(0, C + 1, ring.shape); plant(rng, ring, rt, fn)
    return pack(x, ring, kid, rt, xl, fn, snd)
def setup_inputs_ends(rng):
    x, ring, kid, rt, xl, fn, snd = parts(rng)
    x = halves(rng, N, 8, 16, C); xl = halves(rng, N, 8, 16, LN); x[:, ::2, :, 0] = 255
    ring = edge(rng, ring.shape, C, 0.64); ring[:, :, 5::16, :15] = C; ring[:, :, 5::16, 15] = 0; ring[:, :, 10::16, :15] = 0; ring[:, :, 10::16, 15] = C
    kid = edge(rng, kid.shape, NV - 1, 0.66); rt = edge(rng, rt.shape, NV - 1, 0.9); snd = edge(rng, snd.shape, LN - 1, 0.7)
    fn = (C - 1) * rng.integers(0, 2, fn.shape)
    for n in range(N):
        for g in (3, 7): swaps(rng, n, g, x, ring, rt, xl, fn, False)
    return pack(x, ring, kid, rt, xl, fn, snd)
def setup_inputs_corners(rng):
    x, ring, kid, rt, xl, fn, snd = parts(rng); plant(rng, ring, rt, fn); node = np.arange(NV)
    for n in range(N):
        s = int(rng.integers(0, 8))
        for g in range(8):
            m = (g + s) % 8
            if m == 0: ring[n, g] = C
            if m == 1: ring[n, g] = ring[n, g, :, :1].copy(); ring[n, g, rt[n, g, LN:]] = fn[n, g][:, None]
            if m == 2: kid[n, g] = node; rt[n, g] = rng.permutation(H)[:L] + H * rng.integers(0, 2, L); ring[n, g, rt[n, g]] = rng.permutation(C)[:L, None]
            if m == 3: kid[n, g] = node ^ H
            if m == 4: kid[n, g, 0] = (node + 1) % NV; kid[n, g, 1] = NV - 1; rt[n, g, ::4] = NV - 1; rt[n, g, 1::4] = 0
            if m == 5: ring[n, g] = rng.integers(B, C, (NV, 16)); fn[n, g] = rng.integers(B, B + LN, LN)
            if m == 6: rt[n, g] = rng.choice(np.array([0, H - 1, H, NV - 1]), L); kid[n, g] = (NV - 1) * rng.integers(0, 2, (2, NV))
            if m == 7: snd[n, g] = (LN - 1) * (n % 2); fn[n, g] = rng.integers(0, C)
    return pack(x, ring, kid, rt, xl, fn, snd)
def setup_inputs_crowd(rng):
    x, ring, kid, rt, xl, fn, snd = parts(rng); plant(rng, ring, rt, fn)
    for n in range(N):
        s = int(rng.integers(0, 8))
        for g in range(8):
            m = (g + s) % 8; v = int(rng.integers(0, NV)); c = int(rng.integers(0, C))
            if m == 0: again(rng, n, g, x, ring, kid, rt, xl, fn, snd)
            if m == 1: swaps(rng, n, g, x, ring, rt, xl, fn, True)
            if m == 2: rt[n, g] = v
            if m == 3: rt[n, g] = v; rt[n, g, L - 1] = (v + 1) % NV
            if m == 4: rt[n, g] = v ^ (H * rng.integers(0, 2, L))
            if m == 5: ring[n, g] = c
            if m == 6: ring[n, g] = c; rt[n, g, 0] = v; ring[n, g, v] = (c + 1) % C; rt[n, g, 1:] = np.where(rt[n, g, 1:] == v, (v + 1) % NV, rt[n, g, 1:])
            if m == 7: rt[n, g] = v; kid[n, g] = rng.integers(0, NV); fn[n, g] = c; ring[n, g, v, ::2] = c; snd[n, g] = rng.integers(0, LN)
    return pack(x, ring, kid, rt, xl, fn, snd)
def setup_inputs_ties(rng):
    x, ring, kid, rt, xl, fn, snd = parts(rng)
    b = rng.choice(np.array([0, 100, 252]), (N, 8, 1, 1)); s = rng.choice(np.array([1, 2, 3]), (N, 8, 1, 1))
    x = b + s * rng.integers(0, 2, x.shape); xl = b + s * rng.integers(0, 2, xl.shape)
    q = rng.choice(np.array([1, 2, 3, 16]), (N, 8, NV, 1)); ring = np.take_along_axis(ring, rng.integers(0, 16, ring.shape) % q, 3)
    pool = rng.integers(0, NV, (N, 4, 12)); rt[:, ::2] = np.take_along_axis(pool, rng.integers(0, 12, (N, 4, L)), 2)
    plant(rng, ring, rt, fn)
    return pack(x, ring, kid, rt, xl, fn, snd)
def check_inputs(d):
    bad = []
    for k, lo, hi in (("x", 0, 255), ("ring", 0, C), ("kid", 0, NV - 1), ("rt", 0, NV - 1), ("xl", 0, 255), ("fn", 0, C - 1), ("snd", 0, LN - 1)):
        a = np.asarray(d[k]).astype(np.float64)
        if not (np.min(a) >= lo and np.max(a) <= hi): bad.append("range of " + k)
        elif np.any(a != np.floor(a)): bad.append("whole numbers in " + k)
    return bad
def first(key, on):
    low = np.arange(L)[:, None] > np.arange(L)[None, :]
    return on & ~np.any((key[..., :, None] == key[..., None, :]) & on[..., None, :] & low, axis=-1)
def reference(x, ring, kid, rt, xl, fn, snd):
    X = np.zeros((N, 8, 16, C + 1), np.int32); X[..., :C] = x.astype(np.float32).astype(np.int32).reshape(N, 8, 16, C)
    R = ring.astype(np.int32).reshape(N, 8, 16, NV); K = kid.astype(np.int32).reshape(N, 8, 2, NV)
    st = np.stack([gentries(a) for a in rt]).astype(np.int64).reshape(N, 8, 2, LN); to = np.stack([gentries(a) for a in snd]).astype(np.int64)
    fname = np.stack([gentries(a) for a in fn]).astype(np.int64); come = xl.astype(np.float32).astype(np.int32).reshape(N, 8, 16, LN)
    A = np.zeros((N, 8, 1), np.int64)
    for t in range(RO):
        p0 = B + LN * t; X[..., p0:p0 + LN] = come
        lname = np.broadcast_to(p0 + np.arange(LN), (N, 8, LN)); name = np.concatenate([lname, fname], axis=2)
        w = np.take_along_axis(X, name[:, :, None, :], 3)
        v = np.concatenate([st[:, :, t & 1], st[:, :, (t + 1) & 1]], axis=2); new = np.zeros((N, 8, NV), bool)
        for l in range(LV):
            u = v ^ H
            rv = np.take_along_axis(R, v[:, :, None, :], 3); ru = np.take_along_axis(R, u[:, :, None, :], 3)
            z = np.take_along_axis(X, rv.reshape(N, 8, 1, 16 * L), 3).reshape(N, 8, 16, 16, L)
            zu = np.take_along_axis(X, ru.reshape(N, 8, 1, 16 * L), 3).reshape(N, 8, 16, 16, L)
            m = (np.max(z, axis=3) + np.min(z, axis=3)) >> 1; mu = (np.max(zu, axis=3) + np.min(zu, axis=3)) >> 1
            near = np.argmin(np.add.reduce(np.abs(z - w[:, :, :, None, :]), axis=2), axis=2)
            c = np.take_along_axis(rv, near[:, :, None, :], 2)[:, :, 0]
            dv = np.add.reduce(np.abs(w - m), axis=2); du = np.add.reduce(np.abs(w - mu), axis=2)
            b = np.count_nonzero(w >= m, axis=2) >= 9
            act = first(v & (H - 1), np.ones((N, 8, L), bool)); ex = act & (du + A < dv)
            kv = np.take_along_axis(K, v[:, :, None, :], 3); nxt = np.where(b, kv[:, :, 1], kv[:, :, 0]).astype(np.int64)
            n, g, j = np.nonzero(first(c, c < C)); a = c[n, g, j]
            X[n, g, :, a] = (X[n, g, :, a] + w[n, g, :, j]) >> 1
            n, g, j = np.nonzero(ex); a = v[n, g, j]; e = u[n, g, j]
            R[n, g, :, a] = ru[n, g, :, j]; R[n, g, :, e] = rv[n, g, :, j]
            ka = K[n, g, :, a].copy(); ke = K[n, g, :, e].copy(); K[n, g, :, a] = ke; K[n, g, :, e] = ka
            new[n, g, a] = True; new[n, g, e] = True
            n, g, j = np.nonzero(act[..., :LN]); R[n, g, (j + t) & 15, v[n, g, j]] = p0 + j
            n, g, j = np.nonzero(act[..., LN:]); j = j + LN; a = v[n, g, j]; col = R[n, g, :, a]
            R[n, g, :, a] = np.where((col == name[n, g, j][:, None]) & ~new[n, g, a][:, None], C, col)
            A = np.count_nonzero(ex, axis=2)[..., None]
            if l < LV - 1: v = nxt
        if t < RO - 1:
            gone = np.take_along_axis(X, fname[:, :, None, :], 3); come = np.zeros((N, 8, 16, LN), np.int32)
            for q in range(N):
                for d in range(N): come[(q + d) % N, :, :, d * S:d * S + S] = np.take_along_axis(gone[q], to[q][:, None, d * S:d * S + S], 2)
            fname = lname
    return {"yx": X[..., :C].astype(np.float32).astype(BF).reshape(N, 128, C), "yr": R.reshape(N, 128, NV).astype(np.float32), "yk": K.reshape(N, 16, NV).astype(np.float32)}

@@ -1,0 +1,610 @@
+from concourse.bass import DstId, RemoteDMATransfer
+from concourse.mybir import AluOpType as A, ActivationFunctionType as F, AxisListType
+
+C, NV, LN, RO, L, N = 3072, 1024, 96, 4, 192, 6
+B0 = C - LN * RO
+XW, RW, IW = 3280, 1408, 3088
+MAG = 12582912.0
+M30 = 1.5 * 2.0 ** 30
+ORG = 5.0 / 16
+BIG = 2.0 ** 70
+PEF = 0.75
+UCH = 384
+NF = 96
+NP = L - NF
+UV = 0
+
+bf, f32, i32, u16 = "bfloat16", "float32", "int32", "uint16"
+SB = dict(
+    X=(XW, bf), R=(RW, f32), RI=(NV, i32), KI=(NV, i32), KF=(NV, f32), KD=(512, f32), YR=(NV, f32), YK=(NV, f32),
+    IO=(IW, f32), RTI=(12, i32), FNI=(8, i32), SNI=(8, i32), FN16=(8, u16), SN16=(8, u16),
+    LAND0=(LN, bf), LAND1=(LN, bf), LAND2=(LN, bf), LAND3=(LN, bf), SEND0=(LN, bf), SEND1=(LN, bf), SEND2=(LN, bf),
+    GONE=(LN, bf), W=(L, bf), WT=(768, bf), WIX=(LN, u16), WSP=(1536, bf), WREP=(1536, bf), NMF=(LN, f32), GG=(LN, f32),
+    O16=(384, u16), RVU=(384, f32), RVP=(384, f32), Y1=(288, f32), NM=(288, f32), HI=(L, bf),
+    C0=(L, f32), RDC=(L, bf), PHALF=(L, bf),
+    ZV=(3072, bf), ZU=(3072, bf), AB=(3072, bf), MXV=(3072, bf), MNV=(3072, bf), MXU=(3072, bf), MNU=(3072, bf),
+    ST=(512, f32), RR=(32, f32), DIG=(32, bf), CS=(96, f32), C16=(12, u16), REP=(L, u16), REPA=(L, u16),
+    E=(12 * L, bf), EA=(12 * L, bf), SD=(L, f32), SDA=(L, f32), T1=(12, f32), T2=(12, f32), XO16=(12, u16),
+    T3=(24, f32), T4=(24, f32), XC=(L, bf), Y3=(L, f32), VAL=(L, bf),
+    Y4=(384, f32), HA=(384, bf), SG=(384, bf), A1=(LN, f32), A2=(LN, f32), SA=(384, f32), SBB=(384, f32),
+    JUNK=(L, bf), SUM=(4, f32), DP=(128, bf),
+    LV0=(36, f32), LV1=(36, f32), LV2=(36, f32), U0=(36, u16), U1=(36, u16), U2=(36, u16),
+    OF0=(24, u16), OF1=(24, u16), OF2=(24, u16), PN0=(L, bf), PN1=(L, bf), PN2=(L, bf), H1=(12, f32), H2=(12, f32),
+    KG=(384, f32), KL=(48, f32), MID0=(24, f32), MID1=(24, f32), HH0=(24, f32), HH1=(24, f32), OO=(24, f32),
+    KM=(24, f32), SBL=(12, f32), Y5=(512, f32),
+    PI=(4, i32), COL=(16, f32), IF=(128, f32), NIF=(128, f32), IB=(128, bf), I2=(128, bf), IK=(256, bf),
+    IP=(128, bf), IN=(128, bf), WD=(144, bf), WM=(144, f32), WH=(144, f32), G2=(16, bf),
+    JB=(128, f32), BOP=(128, bf), BON=(128, bf), BOD=(128, bf), BOO=(128, bf), LM=(208, f32), CD=(L, bf),
+    EX=(512, bf), LM1=(768, bf), LM64=(768, bf), PEN8=(96, bf), RS8=(96, bf), RT=(256, bf), MXR=(768, bf),
+    MNR=(768, bf), RD=(L, bf), HALF=(L, bf), DC=(12, f32), DVU=(24, f32), PW=(32, f32),
+)
+SCRATCH, PLACE, _at = {}, {}, 0
+for _k, _v in SB.items():
+    if _v[1] == f32 and _v[0] <= 48:
+        PLACE[_k] = ("SMALL", _at, _v[0], f32)
+        _at += (_v[0] + 7) // 8 * 8
+    else:
+        PLACE[_k] = (_k, 0, _v[0], _v[1])
+        SCRATCH[_k] = ("sbuf", [128, _v[0]], _v[1])
+SCRATCH["SMALL"] = ("sbuf", [128, _at], f32)
+for _b in range(8):
+    SCRATCH["P%d" % _b] = ("psum", [128, 512], "float32")
+    PLACE["P%d" % _b] = ("P%d" % _b, 0, 512, f32)
+DMAS = ["ring", "x", "rt", "xl", "fn", "k0", "k1", "snd", "yx", "yr", "y0", "y1"]
+SEMAPHORES = ["sV", "sS", "sP", "sG", "sent", "arr0", "arr1", "arr2"] + ["d" + n for n in DMAS]
+CYC = 0.83e-3
+
+
+def build(T, topo, rank):
+    ops = []
+
+    def ap(name, a=0, b=None, s=1, p=None):
+        buf, at, width, dt = PLACE[name]
+        if b is None:
+            b = width
+        rows = slice(0, 128) if p is None else slice(p[0], p[1])
+        v = T[buf][rows, at + a:at + b] if s == 1 else T[buf][rows, at + a:at + b:s]
+        return dict(v=v, n=len(range(a, b, s)), r=[(name, a, b)], dt=dt, ps=is_bank(name))
+
+    def ind(name, a, b, off):
+        return dict(v=T[name][:, a:b].indirect(off["v"]), n=16 * off["n"], r=[(name, a, b)], o=off["r"], dt=SCRATCH[name][2], ps=False, ind=1)
+
+    def val(x):
+        return x["v"] if isinstance(x, dict) else x
+
+    def add(eng, fn, ins, outs, cyc, acc=False, sem=None, lat=0.0):
+        rd, wr = [], []
+        for x in ins:
+            if isinstance(x, dict):
+                rd += x["r"] + x.get("o", [])
+        for x in outs:
+            wr += x["r"]
+            rd += x.get("o", [])
+        ops.append(dict(e=eng, fn=fn, rd=rd, wr=wr, t=cyc * CYC, acc=acc, sem=sem, lat=lat))
+
+    def vcost(out, ins, rate=None):
+        n = ins[0]["n"] if ins else out["n"]
+        if "ind" in out:
+            return 60 + 3.8 * n
+        if ins and "ind" in ins[0]:
+            return 60 + 1.56 * n
+        if rate is None:
+            rate = 0.5 if all(x["dt"] in (bf, u16) for x in ins + [out]) else 1.0
+        return 1.2 * max(64, n * rate)
+
+    def copy(out, a):
+        add("V", lambda g: g.vector.tensor_copy(out["v"], a["v"]), [a], [out], vcost(out, [a]))
+
+    def tt(out, a, b, op):
+        add("V", lambda g: g.vector.tensor_tensor(out["v"], a["v"], b["v"], op), [a, b], [out],
+            vcost(out, [a, b], 1.0 if a["ps"] or b["ps"] else 2.0))
+
+    def ts(out, a, s1, op0, s2=None, op1=None):
+        if op1 is None:
+            fn = lambda g: g.vector.tensor_scalar(out["v"], a["v"], val(s1), None, op0)
+        else:
+            fn = lambda g: g.vector.tensor_scalar(out["v"], a["v"], val(s1), val(s2), op0, op1)
+        add("V", fn, [a, s1, s2], [out], vcost(out, [a]))
+
+    def scan(out, d0, d1, op0, op1, init=0.0):
+        add("V", lambda g: g.vector.tensor_tensor_scan(out["v"], d0["v"], d1["v"], init, op0, op1), [d0, d1], [out], vcost(out, [d0, d1]))
+
+    def mset(out, c):
+        add("V", lambda g: g.vector.memset(out["v"], c), [], [out], vcost(out, []))
+
+    def act(out, a, func, bias=0.0, scale=1.0, accum=None):
+        if accum is None:
+            fn = lambda g: g.scalar.activation(out["v"], a["v"], func, bias=val(bias), scale=val(scale))
+        else:
+            fn = lambda g: g.scalar.activation(out["v"], a["v"], func, bias=val(bias), scale=val(scale), accum_out=accum["v"])
+        cyc = 80 + 1.56 * a["n"] if "ind" in a else 1.2 * max(64, a["n"])
+        add("S", fn, [a, bias, scale], [out] + ([accum] if accum else []), cyc)
+
+    def mm(out, lhsT, rhs, start, stop):
+        cyc = max(min(64, lhsT["n"]), rhs["n"]) * (4 if rhs["dt"] == f32 else 1) * PEF
+        add("P", lambda g: g.tensor.matmul(out["v"], lhsT["v"], rhs["v"], start, stop), [lhsT, rhs], [out], cyc, acc=True)
+
+    def group(items):
+        for i, (o, l, r) in enumerate(items):
+            mm(o, l, r, i == 0, i == len(items) - 1)
+
+    def iota(out, pat, base=0, cm=0):
+        if out["dt"] == i32:
+            fn = lambda g: g.iota(out["v"], pat, base, cm)
+        else:
+            fn = lambda g: g.iota(out["v"], pat, base, cm, allow_small_or_imprecise_dtypes=True)
+        add("G", fn, [], [out], 190 + 2.4 * out["n"])
+        ops[-1]["chain"] = "G"
+
+    def dma(q, name, out, in_, rd, wr, us):
+        eng = (lambda g: g.sync) if q == "Y" else (lambda g: g.scalar)
+        add(q, lambda g: eng(g).dma_start(out, in_), rd, wr, 80, sem="d" + name, lat=us)
+        if wr:
+            ops[-1]["chain"] = q
+
+    col = lambda j: ap("COL", j, j + 1)
+    dma("Y", "ring", T.RI[:], T.ring[:], [], [ap("RI")], 3.0)
+    dma("S", "rt", T.RTI[:], T.rt[:], [], [ap("RTI")], 2.0)
+    dma("Y", "x", T.X[:, 0:C], T.x[:], [], [ap("X", 0, C)], 5.0)
+    dma("S", "xl", T.LAND0[:], T.xl[:], [], [ap("LAND0")], 2.2)
+    dma("S", "fn", T.FNI[:, 0:6], T.fn[:], [], [ap("FNI")], 2.2)
+    mset(dict(ap("KI"), r=[("KI", 0, NV), ("KI", 0, 0)]), 0)
+    dma("Y", "k0", T.KI[0:128:16, :], T.kid[0:16:2, :], [], [ap("KI")], 2.5)
+    dma("Y", "k1", T.KI[1:128:16, :], T.kid[1:16:2, :], [], [ap("KI", 0, 0)], 2.5)
+    dma("Y", "snd", T.SNI[:, 0:6], T.snd[:], [], [ap("SNI")], 2.2)
+    iota(ap("PI", 0, 1), [[1, 1]], 0, 1)
+    iota(ap("IO", 0, 512), [[1, 512]])
+    iota(ap("EX", p=(0, 32)), [[1, 32], [0, 16]], 0, -1)
+    iota(ap("LM"), [[0, 13], [1, 16]])
+    iota(ap("JB"), [[16, 8], [0, 16]])
+    iota(ap("G2"), [[0, 2], [16, 8]])
+    iota(ap("PEN8"), [[0, 12], [16, 8]])
+    iota(ap("LM64", p=(0, 96)), [[-16, 6], [0, 8], [-1, 16]], 0, 1)
+    for a in range(512, IW, 512):
+        act(ap("IO", a, min(IW, a + 512)), ap("IO", 0, min(IW - a, 512)), F.Identity, bias=float(a))
+    ts(ap("PI", 1, 2), ap("PI", 0, 1), 15, A.bitwise_and)
+    copy(ap("COL", 0, 2), ap("PI", 0, 2))
+    tt(col(2), col(0), col(1), A.subtract)
+    ts(col(3), col(2), 15.0, A.add)
+    J = ap("IO", 0, 128)
+    ts(ap("IF"), J, col(0), A.is_equal)
+    for name, a, sc in (("NIF", 0, -1.0), ("IB", 0, 1.0), ("I2", 0, -2.0), ("IK", 0, -64.0), ("IK", 128, 1.0),
+                        ("IP", 0, 16384.0), ("IN", 0, -16384.0)):
+        act(ap(name, a, a + 128), ap("IF"), F.Identity, scale=sc)
+    ts(ap("WD"), ap("IO", 0, 144), col(3), A.is_equal)
+    ts(ap("G2"), ap("G2"), col(2), A.is_equal, 2048.0, A.mult)
+    ts(ap("JB"), ap("JB"), col(2), A.is_equal)
+    ts(ap("LM"), ap("LM"), col(1), A.is_equal)
+    mset(ap("PW", 0, 16), 0.5)
+    scan(ap("PW", 16, 32), ap("PW", 0, 16), ap("PW", 0, 16), A.mult, A.max, 2.0 ** 29)
+    tt(ap("PW", 0, 16), ap("PW", 16, 32), ap("LM", 0, 16), A.mult)
+    add("V", lambda g: g.vector.tensor_reduce(col(4)["v"], ap("PW", 0, 16)["v"], AxisListType.X, A.add), [ap("PW", 0, 16)], [col(4)], 80)
+    ts(col(5), col(4), -2.0, A.mult)
+    for name, sc in (("BOP", 16384.0), ("BON", -16384.0), ("BOO", 2.0 ** 40), ("BOD", col(4))):
+        act(ap(name), ap("JB"), F.Identity, scale=sc)
+    act(ap("SA", 0, L), ap("LM", 0, L), F.Identity, scale=col(5))
+    act(ap("SBB", 0, L), ap("LM", 0, L), F.Identity, scale=BIG, bias=-BIG)
+    tt(ap("CD"), ap("SA", 0, L), ap("SBB", 0, L), A.add)
+    ts(ap("EX", p=(0, 32)), ap("EX", p=(0, 32)), 0.0, A.is_equal, -1.0, A.mult)
+    ts(ap("LM1", p=(0, 96)), ap("LM64", p=(0, 96)), 0.0, A.is_equal)
+    act(ap("LM64", p=(0, 96)), ap("LM1", p=(0, 96)), F.Identity, scale=64.0)
+    ts(ap("PEN8"), ap("PEN8"), col(2), A.not_equal, 2.0 ** 20, A.mult)
+    for name, base, st, c in (("RS8", 0.0, 8, 2.0 ** 20), ("RT", -128.0, 16, 2.0 ** 30), ("MXR", 0.0, 16, -1024.0), ("RD", 0.0, 16, -8 * BIG)):
+        mset(ap(name), base)
+        mset(ap(name, s=st), c)
+    act(ap("MNR"), ap("MXR"), F.Identity, scale=-1.0)
+    mset(ap("HALF"), -0.5)
+    copy(ap("WIX"), ap("IO", 0, LN))
+    mset(ap("WSP"), -1024.0)
+    mset(ap("X", C, XW), 0.0)
+    act(ap("R", NV, RW), ap("IO", 0, RW - NV), F.Identity)
+    mset(ap("DP"), 0.0)
+    mset(ap("PHALF"), 0.5)
+    copy(ap("RDC"), ap("RD"))
+    ts(ap("DC"), ap("IO", 0, L, 16), col(1), A.add, float(C + 1), A.add)
+    ts(ap("DVU"), ap("IO", 0, 384, 16), col(1), A.add, float(NV), A.add)
+    ts(ap("R", 0, 512), ap("RI", 0, 512), 0.0, A.add)
+    ts(ap("R", 512, NV), ap("RI", 512, NV), ORG, A.add)
+    copy(ap("FN16", 0, 6), ap("FNI", 0, 6))
+    copy(ap("SN16", 0, 6), ap("SNI", 0, 6))
+
+    def firsts(key16, keys, rep, E, bank, sd, reset):
+        copy(ap(rep), ind("IO", 0, IW, key16))
+        items = [(ap(bank, 0, L), ap("IB"), ap("CD"))]
+        for m in range(12):
+            ts(ap(E, m * L + 16 * m, m * L + L), ap(rep, 16 * m, L), keys(m), A.is_equal)
+            items.append((ap(bank, 16 * m, 16 * m + 16), ap("BOD"), ap(E, m * L + 16 * m, m * L + 16 * m + 16)))
+            if m < 11:
+                items.append((ap(bank, 16 * m + 16, L), ap("BOO"), ap(E, m * L + 16 * m + 16, m * L + L)))
+        group(items)
+        scan(ap(sd), ap(reset), ap(bank, 0, L), A.add, A.max)
+
+    def nodes(k):
+        lv, u, of = "LV%d" % k, "U%d" % k, "OF%d" % k
+        ts(ap("H1"), ap(lv, 0, 12), 512.0, A.is_ge, -512.0, A.mult)
+        ts(ap("H2"), ap(lv, 0, 12), 512.0, A.is_lt, 512.0, A.mult)
+        tt(ap(lv, 24, 36), ap(lv, 0, 12), ap("H1"), A.add)
+        tt(ap(lv, 12, 24), ap(lv, 24, 36), ap("H2"), A.add)
+        copy(ap(u), ap(lv))
+        firsts(ap(u, 24, 36), lambda m: ap(lv, 24 + m, 25 + m), "REPA", "EA", "P7", "SDA", "RD")
+        tt(ap("T3", 0, 12), ap(lv, 0, 12), ap("SDA", 15, L, 16), A.max)
+        tt(ap("T3", 12, 24), ap(lv, 12, 24), ap("SDA", 15, L, 16), A.max)
+        tt(ap("T4"), ap("T3"), ap("DVU"), A.min)
+        copy(ap(of), ap("T4"))
+        act(ap("PN%d" % k), ind("IO", 0, IW, ap(of, 0, 12)), F.Relu, scale=16384.0, bias=-1023.5 * 16384)
+        act(ap("PN%d" % k), ap("PN%d" % k), F.Identity, bias=0.5)
+
+    copy(ap("LV0", 0, 12), ap("RTI"))
+    nodes(0)
+
+    def kids():
+        kin = dict(ap("KI"), r=[("KI", 0, NV), ("KI", 0, 0)])
+        copy(ap("KF"), kin)
+        act(ap("KG"), ind("KF", 0, NV, ap("U0", 0, 24)), F.Identity)
+        ts(col(6), col(1), 2.0, A.is_lt, 0.25, A.mult)
+        ts(col(8), col(1), 0.5, A.mult, -0.25, A.add)
+        tt(col(7), col(8), col(6), A.mult)
+        act(ap("WM"), ap("WD"), F.Identity, scale=col(6))
+        ts(ap("WH"), ap("WD"), col(7), A.mult, 4.0, A.mult)
+        for j, w in enumerate(("WM", "WH")):
+            group([(ap("P6", 24 * j, 24 * j + 24), ap(w, 15 - q, 143 - q), ap("KG", q, 384, 16)) for q in range(16)])
+        act(ap("KL"), ap("P6", 0, 48), F.Identity)
+        ts(ap("T1"), ap("LV0", 0, 12), 512.0, A.is_ge, 2.0, A.mult)
+        ts(ap("T2"), ap("T1"), -1.0, A.add)
+        for j in range(2):
+            tt(ap("MID0", 12 * j, 12 * j + 12), ap("KL", 24 * j, 24 * j + 12), ap("KL", 24 * j + 12, 24 * j + 24), A.add)
+            tt(ap("KM", 12 * j, 12 * j + 12), ap("KL", 24 * j, 24 * j + 12), ap("KL", 24 * j + 12, 24 * j + 24), A.subtract)
+            tt(ap("HH0", 12 * j, 12 * j + 12), ap("KM", 12 * j, 12 * j + 12), ap("T2"), A.mult)
+        for nm in ("MID", "HH"):
+            for j in range(4):
+                act(ap(nm + "1", 6 * j, 6 * j + 6), ap(nm + "0", 6 * (j ^ 1), 6 * (j ^ 1) + 6), F.Identity)
+
+    def level(t, l):
+        k = (t & 1) if l == 0 else 2
+        U, OF, PN = "U%d" % k, "OF%d" % k, "PN%d" % k
+        p0 = B0 + LN * t
+        nameL = ap("IO", p0, p0 + LN)
+        nameF = ap("NMF") if t == 0 else ap("IO", p0 - LN, p0)
+        thr = 2.0 ** t / 128
+        last = t == RO - 1 and l == 1
+        copy(ap("O16", 0, L), ind("R", 0, RW, ap(U, 0, 12)))
+        copy(ap("O16", L, 384), ind("R", 0, RW, ap(U, 12, 24)))
+        X = lambda a, b: ind("X", 0, XW, ap("O16", a, b))
+        plain = [(a, min(NP, a + 32)) for a in range(0, NP, 32)]
+        fused = [(a, min(L, a + 32)) for a in range(NP, L, 32)]
+        for a, b in plain:
+            act(ap("ZV", 16 * a, 16 * b), X(a, b), F.Identity)
+        for a, b in fused:
+            tt(ap("ZV", 16 * a, 16 * b), X(a, b), ap("WREP", 16 * (a - NP), 16 * (b - NP)), A.subtract)
+        act(ap("RVU"), ind("R", 0, RW, ap(U, 0, 24)), F.Identity)
+        act(ap("Y1"), ap("RVU", 0, 288), F.Identity, bias=MAG)
+        act(ap("NM"), ap("Y1"), F.Identity, bias=-MAG)
+        act(ap("HI"), ap("RVU", 0, L), F.Identity, bias=128.0, scale=1.0 / 64)
+        if l == 0:
+            act(ap("RVP"), ap("RVU"), F.Identity, bias=thr)
+        else:
+            act(ap("RVP", L, 384), ap("RVU", L, 384), F.Identity)
+        for c, (a, b) in enumerate(plain):
+            o = ap("P%d" % (2 + c % 2), 0, 16 * (b - a))
+            group([(o, ap("IB"), ap("ZV", 16 * a, 16 * b)),
+                   (o, ap("WT", 128 * c, 128 * c + 128, p=(0, 32)), ap("EX", 0, 16 * (b - a), p=(0, 32)))])
+            act(ap("AB", 16 * a, 16 * b), o, F.Abs)
+        for a, b in fused:
+            act(ap("AB", 16 * a, 16 * b), ap("ZV", 16 * a, 16 * b), F.Abs)
+        P96 = (0, 96)
+        for h in range(2):
+            bk = "P%d" % h
+            items = [(ap(bk, 0, 256, p=P96), ap("HI", 96 * h, 96 * h + 96), ap("IK")),
+                     (ap(bk, 0, 128, p=P96), ap("NM", 96 * h, 96 * h + 96), ap("IF"))]
+            items += [(ap(bk, s, 256, 16, p=P96), ap("AB", 1536 * h + s, 1536 * h + 1536, 16), ap("G2")) for s in range(16)]
+            group(items)
+            scan(ap("ST", 256 * h, 256 * h + 256, p=P96), ap("RT", p=P96), ap(bk, 0, 256, p=P96), A.add, A.min)
+            ts(ap("RR", 16 * h, 16 * h + 16, p=P96), ap("ST", 256 * h + 15, 256 * h + 256, 16, p=P96), M30, A.add, M30, A.subtract)
+            tt(ap("DIG", 16 * h, 16 * h + 16, p=P96), ap("ST", 256 * h + 15, 256 * h + 256, 16, p=P96), ap("RR", 16 * h, 16 * h + 16, p=P96), A.subtract)
+        items = [(ap("P2", 0, 96), ap("IB"), ap("PEN8"))]
+        for h in range(2):
+            for m in range(6):
+                for ab in range(2):
+                    items.append((ap("P2", 48 * h + 8 * m, 48 * h + 8 * m + 8), ap("LM64" if ab else "LM1", 128 * m, 128 * m + 128, p=P96),
+                                  ap("DIG", 16 * h + 8 * ab, 16 * h + 8 * ab + 8, p=P96)))
+        group(items)
+        scan(ap("CS"), ap("RS8"), ap("P2", 0, 96), A.add, A.min)
+        copy(ap("C16"), ap("CS", 7, 96, 8))
+        group([(ap("P5", 0, 96), ap("IF"), ap("NM", 0, 96)), (ap("P5", 0, 96), ap("NIF"), nameL)])
+        group([(ap("P5", 96, L), ap("IF"), ap("NM", L, 288)), (ap("P5", 96, L), ap("NIF"), nameL)])
+        group([(ap("P5", L, 288), ap("IF"), ap("RVU", 96, L)), (ap("P5", L, 288), ap("NIF"), nameF)])
+        if l == 0:
+            group([(ap("P5", 288, 480), ap("IF"), ap("RVU", 0, L)), (ap("P5", 288, 480), ap("NIF"), ap("NM", 0, L))])
+            act(ap("SG", 0, L), ap("P5", 288, 480), F.Sign, bias=-0.2)
+        act(ap("A1"), ap("P5", L, 288), F.Abs, bias=-ORG / 2 - thr / 2 + 1.0 / 512)
+        act(ap("A2"), ap("A1"), F.Abs, bias=-ORG / 2)
+        act(ap("P5", L, 288), ap("A2"), F.Relu, scale=-2.0 ** 22, bias=2.0 ** 21 * thr)
+        tt(ap("P5", 0, L), ap("P5", 0, L), ap("LM", t, t + L), A.mult)
+        tt(ap("P5", L, 288), ap("P5", L, 288), ap("GG"), A.min)
+        tt(ap("C0", 0, 96), ap("RVU", 0, 96), ap("P5", 0, 96), A.subtract)
+        tt(ap("RVP", L, 288), ap("RVP", L, 288), ap("P5", 96, L), A.subtract)
+        tt(ap("C0", 96, L), ap("RVU", 96, L), ap("P5", L, 288), A.add)
+        for c in range(4):
+            for o, r, op in (("MXV", "MXR", A.max), ("MNV", "MNR", A.min)):
+                scan(ap(o, 768 * c, 768 * c + 768), ap(r), ap("ZV", 768 * c, 768 * c + 768), A.add, op)
+        group([(ap("P4", 0, L), ap("IB"), ap("HALF")), (ap("P4", 0, NP), ap("I2"), ap("W", 0, NP)),
+               (ap("P4", 0, L), ap("IB"), ap("MXV", 15, 3072, 16)), (ap("P4", 0, L), ap("IB"), ap("MNV", 15, 3072, 16))])
+        if l == 0:
+            act(ap("SG", L, 384), ap("P4", 0, L), F.Sign, scale=-1.0, bias=1.0)
+        act(ap("Y4", 0, L), ap("P4", 0, L), F.Identity, scale=0.5, bias=MAG)
+        act(ap("HA", 0, L), ap("Y4", 0, L), F.Abs, bias=-MAG)
+        if l == 0:
+            if t == 0:
+                kids()
+            group([(ap("P6", 0, 24), ap("WD", 15 - q, 143 - q), ap("SG", q, 384, 16)) for q in range(16)])
+            act(ap("OO", 0, 12), ap("P6", 0, 12), F.Sign)
+            act(ap("OO", 12, 24), ap("P6", 0, 12), F.Sign)
+            act(ap("SBL"), ap("P6", 12, 24), F.Sign, bias=-1.0)
+            tt(ap("T4"), ap("OO"), ap("HH%d" % k), A.mult)
+            tt(ap("KM"), ap("T4"), ap("MID%d" % k), A.add)
+            tt(ap("H1"), ap("SBL"), ap("KM", 12, 24), A.mult)
+            tt(ap("LV2", 0, 12), ap("H1"), ap("KM", 0, 12), A.add)
+            nodes(2)
+        nu = 3072 // UCH
+        for c in range(nu):
+            o, src = ap("ZU", UCH * c, UCH * c + UCH), X(L + UCH // 16 * c, L + UCH // 16 * (c + 1))
+            if c < UV:
+                copy(o, src)
+            else:
+                act(o, src, F.Identity)
+        act(ap("RDC", 15, L, 16), ap("CS", 7, 96, 8), F.Relu, scale=4 * BIG, bias=-(C - 0.5) * 4 * BIG)
+        act(ap("XC"), ind("X", 0, XW, ap("C16")), F.Identity)
+        firsts(ap("C16"), lambda m: ap("CS", 8 * m + 7, 8 * m + 8), "REP", "E", "P3", "SD", "RDC")
+        tt(ap("T1"), ap("CS", 7, 96, 8), ap("SD", 15, L, 16), A.max)
+        tt(ap("T2"), ap("T1"), ap("DC"), A.min)
+        copy(ap("XO16"), ap("T2"))
+        group([(ap("P6", 0, L), ap("IB"), ap("HALF")), (ap("P6", 0, L), ap("IB"), ap("W")), (ap("P6", 0, L), ap("IB"), ap("XC"))])
+        act(ap("Y3"), ap("P6", 0, L), F.Identity, scale=0.5, bias=MAG)
+        act(ap("VAL"), ap("Y3"), F.Identity, bias=-MAG)
+        copy(ind("X", 0, XW, ap("XO16")), ap("VAL"))
+        if last:
+            dma("Y", "yx", T.yx[:], T.X[:, 0:C], [ap("X", 0, C)], [], 4.0)
+        elif l == 1:
+            hand_on(t)
+        for c in range(4):
+            for o, r, op in (("MXU", "MXR", A.max), ("MNU", "MNR", A.min)):
+                scan(ap(o, 768 * c, 768 * c + 768), ap(r), ap("ZU", 768 * c, 768 * c + 768), A.add, op)
+        group([(ap("P4", 0, L), ap("IB"), ap("HALF")), (ap("P4", 0, L), ap("I2"), ap("W")),
+               (ap("P4", 0, L), ap("IB"), ap("MXU", 15, 3072, 16)), (ap("P4", 0, L), ap("IB"), ap("MNU", 15, 3072, 16))])
+        act(ap("Y4", L, 384), ap("P4", 0, L), F.Identity, scale=0.5, bias=MAG)
+        act(ap("HA", L, 384), ap("Y4", L, 384), F.Abs, bias=-MAG)
+        for bk, a, b, i1, i2, d in (("P0", "BOP", "BON", "IP", "IN", "HALF"), ("P1", "BON", "BOP", "IN", "IP", "PHALF")):
+            o = ap(bk, 0, L)
+            group([(o, ap("DP"), ap(d)), (o, ap(i2), ap(PN)), (o, ap(a), ap("HA", 0, L)), (o, ap(b), ap("HA", L, 384))])
+        tt(ap("SBB", 0, L), ap("RVP", L, 384), ap("P0", 0, L), A.min)
+        tt(ap("SBB", L, 384), ap("RVP" if l == 0 else "RVU", 0, L), ap("P0", 0, L), A.min)
+        tt(ap("SA", 0, L), ap("C0"), ap("P1", 0, L), A.min)
+        tt(ap("SA", L, 384), ap("RVU", L, 384), ap("P1", 0, L), A.min)
+        tt(ind("R", 0, RW, ap(OF)), ap("SA"), ap("SBB"), A.max)
+        if not last:
+            act(ap("JUNK"), ap("P0", 0, L), F.Sign, accum=ap("SUM", 0, 1))
+            act(ap("SUM", 1, 2), ap("SUM", 0, 1), F.Identity, scale=16384.0, bias=96.0 * 32768)
+            act(ap("DP"), ap("IF"), F.Identity, scale=ap("SUM", 1, 2))
+
+    def shares(r):
+        me = T.cores[r]
+        ds = sorted(range(1, N), key=lambda d: len(topo.engines(me, T.cores[(r + d) % N])))
+        used, res = set(), {}
+        for i, d in enumerate(ds):
+            allowed = topo.engines(me, T.cores[(r + d) % N])
+            free = [e for e in allowed if e not in used]
+            rivals = sum(1 for d2 in ds[i:] if topo.engines(me, T.cores[(r + d2) % N]) == allowed)
+            n = 1
+            while 2 * n * rivals <= len(free):
+                n *= 2
+            res[d] = free[:n]
+            used.update(res[d])
+        return res
+
+    def hand_on(t):
+        snd, land = "SEND%d" % t, "LAND%d" % (t + 1)
+        p0 = B0 + LN * t
+        if t == 0:
+            act(ap("GONE"), ind("X", 0, XW, ap("FN16", 0, 6)), F.Identity)
+            act(ap(snd), ind("GONE", 0, LN, ap("SN16", 0, 6)), F.Identity)
+        else:
+            act(ap(snd), ind("X", p0 - LN, p0, ap("SN16", 0, 6)), F.Identity)
+        mine = shares(rank)
+
+        def send(g):
+            tr = []
+            for d in range(1, N):
+                rid, pid, _ = topo.addr(T.cores[(rank + d) % N])
+                tr.append(RemoteDMATransfer(dst_ids=[DstId(rid=rid, pnc=pid)], dma_engine_mask=sum(1 << e for e in mine[d]),
+                                            remote_sem=T.sem["arr%d" % t], src=T[snd][:, 16 * d:16 * d + 16], dst=T[land][:, 16 * d:16 * d + 16]))
+            g.remote_dma_fused(tr, local_sem=T.sem.sent)
+            return None
+        add("G", send, [ap(snd)], [dict(r=[("wire", t, t + 1)])], 600, sem="", lat=2.5)
+        ops[-1]["sent"] = sum(len(v) for v in mine.values())
+        act(ap(land, 0, 16), ap(snd, 0, 16), F.Identity)
+        ops.append(dict(e="X", fn=None, rd=[("wire", t, t + 1)], wr=[(land, 16, LN)], t=0.0, acc=False, lat=0.0, sem="arr%d" % t,
+                        cnt=sum(len(shares((rank - d) % N)[d]) for d in range(1, N))))
+
+    for t in range(RO):
+        p0 = B0 + LN * t
+        land = "LAND%d" % t
+        if t > 0:
+            act(ap("W", LN, L), ap("X", p0 - LN, p0), F.Identity)
+        copy(ap("X", p0, p0 + LN), ap(land))
+        act(ap("W", 0, LN), ap(land), F.Identity)
+        if t == 0:
+            act(ap("W", LN, L), ind("X", 0, XW, ap("FN16", 0, 6)), F.Identity)
+            act(ap("NMF"), ind("IO", 0, IW, ap("FN16", 0, 6)), F.Identity)
+        act(ap("GG"), ap("NMF") if t == 0 else ap("IO", p0 - LN, p0), F.Identity, scale=-1.0, bias=float(C))
+        for a in range(0, NF, 32):
+            b = min(NF, a + 32)
+            if t > 0:
+                act(ap("WREP", 16 * a, 16 * b), ind("W", NP, L, ap("WIX", a, b)), F.Identity)
+            else:
+                copy(ap("WSP", 16 * a, 16 * b, 16), ap("W", NP + a, NP + b))
+                scan(ap("WREP", 16 * a, 16 * b), ap("MXR", 0, 16 * (b - a)), ap("WSP", 16 * a, 16 * b), A.add, A.max)
+        for c0, c1 in ((3, (NP + 31) // 32), (0, 3)):
+            for c in range(c0, c1):
+                src = ap(land, 32 * c, 32 * c + 32) if c < 3 else ap("W", 32 * c, 32 * c + 32)
+                mm(ap("P6", 128 * (c - c0), 128 * (c - c0) + 128, p=(0, 32)), src, ap("IB"), True, True)
+            if c1 > c0:
+                act(ap("WT", 128 * c0, 128 * c1, p=(0, 32)), ap("P6", 0, 128 * (c1 - c0), p=(0, 32)), F.Identity)
+        level(t, 0)
+        if t == 0:
+            copy(ap("LV1", 0, 6), ap("RTI", 6, 12))
+            copy(ap("LV1", 6, 12), ap("RTI", 0, 6))
+            nodes(1)
+        if t == 1:
+            group([(ap("P7"), ap("IF"), ap("KF", 512, NV)), (ap("P7"), ap("NIF"), ap("KF", 0, 512))])
+            act(ap("KD"), ap("P7"), F.Identity, scale=2.0)
+        level(t, 1)
+    ts(ap("YR"), ap("R", 0, NV), MAG, A.add, MAG, A.subtract)
+    dma("Y", "yr", T.yr[:], T.YR[:], [ap("YR")], [], 3.0)
+    act(ap("Y5"), ap("R", 0, 512), F.Identity, bias=MAG / 2)
+    act(ap("P2"), ap("Y5"), F.Identity, bias=-MAG / 2)
+    tt(ap("P2"), ap("P2"), ap("YR", 0, 512), A.subtract)
+    tt(ap("P2"), ap("P2"), ap("KD"), A.mult)
+    tt(ap("YK", 0, 512), ap("KF", 0, 512), ap("P2"), A.add)
+    tt(ap("YK", 512, NV), ap("KF", 512, NV), ap("P2"), A.subtract)
+    dma("Y", "y0", T.yk[0:16:2, :], T.YK[0:128:16, :], [ap("YK")], [], 2.0)
+    dma("S", "y1", T.yk[1:16:2, :], T.YK[1:128:16, :], [ap("YK")], [], 2.0)
+    return ops
+
+
+def is_bank(name):
+    return name[0] == "P" and name[1:].isdigit()
+
+
+def edges(ops):
+    hist, deps = {}, []
+    for i, o in enumerate(ops):
+        d = {}
+        for kind, regs in (("r", o["rd"]), ("w", o["wr"])):
+            for (nm, a, b) in regs:
+                h = hist.setdefault(nm, [])
+                bank = is_bank(nm)
+                for (j, k2, a2, b2) in h:
+                    if j == i:
+                        continue
+                    hit = (a < b2 and a2 < b) or (a, b) == (a2, b2)
+                    if hit and (k2 == "w" or kind == "w"):
+                        d[j] = d.get(j, False) or (k2 == "w" and kind == "r") or (SYNC_ALL and not (o["acc"] and ops[j]["acc"]))
+                if bank and h:
+                    d.setdefault(h[-1][0], False)
+        for kind, regs in (("r", o["rd"]), ("w", o["wr"])):
+            for (nm, a, b) in regs:
+                h = hist[nm]
+                if kind == "w":
+                    h[:] = [x for x in h if not (a <= x[2] and x[3] <= b and x[3] > x[2])]
+                h.append((i, kind, a, b))
+        deps.append(d)
+    return deps
+
+
+SYNC_ALL = True
+HOP, SELF, SLACK = 0.15, 0.08, 0.05
+
+
+def schedule(ops, deps):
+    n = len(ops)
+    succ = [[] for _ in range(n)]
+    for i, d in enumerate(deps):
+        for j in d:
+            succ[j].append(i)
+
+    after, prev = {}, {}
+    for i, o in enumerate(ops):
+        if "chain" in o:
+            if o["chain"] in prev:
+                after[i] = prev[o["chain"]]
+            prev[o["chain"]] = i
+    done = set()
+
+    def gap(j, i):
+        if ops[j]["e"] != ops[i]["e"] or ops[j]["sem"] is not None:
+            return HOP + ops[j]["lat"]
+        return SELF if deps[i][j] else 0.0
+    pr = [0.0] * n
+    for j in range(n - 1, -1, -1):
+        pr[j] = ops[j]["t"] + max([gap(j, i) + pr[i] for i in succ[j]] + [ops[j]["lat"]])
+    left = [len(d) for d in deps]
+    est = [0.0] * n
+    ready = [i for i in range(n) if left[i] == 0]
+    free, order, end = {}, [], [0.0] * n
+    while ready:
+        best = {}
+        may = [i for i in ready if i not in after or after[i] in done]
+        for i in may:
+            e = ops[i]["e"]
+            best[e] = min(best.get(e, 1e9), max(est[i], free.get(e, 0.0)))
+        e = min(best, key=lambda k: best[k])
+        cand = [i for i in may if ops[i]["e"] == e and est[i] <= best[e] + SLACK]
+        i = max(cand, key=lambda k: (pr[k], -k))
+        done.add(i)
+        st = max(est[i], free.get(e, 0.0))
+        end[i] = free[e] = st + ops[i]["t"]
+        ready.remove(i)
+        order.append(i)
+        for s in succ[i]:
+            est[s] = max(est[s], end[i] + gap(i, s))
+            left[s] -= 1
+            if left[s] == 0:
+                ready.append(s)
+    return order, end
+
+
+def rank_program(g, core, T, topo):
+    rank = T.rank_of(core)
+    if rank is None:
+        return
+    ops = build(T, topo, rank)
+    deps = edges(ops)
+    order, _ = schedule(ops, deps)
+    queue = {"V": g.vector, "S": g.scalar, "P": g.tensor, "G": g, "Y": g.sync}
+    pos, cnt = {}, {}
+    for i in order:
+        pos[i] = cnt.get(ops[i]["e"], 0)
+        cnt[ops[i]["e"]] = pos[i] + 1
+    seen, waits, needed = {}, {}, set()
+    for i in order:
+        e = ops[i]["e"]
+        if e == "X":
+            continue
+        w = {}
+        for j, hard in deps[i].items():
+            oj = ops[j]
+            if oj["sem"] is not None:
+                if (e, "dma", j) not in seen:
+                    seen[(e, "dma", j)] = 1
+                    w[("dma", j)] = j
+            elif (oj["e"] != e or hard) and pos[j] > seen.get((e, oj["e"]), -1):
+                if oj["e"] not in w or pos[j] > pos[w[oj["e"]]]:
+                    w[oj["e"]] = j
+        for k, j in w.items():
+            if ops[j]["sem"] is None:
+                seen[(e, k)] = pos[j]
+                needed.add(j)
+        waits[i] = list(w.values())
+    count, tick, sent = {}, {}, 0
+    for i in order:
+        if i in needed:
+            count[ops[i]["e"]] = tick[i] = count.get(ops[i]["e"], 0) + 1
+    for i in order:
+        o = ops[i]
+        if o["e"] == "X":
+            continue
+        for j in waits[i]:
+            oj = ops[j]
+            if oj["sem"] is None:
+                queue[o["e"]].wait_ge(T.sem["s" + oj["e"]], tick[j])
+            else:
+                queue[o["e"]].wait_ge(T.sem[oj["sem"]], oj.get("cnt", 16))
+        ins = o["fn"](g)
+        if o["sem"]:
+            ins.then_inc(T.sem[o["sem"]], 16)
+        elif i in needed:
+            ins.then_inc(T.sem["s" + o["e"]], 1)
+        sent += o.get("sent", 0)
+    g.wait_ge(T.sem.sent, sent)
+    for nm in ("yx", "yr", "y0", "y1"):
+        g.wait_ge(T.sem["d" + nm], 16)

@@ -6,37 +6,44 @@ B0 = C - LN * RO
 XW, RW, IW = 3280, 1408, 3088
 MAG = 12582912.0
 M30 = 1.5 * 2.0 ** 30
-ORG = 5.0 / 16
+MID, EPS = 0.25, 1.0 / 256
+HN = 1536.0
 BIG = 2.0 ** 70
-PEF = 0.75
-UCH = 384
-NF = 96
-NP = L - NF
-UV = 0
+PEF = 0.525
+VVS = (96, 128)
+VUS = (32, 0)
+SV, SU, VH = L - min(VVS), L - min(VUS), max(a + b for a, b in zip(VVS, VUS))
+CUT = 96
+IS = 1536
+YB = ("P2", "P3", "P4", "P0", "P3", "P4")
+YV = 640
 
-bf, f32, i32, u16 = "bfloat16", "float32", "int32", "uint16"
+bf, f32, i32, u16, f16 = "bfloat16", "float32", "int32", "uint16", "float16"
 SB = dict(
-    X=(XW, bf), R=(RW, f32), RI=(NV, i32), KI=(NV, i32), KF=(NV, f32), KD=(512, f32), YR=(NV, f32), YK=(NV, f32),
+    X=(XW, bf), R=(RW, f32), RI=(NV, i32), K2=(128, i32), KS=(128, f32), KD=(64, f32), YK=(128, f32),
+    YR=(NV, f32), Y1=(NV - YV, f32), DM=(NV, f32), RS=(256, f32),
     IO=(IW, f32), RTI=(12, i32), FNI=(8, i32), SNI=(8, i32), FN16=(8, u16), SN16=(8, u16),
-    LAND0=(LN, bf), LAND1=(LN, bf), LAND2=(LN, bf), LAND3=(LN, bf), SEND0=(LN, bf), SEND1=(LN, bf), SEND2=(LN, bf),
-    GONE=(LN, bf), W=(L, bf), WT=(768, bf), WIX=(LN, u16), WSP=(1536, bf), WREP=(1536, bf), NMF=(LN, f32), GG=(LN, f32),
-    O16=(384, u16), RVU=(384, f32), RVP=(384, f32), Y1=(288, f32), NM=(288, f32), HI=(L, bf),
-    C0=(L, f32), RDC=(L, bf), PHALF=(L, bf),
-    ZV=(3072, bf), ZU=(3072, bf), AB=(3072, bf), MXV=(3072, bf), MNV=(3072, bf), MXU=(3072, bf), MNU=(3072, bf),
+    W0=(L, bf), W1=(L, bf), W2=(L, bf), W3=(L, bf), SEND0=(LN, bf), SEND1=(LN, bf), SEND2=(LN, bf),
+    GONE=(LN, bf), WT=(256, bf), NF0=(LN, f16), NL=(384, f16), NB=(384, bf),
+    O16=(384, u16), RVU=(384, f32), NM=(288, f16), HI=(L, bf), TL=(L, f16), DG=(LN, f32), TT=(384, f32), EB=(L, bf),
+    RDC=(L, bf),
+    ZV=(16 * SV, bf), ZU=(16 * SU, bf), AB=(3072, bf), MXV=(16 * SV, bf), MNV=(16 * SV, bf), MXU=(16 * SU, bf), MNU=(16 * SU, bf),
+    ZH=(16 * VH, f16), MXH=(8 * VH, f16), MNH=(8 * VH, f16), OFS=(512, bf), OFL=(L, bf), MAGT=(L, bf),
+    DN=(24, f32), XO=(24, f32), JUNK=(L, bf),
     ST=(512, f32), RR=(32, f32), DIG=(32, bf), CS=(96, f32), C16=(12, u16), REP=(L, u16), REPA=(L, u16),
-    E=(12 * L, bf), EA=(12 * L, bf), SD=(L, f32), SDA=(L, f32), T1=(12, f32), T2=(12, f32), XO16=(12, u16),
-    T3=(24, f32), T4=(24, f32), XC=(L, bf), Y3=(L, f32), VAL=(L, bf),
-    Y4=(384, f32), HA=(384, bf), SG=(384, bf), A1=(LN, f32), A2=(LN, f32), SA=(384, f32), SBB=(384, f32),
-    JUNK=(L, bf), SUM=(4, f32), DP=(128, bf),
+    E=(12 * L, bf), EA=(12 * L, bf), SD=(L, f32), T1=(12, f32), T2=(12, f32), XO16=(12, u16),
+    T3=(24, f32), T4=(24, f32), XC=(L, bf), VAL=(L, bf),
+    HA=(384, bf), SG=(384, bf), A1=(LN, f32), A2=(LN, bf), SUM=(4, f32), DP=(128, bf),
     LV0=(36, f32), LV1=(36, f32), LV2=(36, f32), U0=(36, u16), U1=(36, u16), U2=(36, u16),
     OF0=(24, u16), OF1=(24, u16), OF2=(24, u16), PN0=(L, bf), PN1=(L, bf), PN2=(L, bf), H1=(12, f32), H2=(12, f32),
-    KG=(384, f32), KL=(48, f32), MID0=(24, f32), MID1=(24, f32), HH0=(24, f32), HH1=(24, f32), OO=(24, f32),
-    KM=(24, f32), SBL=(12, f32), Y5=(512, f32),
-    PI=(4, i32), COL=(16, f32), IF=(128, f32), NIF=(128, f32), IB=(128, bf), I2=(128, bf), IK=(256, bf),
-    IP=(128, bf), IN=(128, bf), WD=(144, bf), WM=(144, f32), WH=(144, f32), G2=(16, bf),
-    JB=(128, f32), BOP=(128, bf), BON=(128, bf), BOD=(128, bf), BOO=(128, bf), LM=(208, f32), CD=(L, bf),
-    EX=(512, bf), LM1=(768, bf), LM64=(768, bf), PEN8=(96, bf), RS8=(96, bf), RT=(256, bf), MXR=(768, bf),
-    MNR=(768, bf), RD=(L, bf), HALF=(L, bf), DC=(12, f32), DVU=(24, f32), PW=(32, f32),
+    KG=(384, f16), KL=(48, f32), MID0=(24, f32), MID1=(24, f32), HH0=(24, f32), HH1=(24, f32), OO=(24, f32),
+    KM=(24, f32), SBL=(12, f32),
+    PI=(4, i32), COL=(16, f32), IF=(128, f32), NIF=(128, f32), IA=(128, f32), IB=(128, bf), NI=(128, bf), IH=(128, bf),
+    IK=(256, bf), IN=(128, bf), IL=(128, bf), IQ=(128, bf), TP=(128, bf), TN=(128, bf),
+    WD=(144, bf), WM=(144, bf), WH=(144, bf), G2=(16, bf),
+    JB=(128, bf), BOP=(128, bf), BON=(128, bf), BOD=(128, bf), BOO=(128, bf), LM=(208, bf), CD=(L, bf), CDR=(L, bf),
+    EX=(512, bf), LM1=(768, bf), LM64=(768, bf), PEN8=(48, bf), RS8=(48, bf), RT=(256, bf), MXR=(512, bf),
+    MNR=(512, bf), HALF=(L, bf), DVU=(24, f32), PW=(16, f32),
 )
 SCRATCH, PLACE, _at = {}, {}, 0
 for _k, _v in SB.items():
@@ -50,9 +57,11 @@ SCRATCH["SMALL"] = ("sbuf", [128, _at], f32)
 for _b in range(8):
     SCRATCH["P%d" % _b] = ("psum", [128, 512], "float32")
     PLACE["P%d" % _b] = ("P%d" % _b, 0, 512, f32)
-DMAS = ["ring", "x", "rt", "xl", "fn", "k0", "k1", "snd", "yx", "yr", "y0", "y1"]
-SEMAPHORES = ["sV", "sS", "sP", "sG", "sent", "arr0", "arr1", "arr2"] + ["d" + n for n in DMAS]
+LOADS = ["ring", "x", "rt", "xl", "fn", "k0", "k1", "k2", "k3", "snd"]
+STORES = ["yx", "yr0", "yr1", "y0", "y1"]
+SEMAPHORES = ["sV", "sS", "sP", "sG", "sent", "arr0", "arr1", "arr2"] + ["d" + n for n in LOADS + STORES]
 CYC = 0.83e-3
+FAC, GAT, SCA = 1.05, 1.56, 3.8
 
 
 def build(T, topo, rank):
@@ -63,8 +72,13 @@ def build(T, topo, rank):
         if b is None:
             b = width
         rows = slice(0, 128) if p is None else slice(p[0], p[1])
-        v = T[buf][rows, at + a:at + b] if s == 1 else T[buf][rows, at + a:at + b:s]
-        return dict(v=v, n=len(range(a, b, s)), r=[(name, a, b)], dt=dt, ps=is_bank(name))
+        if s == 1:
+            v = T[buf][rows, at + a:at + b]
+        elif s > 0:
+            v = T[buf][rows, at + a:at + b:s]
+        else:
+            v = T[buf][rows, at + b - 1:(at + a - 1 if at + a else None):s]
+        return dict(v=v, n=len(range(a, b, abs(s))), r=[(name, a, b)], dt=dt, ps=is_bank(name))
 
     def ind(name, a, b, off):
         return dict(v=T[name][:, a:b].indirect(off["v"]), n=16 * off["n"], r=[(name, a, b)], o=off["r"], dt=SCRATCH[name][2], ps=False, ind=1)
@@ -72,7 +86,7 @@ def build(T, topo, rank):
     def val(x):
         return x["v"] if isinstance(x, dict) else x
 
-    def add(eng, fn, ins, outs, cyc, acc=False, sem=None, lat=0.0):
+    def add(eng, fn, ins, outs, cost, acc=False, sem=None, lat=0.0):
         rd, wr = [], []
         for x in ins:
             if isinstance(x, dict):
@@ -80,17 +94,18 @@ def build(T, topo, rank):
         for x in outs:
             wr += x["r"]
             rd += x.get("o", [])
-        ops.append(dict(e=eng, fn=fn, rd=rd, wr=wr, t=cyc * CYC, acc=acc, sem=sem, lat=lat))
+        t = (cost[0] * FAC + cost[1] * GAT + cost[2] * SCA + cost[3] + cost[4] * PEF) * CYC
+        ops.append(dict(e=eng, fn=fn, rd=rd, wr=wr, t=t, c=cost, acc=acc, sem=sem, lat=lat))
 
     def vcost(out, ins, rate=None):
         n = ins[0]["n"] if ins else out["n"]
         if "ind" in out:
-            return 60 + 3.8 * n
+            return (0, 0, n, 60, 0)
         if ins and "ind" in ins[0]:
-            return 60 + 1.56 * n
+            return (0, n, 0, 60, 0)
         if rate is None:
-            rate = 0.5 if all(x["dt"] in (bf, u16) for x in ins + [out]) else 1.0
-        return 1.2 * max(64, n * rate)
+            rate = 0.5 if all(x["dt"] in (bf, u16, f16) for x in ins + [out]) else 1.0
+        return (max(64, n * rate), 0, 0, 0, 0)
 
     def copy(out, a):
         add("V", lambda g: g.vector.tensor_copy(out["v"], a["v"]), [a], [out], vcost(out, [a]))
@@ -117,12 +132,12 @@ def build(T, topo, rank):
             fn = lambda g: g.scalar.activation(out["v"], a["v"], func, bias=val(bias), scale=val(scale))
         else:
             fn = lambda g: g.scalar.activation(out["v"], a["v"], func, bias=val(bias), scale=val(scale), accum_out=accum["v"])
-        cyc = 80 + 1.56 * a["n"] if "ind" in a else 1.2 * max(64, a["n"])
-        add("S", fn, [a, bias, scale], [out] + ([accum] if accum else []), cyc)
+        cost = (0, a["n"], 0, 80, 0) if "ind" in a else (max(64, a["n"]) + (25 if accum else 0), 0, 0, 0, 0)
+        add("S", fn, [a, bias, scale], [out] + ([accum] if accum else []), cost)
 
     def mm(out, lhsT, rhs, start, stop):
-        cyc = max(min(64, lhsT["n"]), rhs["n"]) * (4 if rhs["dt"] == f32 else 1) * PEF
-        add("P", lambda g: g.tensor.matmul(out["v"], lhsT["v"], rhs["v"], start, stop), [lhsT, rhs], [out], cyc, acc=True)
+        cyc = max(min(64, lhsT["n"]), rhs["n"]) * (4 if rhs["dt"] == f32 else 1)
+        add("P", lambda g: g.tensor.matmul(out["v"], lhsT["v"], rhs["v"], start, stop), [lhsT, rhs], [out], (0, 0, 0, 0, cyc), acc=True)
 
     def group(items):
         for i, (o, l, r) in enumerate(items):
@@ -133,119 +148,133 @@ def build(T, topo, rank):
             fn = lambda g: g.iota(out["v"], pat, base, cm)
         else:
             fn = lambda g: g.iota(out["v"], pat, base, cm, allow_small_or_imprecise_dtypes=True)
-        add("G", fn, [], [out], 190 + 2.4 * out["n"])
+        add("G", fn, [], [out], (157 + 2 * out["n"], 0, 0, 0, 0))
         ops[-1]["chain"] = "G"
 
     def dma(q, name, out, in_, rd, wr, us):
         eng = (lambda g: g.sync) if q == "Y" else (lambda g: g.scalar)
-        add(q, lambda g: eng(g).dma_start(out, in_), rd, wr, 80, sem="d" + name, lat=us)
+        add(q, lambda g: eng(g).dma_start(out, in_), rd, wr, (0, 0, 0, 80, 0), sem="d" + name, lat=us)
         if wr:
             ops[-1]["chain"] = q
 
     col = lambda j: ap("COL", j, j + 1)
+    P96 = (0, 96)
+    kin = [("RI", 0, NV), ("RI1", 0, NV)]
     dma("Y", "ring", T.RI[:], T.ring[:], [], [ap("RI")], 3.0)
     dma("S", "rt", T.RTI[:], T.rt[:], [], [ap("RTI")], 2.0)
     dma("Y", "x", T.X[:, 0:C], T.x[:], [], [ap("X", 0, C)], 5.0)
-    dma("S", "xl", T.LAND0[:], T.xl[:], [], [ap("LAND0")], 2.2)
+    dma("S", "xl", T.W0[:, 0:LN], T.xl[:], [], [ap("W0", 0, LN)], 2.2)
     dma("S", "fn", T.FNI[:, 0:6], T.fn[:], [], [ap("FNI")], 2.2)
-    mset(dict(ap("KI"), r=[("KI", 0, NV), ("KI", 0, 0)]), 0)
-    dma("Y", "k0", T.KI[0:128:16, :], T.kid[0:16:2, :], [], [ap("KI")], 2.5)
-    dma("Y", "k1", T.KI[1:128:16, :], T.kid[1:16:2, :], [], [ap("KI", 0, 0)], 2.5)
     dma("Y", "snd", T.SNI[:, 0:6], T.snd[:], [], [ap("SNI")], 2.2)
+    dma("Y", "k2", T.K2[:, 0:64], T.kid[:, 0:512], [], [ap("K2", 0, 64)], 2.5)
+    dma("Y", "k3", T.K2[:, 64:128], T.kid[:, 512:NV], [], [ap("K2", 64, 128)], 2.5)
     iota(ap("PI", 0, 1), [[1, 1]], 0, 1)
-    iota(ap("IO", 0, 512), [[1, 512]])
-    iota(ap("EX", p=(0, 32)), [[1, 32], [0, 16]], 0, -1)
+    iota(ap("IO", 0, 256), [[1, 256]])
     iota(ap("LM"), [[0, 13], [1, 16]])
     iota(ap("JB"), [[16, 8], [0, 16]])
+    iota(ap("OFS"), [[0, 2], [256, 16], [0, 16]], -2048)
+    iota(ap("EX", p=P96), [[1, 32], [0, 16]])
     iota(ap("G2"), [[0, 2], [16, 8]])
-    iota(ap("PEN8"), [[0, 12], [16, 8]])
-    iota(ap("LM64", p=(0, 96)), [[-16, 6], [0, 8], [-1, 16]], 0, 1)
-    for a in range(512, IW, 512):
-        act(ap("IO", a, min(IW, a + 512)), ap("IO", 0, min(IW - a, 512)), F.Identity, bias=float(a))
-    ts(ap("PI", 1, 2), ap("PI", 0, 1), 15, A.bitwise_and)
-    copy(ap("COL", 0, 2), ap("PI", 0, 2))
-    tt(col(2), col(0), col(1), A.subtract)
-    ts(col(3), col(2), 15.0, A.add)
-    J = ap("IO", 0, 128)
-    ts(ap("IF"), J, col(0), A.is_equal)
-    for name, a, sc in (("NIF", 0, -1.0), ("IB", 0, 1.0), ("I2", 0, -2.0), ("IK", 0, -64.0), ("IK", 128, 1.0),
-                        ("IP", 0, 16384.0), ("IN", 0, -16384.0)):
+    iota(ap("OFL"), [[0, 12], [256, 16]], -2048)
+    iota(ap("NB"), [[1, 384]], -192)
+    iota(ap("PEN8"), [[0, 6], [16, 8]])
+    iota(ap("LM64", p=P96), [[-16, 6], [0, 8], [-1, 16]], 0, 1)
+    for a, n in ((256, 256), (512, 512), (1024, IS - 1024)):
+        act(ap("IO", a, a + n), ap("IO", 0, n), F.Identity, bias=float(a))
+    iota(ap("IO", IS, IW), [[1, IW - IS]], IS)
+    for j, m in ((1, 15), (2, 31), (3, 7)):
+        ts(ap("PI", j, j + 1), ap("PI", 0, 1), m, A.bitwise_and)
+    copy(ap("COL", 0, 4), ap("PI"))
+    tt(col(4), col(0), col(1), A.subtract)
+    ts(col(5), col(4), 15.0, A.add)
+    ts(ap("IF"), ap("IO", 0, 128), col(0), A.is_equal)
+    for name, a, sc in (("IB", 0, 1.0), ("NI", 0, -1.0), ("IH", 0, 0.5), ("IK", 0, -64.0), ("IK", 128, 1.0), ("NIF", 0, -1.0),
+                        ("IN", 0, -16384.0), ("IL", 0, 1344.0), ("IQ", 0, -2.0 ** 20), ("IA", 0, 32768.0)):
         act(ap(name, a, a + 128), ap("IF"), F.Identity, scale=sc)
-    ts(ap("WD"), ap("IO", 0, 144), col(3), A.is_equal)
-    ts(ap("G2"), ap("G2"), col(2), A.is_equal, 2048.0, A.mult)
-    ts(ap("JB"), ap("JB"), col(2), A.is_equal)
+    act(ap("MAGT"), ap("IO", 0, L), F.Identity, scale=0.0, bias=MAG)
+    act(ap("HALF"), ap("IO", 0, L), F.Identity, scale=0.0, bias=-0.5)
+    ts(ap("WD"), ap("IO", 0, 144), col(5), A.is_equal)
+    ts(ap("G2"), ap("G2"), col(4), A.is_equal, 2048.0, A.mult)
+    ts(ap("JB"), ap("JB"), col(4), A.is_equal)
     ts(ap("LM"), ap("LM"), col(1), A.is_equal)
-    mset(ap("PW", 0, 16), 0.5)
-    scan(ap("PW", 16, 32), ap("PW", 0, 16), ap("PW", 0, 16), A.mult, A.max, 2.0 ** 29)
-    tt(ap("PW", 0, 16), ap("PW", 16, 32), ap("LM", 0, 16), A.mult)
-    add("V", lambda g: g.vector.tensor_reduce(col(4)["v"], ap("PW", 0, 16)["v"], AxisListType.X, A.add), [ap("PW", 0, 16)], [col(4)], 80)
-    ts(col(5), col(4), -2.0, A.mult)
-    for name, sc in (("BOP", 16384.0), ("BON", -16384.0), ("BOO", 2.0 ** 40), ("BOD", col(4))):
+    mset(ap("MXR"), 0.0)
+    mset(ap("MXR", s=16), -1024.0)
+    act(ap("CD"), ap("MXR", 0, L), F.Identity, scale=-2.0 ** 19)
+    act(ap("RDC"), ap("MXR", 0, L), F.Identity, scale=0.0, bias=0.5)
+    scan(ap("EB"), ap("RDC"), ap("CD"), A.mult, A.max)
+    tt(ap("PW"), ap("EB", 0, 16), ap("LM", 0, 16), A.mult)
+    add("V", lambda g: g.vector.tensor_reduce(col(6)["v"], ap("PW")["v"], AxisListType.X, A.add), [ap("PW")], [col(6)], (64, 0, 0, 0, 0))
+    act(ap("CDR"), ap("EB"), F.Identity, scale=-1.0)
+    act(ap("EB"), ap("LM", 0, L), F.Identity, scale=BIG, bias=-BIG)
+    group([(ap("P3", 0, L), ap("IB"), ap("CDR")), (ap("P3", 0, L), ap("IB"), ap("EB"))])
+    act(ap("CD"), ap("P3", 0, L), F.Identity)
+    ts(col(6), col(6), 0.5, A.mult)
+    for name, sc in (("BOO", 2.0 ** 40), ("BOD", col(6)), ("BOP", 16384.0), ("BON", -16384.0)):
         act(ap(name), ap("JB"), F.Identity, scale=sc)
-    act(ap("SA", 0, L), ap("LM", 0, L), F.Identity, scale=col(5))
-    act(ap("SBB", 0, L), ap("LM", 0, L), F.Identity, scale=BIG, bias=-BIG)
-    tt(ap("CD"), ap("SA", 0, L), ap("SBB", 0, L), A.add)
-    ts(ap("EX", p=(0, 32)), ap("EX", p=(0, 32)), 0.0, A.is_equal, -1.0, A.mult)
-    ts(ap("LM1", p=(0, 96)), ap("LM64", p=(0, 96)), 0.0, A.is_equal)
-    act(ap("LM64", p=(0, 96)), ap("LM1", p=(0, 96)), F.Identity, scale=64.0)
-    ts(ap("PEN8"), ap("PEN8"), col(2), A.not_equal, 2.0 ** 20, A.mult)
-    for name, base, st, c in (("RS8", 0.0, 8, 2.0 ** 20), ("RT", -128.0, 16, 2.0 ** 30), ("MXR", 0.0, 16, -1024.0), ("RD", 0.0, 16, -8 * BIG)):
-        mset(ap(name), base)
-        mset(ap(name, s=st), c)
-    act(ap("MNR"), ap("MXR"), F.Identity, scale=-1.0)
-    mset(ap("HALF"), -0.5)
-    copy(ap("WIX"), ap("IO", 0, LN))
-    mset(ap("WSP"), -1024.0)
+    ts(ap("EX", p=P96), ap("EX", p=P96), ap("COL", 2, 3, p=P96), A.is_equal, -1.0, A.mult)
+    ts(ap("LM1", p=P96), ap("LM64", p=P96), 0.0, A.is_equal)
+    ts(ap("LM64", p=P96), ap("LM64", p=P96), 0.0, A.is_equal, 64.0, A.mult)
+    ts(ap("PEN8"), ap("PEN8"), col(4), A.not_equal, 2.0 ** 20, A.mult)
+    for name, n, st, sc, b in (("RS8", 48, 2, -1024.0, 0.0), ("RT", 256, 1, -2.0 ** 20, -128.0), ("MNR", 512, 1, -1.0, 0.0),
+                               ("RDC", L, 1, BIG / 128, 0.0)):
+        act(ap(name), ap("MXR", 0, n * st, st), F.Identity, scale=sc, bias=b)
     mset(ap("X", C, XW), 0.0)
     act(ap("R", NV, RW), ap("IO", 0, RW - NV), F.Identity)
-    mset(ap("DP"), 0.0)
-    mset(ap("PHALF"), 0.5)
-    copy(ap("RDC"), ap("RD"))
-    ts(ap("DC"), ap("IO", 0, L, 16), col(1), A.add, float(C + 1), A.add)
+    ts(ap("DN", 0, 24, 2), ap("IO", 0, L, 16), col(1), A.add, float(C + 1), A.add)
     ts(ap("DVU"), ap("IO", 0, 384, 16), col(1), A.add, float(NV), A.add)
-    ts(ap("R", 0, 512), ap("RI", 0, 512), 0.0, A.add)
-    ts(ap("R", 512, NV), ap("RI", 512, NV), ORG, A.add)
+    ts(ap("NL"), ap("NB"), B0 + 192 - HN, A.add)
+    ts(ap("R", 0, 512), dict(ap("RI", 0, 512), r=kin), MID - EPS, A.add)
+    ts(ap("R", 512, NV), dict(ap("RI", 512, NV), r=kin), MID + EPS, A.add)
     copy(ap("FN16", 0, 6), ap("FNI", 0, 6))
     copy(ap("SN16", 0, 6), ap("SNI", 0, 6))
 
-    def firsts(key16, keys, rep, E, bank, sd, reset):
-        copy(ap(rep), ind("IO", 0, IW, key16))
-        items = [(ap(bank, 0, L), ap("IB"), ap("CD"))]
-        for m in range(12):
+    def matches(key16, keys, top, rep, E, bank, first, parts):
+        items = [(ap(bank, 0, L), ap("IB"), ap(first))]
+        for m in parts:
+            if m == parts[0] or m == 0:
+                e = parts[0] if m < parts[0] else 12
+                copy(ap(rep, 16 * m, 16 * e), ind("IO", 0, top, ap(key16[0], key16[1] + m, key16[1] + e)))
             ts(ap(E, m * L + 16 * m, m * L + L), ap(rep, 16 * m, L), keys(m), A.is_equal)
             items.append((ap(bank, 16 * m, 16 * m + 16), ap("BOD"), ap(E, m * L + 16 * m, m * L + 16 * m + 16)))
             if m < 11:
                 items.append((ap(bank, 16 * m + 16, L), ap("BOO"), ap(E, m * L + 16 * m + 16, m * L + L)))
         group(items)
-        scan(ap(sd), ap(reset), ap(bank, 0, L), A.add, A.max)
+
+    def to_list(out, src, n):
+        group([(out, ap("WD", 15 - q, 143 - q), ap(src, q, n, 16)) for q in range(16)])
 
     def nodes(k):
-        lv, u, of = "LV%d" % k, "U%d" % k, "OF%d" % k
+        lv, u = "LV%d" % k, "U%d" % k
         ts(ap("H1"), ap(lv, 0, 12), 512.0, A.is_ge, -512.0, A.mult)
         ts(ap("H2"), ap(lv, 0, 12), 512.0, A.is_lt, 512.0, A.mult)
         tt(ap(lv, 24, 36), ap(lv, 0, 12), ap("H1"), A.add)
         tt(ap(lv, 12, 24), ap(lv, 24, 36), ap("H2"), A.add)
         copy(ap(u), ap(lv))
-        firsts(ap(u, 24, 36), lambda m: ap(lv, 24 + m, 25 + m), "REPA", "EA", "P7", "SDA", "RD")
-        tt(ap("T3", 0, 12), ap(lv, 0, 12), ap("SDA", 15, L, 16), A.max)
-        tt(ap("T3", 12, 24), ap(lv, 12, 24), ap("SDA", 15, L, 16), A.max)
+
+    def acting(k, bank):
+        lv, u, of, pn = "LV%d" % k, "U%d" % k, "OF%d" % k, "PN%d" % k
+        matches((u, 24), lambda m: ap(lv, 24 + m, 25 + m), 512, "REPA", "EA", bank, "CDR", range(12))
+        act(ap(pn), ap(bank, 0, L), F.Relu)
+        lose = ap(bank, L, L + 12)
+        to_list(lose, pn, L)
+        tt(ap("T3", 0, 12), lose, ap(lv, 0, 12), A.max)
+        tt(ap("T3", 12, 24), lose, ap(lv, 12, 24), A.max)
         tt(ap("T4"), ap("T3"), ap("DVU"), A.min)
         copy(ap(of), ap("T4"))
-        act(ap("PN%d" % k), ind("IO", 0, IW, ap(of, 0, 12)), F.Relu, scale=16384.0, bias=-1023.5 * 16384)
-        act(ap("PN%d" % k), ap("PN%d" % k), F.Identity, bias=0.5)
 
     copy(ap("LV0", 0, 12), ap("RTI"))
     nodes(0)
+    acting(0, "P7")
 
     def kids():
-        kin = dict(ap("KI"), r=[("KI", 0, NV), ("KI", 0, 0)])
-        copy(ap("KF"), kin)
-        act(ap("KG"), ind("KF", 0, NV, ap("U0", 0, 24)), F.Identity)
-        ts(col(6), col(1), 2.0, A.is_lt, 0.25, A.mult)
+        dma("Y", "k0", T.RI[0:128:16, :], T.kid[0:16:2, :], [], [ap("RI")], 2.5)
+        dma("Y", "k1", T.RI[1:128:16, :], T.kid[1:16:2, :], [], [dict(r=kin[1:])], 2.5)
+        copy(ap("KG"), dict(ind("RI", 0, NV, ap("U0", 0, 24)), r=kin))
+        ts(col(7), col(1), 2.0, A.is_lt, 0.25, A.mult)
         ts(col(8), col(1), 0.5, A.mult, -0.25, A.add)
-        tt(col(7), col(8), col(6), A.mult)
-        act(ap("WM"), ap("WD"), F.Identity, scale=col(6))
-        ts(ap("WH"), ap("WD"), col(7), A.mult, 4.0, A.mult)
+        tt(col(9), col(8), col(7), A.mult)
+        act(ap("WM"), ap("WD"), F.Identity, scale=col(7))
+        ts(ap("WH"), ap("WD"), col(9), A.mult, 4.0, A.mult)
         for j, w in enumerate(("WM", "WH")):
             group([(ap("P6", 24 * j, 24 * j + 24), ap(w, 15 - q, 143 - q), ap("KG", q, 384, 16)) for q in range(16)])
         act(ap("KL"), ap("P6", 0, 48), F.Identity)
@@ -261,82 +290,113 @@ def build(T, topo, rank):
 
     def level(t, l):
         k = (t & 1) if l == 0 else 2
-        U, OF, PN = "U%d" % k, "OF%d" % k, "PN%d" % k
-        p0 = B0 + LN * t
-        nameL = ap("IO", p0, p0 + LN)
-        nameF = ap("NMF") if t == 0 else ap("IO", p0 - LN, p0)
+        U, OF, PN, W = "U%d" % k, "OF%d" % k, "PN%d" % k, "W%d" % t
+        nameF = ap("NF0") if t == 0 else ap("NL", LN * t - LN, LN * t)
         thr = 2.0 ** t / 128
-        last = t == RO - 1 and l == 1
-        copy(ap("O16", 0, L), ind("R", 0, RW, ap(U, 0, 12)))
-        copy(ap("O16", L, 384), ind("R", 0, RW, ap(U, 12, 24)))
+        begin, last = t == 0 and l == 0, t == RO - 1 and l == 1
+        VV, VU = VVS[l], VUS[l]
+        SV, SU = L - VV, L - VU
+        copy(ap("O16", 0, L), dict(ind("RI", 0, NV, ap(U, 0, 12)), r=kin) if begin else ind("R", 0, RW, ap(U, 0, 12)))
         X = lambda a, b: ind("X", 0, XW, ap("O16", a, b))
-        plain = [(a, min(NP, a + 32)) for a in range(0, NP, 32)]
-        fused = [(a, min(L, a + 32)) for a in range(NP, L, 32)]
-        for a, b in plain:
-            act(ap("ZV", 16 * a, 16 * b), X(a, b), F.Identity)
-        for a, b in fused:
-            tt(ap("ZV", 16 * a, 16 * b), X(a, b), ap("WREP", 16 * (a - NP), 16 * (b - NP)), A.subtract)
-        act(ap("RVU"), ind("R", 0, RW, ap(U, 0, 24)), F.Identity)
-        act(ap("Y1"), ap("RVU", 0, 288), F.Identity, bias=MAG)
-        act(ap("NM"), ap("Y1"), F.Identity, bias=-MAG)
-        act(ap("HI"), ap("RVU", 0, L), F.Identity, bias=128.0, scale=1.0 / 64)
-        if l == 0:
-            act(ap("RVP"), ap("RVU"), F.Identity, bias=thr)
-        else:
-            act(ap("RVP", L, 384), ap("RVU", L, 384), F.Identity)
-        for c, (a, b) in enumerate(plain):
-            o = ap("P%d" % (2 + c % 2), 0, 16 * (b - a))
-            group([(o, ap("IB"), ap("ZV", 16 * a, 16 * b)),
-                   (o, ap("WT", 128 * c, 128 * c + 128, p=(0, 32)), ap("EX", 0, 16 * (b - a), p=(0, 32)))])
-            act(ap("AB", 16 * a, 16 * b), o, F.Abs)
-        for a, b in fused:
-            act(ap("AB", 16 * a, 16 * b), ap("ZV", 16 * a, 16 * b), F.Abs)
-        P96 = (0, 96)
-        for h in range(2):
-            bk = "P%d" % h
-            items = [(ap(bk, 0, 256, p=P96), ap("HI", 96 * h, 96 * h + 96), ap("IK")),
-                     (ap(bk, 0, 128, p=P96), ap("NM", 96 * h, 96 * h + 96), ap("IF"))]
-            items += [(ap(bk, s, 256, 16, p=P96), ap("AB", 1536 * h + s, 1536 * h + 1536, 16), ap("G2")) for s in range(16)]
+
+        def stepped(o0, h0, n):
+            for a in range(0, n, 32):
+                b = min(n, a + 32)
+                tt(ap("ZH", 16 * (h0 + a), 16 * (h0 + b)), X(o0 + a, o0 + b), ap("OFS", 0, 16 * (b - a)), A.add)
+            for a in range(h0, h0 + n, 16):
+                z0, z1 = 16 * a, 16 * a + 256
+                scan(ap("MXH", 8 * a, 8 * a + 128), ap("ZH", z0, z1, 2), ap("ZH", z0 + 1, z1, 2), A.max, A.max, -4096.0)
+                scan(ap("MNH", 8 * a, 8 * a + 128, -1), ap("ZH", z0, z1, -2), ap("ZH", z0, z1 - 1, -2), A.min, A.min, 4096.0)
+
+        def plain(z, mx, mn, o0, n):
+            for a in range(0, n, 32):
+                b = min(n, a + 32)
+                act(ap(z, 16 * a, 16 * b), X(o0 + a, o0 + b), F.Identity)
+            for a in range(0, n, 32):
+                b = min(n, a + 32)
+                scan(ap(mx, 16 * a, 16 * b), ap("MXR", 0, 16 * (b - a)), ap(z, 16 * a, 16 * b), A.add, A.max)
+                scan(ap(mn, 16 * a, 16 * b), ap("MNR", 0, 16 * (b - a)), ap(z, 16 * a, 16 * b), A.add, A.min)
+
+        def midrange(c0, own, a, b, rounded):
+            o = lambda a, b: ap("P4", c0 + a, c0 + b)
+            mx, mn = ("MXV", "MNV") if own else ("MXU", "MNU")
+            (h0, h1, hz), (s0, s1) = ((SV, L, 0), (0, SV)) if own else ((0, VU, VV), (VU, L))
+            items = [(o(a, b), ap("IH"), ap("HALF", a, b)), (o(a, b), ap("NI"), ap(W, a, b))]
+            x, y = max(a, h0), min(b, h1)
+            if x < y:
+                z0, z1 = 8 * (hz + x - h0), 8 * (hz + y - h0)
+                items += [(o(x, y), ap("NI"), ap("OFL", 0, y - x)), (o(x, y), ap("IH"), ap("MXH", z0 + 7, z1, 8)),
+                          (o(x, y), ap("IH"), ap("MNH", z0, z1, 8))]
+            x, y = max(a, s0), min(b, s1)
+            if x < y:
+                items += [(o(x, y), ap("IH"), ap(m, 16 * (x - s0) + 15, 16 * (y - s0), 16)) for m in (mx, mn)]
+            if rounded:
+                items.append((o(a, b), ap("IB"), ap("MAGT", a, b)))
             group(items)
+
+        stepped(SV, 0, VV)
+        plain("ZV", "MXV", "MNV", 0, SV)
+        act(ap("RVU"), ind("R", 0, RW, ap(U, 0, 24)), F.Identity)
+        copy(ap("O16", L, 384), ap("RVU", L, 384))
+        ts(ap("HI"), ap("O16", 0, L), 1.0 / 64, A.mult, 128.0, A.add)
+        ts(ap("NM"), ap("O16", 0, 288), -HN, A.add)
+        for i, c in enumerate(sorted(range(6), key=lambda c: (c < 3, 32 * c < SV, c))):
+            o, q = ap(YB[i]), (32 * (c % 3), 32 * (c % 3) + 32)
+            items = [(o, ap("WT", 128 * (c // 3), 128 * (c // 3) + 128, p=q), ap("EX", p=q))]
+            if 32 * c < SV:
+                items.append((o, ap("IB"), ap("ZV", 512 * c, 512 * c + 512)))
+            else:
+                items += [(o, ap("NI"), ap("OFS")), (o, ap("IB"), ap("ZH", 512 * c - 16 * SV, 512 * c - 16 * SV + 512))]
+            group(items)
+            act(ap("AB", 512 * c, 512 * c + 512), o, F.Abs)
+        for h in (1, 0):
+            bk = "P%d" % h
+            keys = [(ap(bk, 0, 256, p=P96), ap("HI", 96 * h, 96 * h + 96), ap("IK")),
+                    (ap(bk, 0, 128, p=P96), ap("NM", 96 * h, 96 * h + 96), ap("IB"))]
+            keys += [(ap(bk, s, 256, 16, p=P96), ap("AB", 1536 * h + s, 1536 * h + 1536, 16), ap("G2")) for s in range(16)]
+            group(keys)
             scan(ap("ST", 256 * h, 256 * h + 256, p=P96), ap("RT", p=P96), ap(bk, 0, 256, p=P96), A.add, A.min)
             ts(ap("RR", 16 * h, 16 * h + 16, p=P96), ap("ST", 256 * h + 15, 256 * h + 256, 16, p=P96), M30, A.add, M30, A.subtract)
             tt(ap("DIG", 16 * h, 16 * h + 16, p=P96), ap("ST", 256 * h + 15, 256 * h + 256, 16, p=P96), ap("RR", 16 * h, 16 * h + 16, p=P96), A.subtract)
-        items = [(ap("P2", 0, 96), ap("IB"), ap("PEN8"))]
-        for h in range(2):
-            for m in range(6):
-                for ab in range(2):
-                    items.append((ap("P2", 48 * h + 8 * m, 48 * h + 8 * m + 8), ap("LM64" if ab else "LM1", 128 * m, 128 * m + 128, p=P96),
-                                  ap("DIG", 16 * h + 8 * ab, 16 * h + 8 * ab + 8, p=P96)))
-        group(items)
-        scan(ap("CS"), ap("RS8"), ap("P2", 0, 96), A.add, A.min)
-        copy(ap("C16"), ap("CS", 7, 96, 8))
-        group([(ap("P5", 0, 96), ap("IF"), ap("NM", 0, 96)), (ap("P5", 0, 96), ap("NIF"), nameL)])
-        group([(ap("P5", 96, L), ap("IF"), ap("NM", L, 288)), (ap("P5", 96, L), ap("NIF"), nameL)])
-        group([(ap("P5", L, 288), ap("IF"), ap("RVU", 96, L)), (ap("P5", L, 288), ap("NIF"), nameF)])
+            group([(ap(bk, 256, 304), ap("IB"), ap("PEN8"))]
+                  + [(ap(bk, 256 + 8 * m, 264 + 8 * m), ap("LM64" if ab else "LM1", 128 * m, 128 * m + 128, p=P96),
+                      ap("DIG", 16 * h + 8 * ab, 16 * h + 8 * ab + 8, p=P96)) for m in range(6) for ab in range(2)])
+            scan(ap("CS", 48 * h, 48 * h + 48), ap("RS8"), ap(bk, 256, 304), A.add, A.min)
+            copy(ap("C16", 6 * h, 6 * h + 6), ap("CS", 48 * h + 7, 48 * h + 48, 8))
+        nb = ap("NB", LN * t, LN * t + LN)
+        group([(ap("P5", 0, 96), ap("IB"), ap("NM", 0, 96)), (ap("P5", 0, 96), ap("NI"), nb),
+               (ap("P5", 96, L), ap("IB"), ap("NM", L, 288)), (ap("P5", 96, L), ap("NI"), nb)])
+        tt(ap("TL"), ap("P5", 0, L), ap("LM", t, t + L), A.mult)
+        d = ap("P5", L, 288)
         if l == 0:
-            group([(ap("P5", 288, 480), ap("IF"), ap("RVU", 0, L)), (ap("P5", 288, 480), ap("NIF"), ap("NM", 0, L))])
-            act(ap("SG", 0, L), ap("P5", 288, 480), F.Sign, bias=-0.2)
-        act(ap("A1"), ap("P5", L, 288), F.Abs, bias=-ORG / 2 - thr / 2 + 1.0 / 512)
-        act(ap("A2"), ap("A1"), F.Abs, bias=-ORG / 2)
-        act(ap("P5", L, 288), ap("A2"), F.Relu, scale=-2.0 ** 22, bias=2.0 ** 21 * thr)
-        tt(ap("P5", 0, L), ap("P5", 0, L), ap("LM", t, t + L), A.mult)
-        tt(ap("P5", L, 288), ap("P5", L, 288), ap("GG"), A.min)
-        tt(ap("C0", 0, 96), ap("RVU", 0, 96), ap("P5", 0, 96), A.subtract)
-        tt(ap("RVP", L, 288), ap("RVP", L, 288), ap("P5", 96, L), A.subtract)
-        tt(ap("C0", 96, L), ap("RVU", 96, L), ap("P5", L, 288), A.add)
-        for c in range(4):
-            for o, r, op in (("MXV", "MXR", A.max), ("MNV", "MNR", A.min)):
-                scan(ap(o, 768 * c, 768 * c + 768), ap(r), ap("ZV", 768 * c, 768 * c + 768), A.add, op)
-        group([(ap("P4", 0, L), ap("IB"), ap("HALF")), (ap("P4", 0, NP), ap("I2"), ap("W", 0, NP)),
-               (ap("P4", 0, L), ap("IB"), ap("MXV", 15, 3072, 16)), (ap("P4", 0, L), ap("IB"), ap("MNV", 15, 3072, 16))])
+            group([(ap("P5", 288, 480), ap("IF"), ap("RVU", 0, L)), (ap("P5", 288, 480), ap("NI"), ap("NM", 0, L))])
+            act(ap("SG", 0, L), ap("P5", 288, 480), F.Sign, bias=-HN - MID)
+            group([(d, ap("IB"), ap("NM", 96, L)), (d, ap("NI"), nameF)])
+            act(ap("A2"), d, F.Abs)
+            act(ap("TP"), ap("IF"), F.Identity, scale=thr)
+            act(ap("TN"), ap("IF"), F.Identity, scale=-thr)
+        else:
+            group([(d, ap("IF"), ap("RVU", 96, L)), (d, ap("NI"), nameF)])
+            act(ap("A1"), d, F.Abs, bias=-HN - MID)
+            act(ap("A2"), ap("A1"), F.Relu, bias=-thr)
+        group([(d, ap("IQ"), ap("A2")), (d, ap("NI"), nameF)])
+        act(ap("DG"), d, F.Relu, bias=C - HN)
+        bv, bu = ap("P7", 0, L), ap("P7", L, 384)
+        group([(bu, ap("IF"), ap("RVU", 0, L)), (bu, ap("NIF"), ap("RVU", L, 384))] + ([(bu, ap("TP"), ap("SG", 0, L))] if l == 0 else []))
+        group([(ap("P5", 0, L), ap("IF"), ap("RVU", 0, L)), (ap("P5", 0, 96), ap("NI"), ap("TL", 0, 96)),
+               (ap("P5", 0, 96), ap("IL"), ap("LM", t, t + 96)), (ap("P5", 96, L), ap("IF"), ap("DG"))])
+        act(ap("RVU", 0, L), ap("P5", 0, L), F.Identity)
+        group([(bv, ap("IF"), ap("RVU", L, 384)), (bv, ap("NIF"), ap("RVU", 0, L)), (ap("P7", 0, 96), ap("NI"), ap("TL", 96, L)),
+               (ap("P7", 0, 96), ap("IL"), ap("LM", t, t + 96))] + ([(bv, ap("TN"), ap("SG", 0, L))] if l == 0 else []))
         if l == 0:
-            act(ap("SG", L, 384), ap("P4", 0, L), F.Sign, scale=-1.0, bias=1.0)
-        act(ap("Y4", 0, L), ap("P4", 0, L), F.Identity, scale=0.5, bias=MAG)
-        act(ap("HA", 0, L), ap("Y4", 0, L), F.Abs, bias=-MAG)
+            midrange(L, True, 0, L, False)
+            act(ap("SG", L, 384), ap("P4", L, 384), F.Sign, scale=-1.0, bias=0.5)
+        midrange(0, True, 0, L, True)
+        act(ap("HA", 0, L), ap("P4", 0, L), F.Abs, bias=-MAG)
         if l == 0:
             if t == 0:
                 kids()
-            group([(ap("P6", 0, 24), ap("WD", 15 - q, 143 - q), ap("SG", q, 384, 16)) for q in range(16)])
+            to_list(ap("P6", 0, 24), "SG", 384)
             act(ap("OO", 0, 12), ap("P6", 0, 12), F.Sign)
             act(ap("OO", 12, 24), ap("P6", 0, 12), F.Sign)
             act(ap("SBL"), ap("P6", 12, 24), F.Sign, bias=-1.0)
@@ -345,46 +405,38 @@ def build(T, topo, rank):
             tt(ap("H1"), ap("SBL"), ap("KM", 12, 24), A.mult)
             tt(ap("LV2", 0, 12), ap("H1"), ap("KM", 0, 12), A.add)
             nodes(2)
-        nu = 3072 // UCH
-        for c in range(nu):
-            o, src = ap("ZU", UCH * c, UCH * c + UCH), X(L + UCH // 16 * c, L + UCH // 16 * (c + 1))
-            if c < UV:
-                copy(o, src)
-            else:
-                act(o, src, F.Identity)
+        stepped(L, VV, VU)
+        plain("ZU", "MXU", "MNU", L + VU, SU)
         act(ap("RDC", 15, L, 16), ap("CS", 7, 96, 8), F.Relu, scale=4 * BIG, bias=-(C - 0.5) * 4 * BIG)
         act(ap("XC"), ind("X", 0, XW, ap("C16")), F.Identity)
-        firsts(ap("C16"), lambda m: ap("CS", 8 * m + 7, 8 * m + 8), "REP", "E", "P3", "SD", "RDC")
-        tt(ap("T1"), ap("CS", 7, 96, 8), ap("SD", 15, L, 16), A.max)
-        tt(ap("T2"), ap("T1"), ap("DC"), A.min)
-        copy(ap("XO16"), ap("T2"))
-        group([(ap("P6", 0, L), ap("IB"), ap("HALF")), (ap("P6", 0, L), ap("IB"), ap("W")), (ap("P6", 0, L), ap("IB"), ap("XC"))])
-        act(ap("Y3"), ap("P6", 0, L), F.Identity, scale=0.5, bias=MAG)
-        act(ap("VAL"), ap("Y3"), F.Identity, bias=-MAG)
+        matches(("C16", 0), lambda m: ap("CS", 8 * m + 7, 8 * m + 8), IW, "REP", "E", "P2", "CD", [6, 7, 8, 9, 10, 11, 0, 1, 2, 3, 4, 5])
+        copy(ap("DN", 1, 24, 2), ap("CS", 7, 96, 8))
+        scan(ap("SD"), ap("RDC"), ap("P2", 0, L), A.add, A.max)
+        scan(ap("XO"), ap("SD", 7, L, 8), ap("DN"), A.min, A.max)
+        copy(ap("XO16"), ap("XO", 1, 24, 2))
+        o = ap("P6", 0, L)
+        group([(o, ap("IH"), ap(x)) for x in ("HALF", W, "XC")] + [(o, ap("IB"), ap("MAGT"))])
+        act(ap("VAL"), o, F.Identity, bias=-MAG)
         copy(ind("X", 0, XW, ap("XO16")), ap("VAL"))
         if last:
             dma("Y", "yx", T.yx[:], T.X[:, 0:C], [ap("X", 0, C)], [], 4.0)
         elif l == 1:
             hand_on(t)
-        for c in range(4):
-            for o, r, op in (("MXU", "MXR", A.max), ("MNU", "MNR", A.min)):
-                scan(ap(o, 768 * c, 768 * c + 768), ap(r), ap("ZU", 768 * c, 768 * c + 768), A.add, op)
-        group([(ap("P4", 0, L), ap("IB"), ap("HALF")), (ap("P4", 0, L), ap("I2"), ap("W")),
-               (ap("P4", 0, L), ap("IB"), ap("MXU", 15, 3072, 16)), (ap("P4", 0, L), ap("IB"), ap("MNU", 15, 3072, 16))])
-        act(ap("Y4", L, 384), ap("P4", 0, L), F.Identity, scale=0.5, bias=MAG)
-        act(ap("HA", L, 384), ap("Y4", L, 384), F.Abs, bias=-MAG)
-        for bk, a, b, i1, i2, d in (("P0", "BOP", "BON", "IP", "IN", "HALF"), ("P1", "BON", "BOP", "IN", "IP", "PHALF")):
-            o = ap(bk, 0, L)
-            group([(o, ap("DP"), ap(d)), (o, ap(i2), ap(PN)), (o, ap(a), ap("HA", 0, L)), (o, ap(b), ap("HA", L, 384))])
-        tt(ap("SBB", 0, L), ap("RVP", L, 384), ap("P0", 0, L), A.min)
-        tt(ap("SBB", L, 384), ap("RVP" if l == 0 else "RVU", 0, L), ap("P0", 0, L), A.min)
-        tt(ap("SA", 0, L), ap("C0"), ap("P1", 0, L), A.min)
-        tt(ap("SA", L, 384), ap("RVU", L, 384), ap("P1", 0, L), A.min)
-        tt(ind("R", 0, RW, ap(OF)), ap("SA"), ap("SBB"), A.max)
+        if l == 0:
+            acting(2, "P6")
+        for i, (a, b) in enumerate(((0, CUT), (CUT, L))):
+            midrange(0, False, a, b, True)
+            act(ap("HA", L + a, L + b), ap("P4", a, b), F.Abs, bias=-MAG)
+            o = ap("P1", a, b)
+            group(([] if begin else [(o, ap("DP"), ap("HALF", a, b))])
+                  + [(o, ap("IN"), ap(PN, a, b)), (o, ap("BOP"), ap("HA", a, b)), (o, ap("BON"), ap("HA", L + a, L + b))])
+            ts(ap("EB", a, b), o, 8192.0, A.is_gt)
+            for c in (0, L):
+                tt(ap("TT", c + a, c + b), ap("P7", c + a, c + b), ap("EB", a, b), A.mult)
+                tt(ind("R", 0, RW, ap(OF, (c + a) // 16, (c + b) // 16)), ap("RVU", c + a, c + b), ap("TT", c + a, c + b), A.add)
         if not last:
-            act(ap("JUNK"), ap("P0", 0, L), F.Sign, accum=ap("SUM", 0, 1))
-            act(ap("SUM", 1, 2), ap("SUM", 0, 1), F.Identity, scale=16384.0, bias=96.0 * 32768)
-            act(ap("DP"), ap("IF"), F.Identity, scale=ap("SUM", 1, 2))
+            act(ap("JUNK"), ap("EB"), F.Identity, accum=ap("SUM", 0, 1))
+            act(ap("DP"), ap("IA"), F.Identity, scale=ap("SUM", 0, 1))
 
     def shares(r):
         me = T.cores[r]
@@ -402,13 +454,13 @@ def build(T, topo, rank):
         return res
 
     def hand_on(t):
-        snd, land = "SEND%d" % t, "LAND%d" % (t + 1)
+        snd, land = "SEND%d" % t, "W%d" % (t + 1)
         p0 = B0 + LN * t
         if t == 0:
-            act(ap("GONE"), ind("X", 0, XW, ap("FN16", 0, 6)), F.Identity)
-            act(ap(snd), ind("GONE", 0, LN, ap("SN16", 0, 6)), F.Identity)
+            copy(ap("GONE"), ind("X", 0, XW, ap("FN16", 0, 6)))
+            copy(ap(snd), ind("GONE", 0, LN, ap("SN16", 0, 6)))
         else:
-            act(ap(snd), ind("X", p0 - LN, p0, ap("SN16", 0, 6)), F.Identity)
+            copy(ap(snd), ind("X", p0 - LN, p0, ap("SN16", 0, 6)))
         mine = shares(rank)
 
         def send(g):
@@ -419,55 +471,51 @@ def build(T, topo, rank):
                                             remote_sem=T.sem["arr%d" % t], src=T[snd][:, 16 * d:16 * d + 16], dst=T[land][:, 16 * d:16 * d + 16]))
             g.remote_dma_fused(tr, local_sem=T.sem.sent)
             return None
-        add("G", send, [ap(snd)], [dict(r=[("wire", t, t + 1)])], 600, sem="", lat=2.5)
+        add("G", send, [ap(snd)], [dict(r=[("wire", t, t + 1)])], (0, 0, 0, 600, 0), sem="", lat=2.5)
         ops[-1]["sent"] = sum(len(v) for v in mine.values())
         act(ap(land, 0, 16), ap(snd, 0, 16), F.Identity)
-        ops.append(dict(e="X", fn=None, rd=[("wire", t, t + 1)], wr=[(land, 16, LN)], t=0.0, acc=False, lat=0.0, sem="arr%d" % t,
+        ops.append(dict(e="X", fn=None, rd=[("wire", t, t + 1)], wr=[(land, 16, LN)], t=0.0, c=(0, 0, 0, 0, 0), acc=False, lat=0.0, sem="arr%d" % t,
                         cnt=sum(len(shares((rank - d) % N)[d]) for d in range(1, N))))
 
     for t in range(RO):
-        p0 = B0 + LN * t
-        land = "LAND%d" % t
+        p0, W = B0 + LN * t, "W%d" % t
         if t > 0:
-            act(ap("W", LN, L), ap("X", p0 - LN, p0), F.Identity)
-        copy(ap("X", p0, p0 + LN), ap(land))
-        act(ap("W", 0, LN), ap(land), F.Identity)
+            act(ap(W, LN, L), ap("X", p0 - LN, p0), F.Identity)
+        act(ap("X", p0, p0 + LN), ap(W, 0, LN), F.Identity)
         if t == 0:
-            act(ap("W", LN, L), ind("X", 0, XW, ap("FN16", 0, 6)), F.Identity)
-            act(ap("NMF"), ind("IO", 0, IW, ap("FN16", 0, 6)), F.Identity)
-        act(ap("GG"), ap("NMF") if t == 0 else ap("IO", p0 - LN, p0), F.Identity, scale=-1.0, bias=float(C))
-        for a in range(0, NF, 32):
-            b = min(NF, a + 32)
-            if t > 0:
-                act(ap("WREP", 16 * a, 16 * b), ind("W", NP, L, ap("WIX", a, b)), F.Identity)
-            else:
-                copy(ap("WSP", 16 * a, 16 * b, 16), ap("W", NP + a, NP + b))
-                scan(ap("WREP", 16 * a, 16 * b), ap("MXR", 0, 16 * (b - a)), ap("WSP", 16 * a, 16 * b), A.add, A.max)
-        for c0, c1 in ((3, (NP + 31) // 32), (0, 3)):
-            for c in range(c0, c1):
-                src = ap(land, 32 * c, 32 * c + 32) if c < 3 else ap("W", 32 * c, 32 * c + 32)
-                mm(ap("P6", 128 * (c - c0), 128 * (c - c0) + 128, p=(0, 32)), src, ap("IB"), True, True)
-            if c1 > c0:
-                act(ap("WT", 128 * c0, 128 * c1, p=(0, 32)), ap("P6", 0, 128 * (c1 - c0), p=(0, 32)), F.Identity)
+            act(ap(W, LN, L), ind("X", 0, XW, ap("FN16", 0, 6)), F.Identity)
+            ts(ap("NF0"), ind("IO", 0, IW, ap("FN16", 0, 6)), -HN, A.add)
+        for h in (1, 0):
+            for q in range(3):
+                mm(ap("P6", 0, 128, p=(32 * q, 32 * q + 32)), ap(W, 96 * h + 32 * q, 96 * h + 32 * q + 32), ap("IB"), True, True)
+            act(ap("WT", 128 * h, 128 * h + 128, p=P96), ap("P6", 0, 128, p=P96), F.Identity)
         level(t, 0)
+        if t == 1:
+            ts(col(10), col(3), 128.0, A.mult, col(0), A.add)
+            ts(ap("DM"), ap("IO", 0, NV), col(10), A.is_equal)
+            copy(ap("KS"), ap("K2"))
+            tt(ap("KD"), ap("KS", 64, 128), ap("KS", 0, 64), A.subtract)
+        level(t, 1)
         if t == 0:
             copy(ap("LV1", 0, 6), ap("RTI", 6, 12))
             copy(ap("LV1", 6, 12), ap("RTI", 0, 6))
             nodes(1)
-        if t == 1:
-            group([(ap("P7"), ap("IF"), ap("KF", 512, NV)), (ap("P7"), ap("NIF"), ap("KF", 0, 512))])
-            act(ap("KD"), ap("P7"), F.Identity, scale=2.0)
-        level(t, 1)
-    ts(ap("YR"), ap("R", 0, NV), MAG, A.add, MAG, A.subtract)
-    dma("Y", "yr", T.yr[:], T.YR[:], [ap("YR")], [], 3.0)
-    act(ap("Y5"), ap("R", 0, 512), F.Identity, bias=MAG / 2)
-    act(ap("P2"), ap("Y5"), F.Identity, bias=-MAG / 2)
-    tt(ap("P2"), ap("P2"), ap("YR", 0, 512), A.subtract)
-    tt(ap("P2"), ap("P2"), ap("KD"), A.mult)
-    tt(ap("YK", 0, 512), ap("KF", 0, 512), ap("P2"), A.add)
-    tt(ap("YK", 512, NV), ap("KF", 512, NV), ap("P2"), A.subtract)
-    dma("Y", "y0", T.yk[0:16:2, :], T.YK[0:128:16, :], [ap("YK")], [], 2.0)
-    dma("S", "y1", T.yk[1:16:2, :], T.YK[1:128:16, :], [ap("YK")], [], 2.0)
+            acting(1, "P4")
+    ts(ap("YR", 0, YV), ap("R", 0, YV), MAG, A.add, MAG, A.subtract)
+    dma("Y", "yr0", T.yr[:, 0:YV], T.YR[:, 0:YV], [ap("YR", 0, YV)], [], 2.5)
+    act(ap("Y1"), ap("R", YV, NV), F.Identity, bias=MAG)
+    act(ap("YR", YV, NV), ap("Y1"), F.Identity, bias=-MAG)
+    dma("S", "yr1", T.yr[:, YV:NV], T.YR[:, YV:NV], [ap("YR", YV, NV)], [], 2.5)
+    o = ap("P2", 0, 64)
+    group([(o, ap("DM", 128 * a, 128 * a + 128), ap("R", 64 * a, 64 * a + 64)) for a in range(8)])
+    ts(ap("RS", 0, 64), o, MAG, A.add, MAG, A.subtract)
+    tt(ap("RS", 64, 128), o, ap("RS", 0, 64), A.subtract)
+    ts(o, ap("RS", 64, 128), MID, A.is_gt)
+    tt(o, o, ap("KD"), A.mult)
+    tt(ap("YK", 0, 64), o, ap("KS", 0, 64), A.add)
+    tt(ap("YK", 64, 128), ap("KS", 64, 128), o, A.subtract)
+    dma("Y", "y0", T.yk[:, 0:512], T.YK[:, 0:64], [ap("YK", 0, 64)], [], 2.0)
+    dma("S", "y1", T.yk[:, 512:NV], T.YK[:, 64:128], [ap("YK", 64, 128)], [], 2.0)
     return ops
 
 
@@ -488,7 +536,7 @@ def edges(ops):
                         continue
                     hit = (a < b2 and a2 < b) or (a, b) == (a2, b2)
                     if hit and (k2 == "w" or kind == "w"):
-                        d[j] = d.get(j, False) or (k2 == "w" and kind == "r") or (SYNC_ALL and not (o["acc"] and ops[j]["acc"]))
+                        d[j] = d.get(j, False) or not (o["acc"] and ops[j]["acc"])
                 if bank and h:
                     d.setdefault(h[-1][0], False)
         for kind, regs in (("r", o["rd"]), ("w", o["wr"])):
@@ -501,56 +549,58 @@ def edges(ops):
     return deps
 
 
-SYNC_ALL = True
-HOP, SELF, SLACK = 0.15, 0.08, 0.05
+HOP, SELF, PASSES = 0.3, 0.12, 6
+LOOKS = ((0.0, 0.0), (0.5, 0.3), (0.3, 0.1), (0.7, 0.7))
 
 
 def schedule(ops, deps):
     n = len(ops)
-    succ = [[] for _ in range(n)]
-    for i, d in enumerate(deps):
-        for j in d:
-            succ[j].append(i)
-
-    after, prev = {}, {}
+    pred, succ, prev = [{} for _ in range(n)], [{} for _ in range(n)], {}
     for i, o in enumerate(ops):
+        for j, hard in deps[i].items():
+            far = ops[j]["e"] != o["e"] or ops[j]["sem"] is not None
+            pred[i][j] = HOP + ops[j]["lat"] if far else SELF if hard else 0.0
         if "chain" in o:
             if o["chain"] in prev:
-                after[i] = prev[o["chain"]]
+                pred[i].setdefault(prev[o["chain"]], 0.0)
             prev[o["chain"]] = i
-    done = set()
+        for j, gap in pred[i].items():
+            succ[j][i] = gap
 
-    def gap(j, i):
-        if ops[j]["e"] != ops[i]["e"] or ops[j]["sem"] is not None:
-            return HOP + ops[j]["lat"]
-        return SELF if deps[i][j] else 0.0
-    pr = [0.0] * n
+    def greedy(before, after, head, urgency, slack):
+        left, est, ready, free, end, order = [len(p) for p in before], list(head), {}, {}, [0.0] * n, []
+        for i in range(n):
+            if left[i] == 0:
+                ready.setdefault(ops[i]["e"], []).append(i)
+        while len(order) < n:
+            t, e = min((max(free.get(e, 0.0), min(est[i] for i in r)), e) for e, r in ready.items() if r)
+            now = max((k for k in ready[e] if est[k] <= t + 1e-9), key=lambda k: urgency[k])
+            i = max((k for k in ready[e] if est[k] <= t + 1e-9 + min(slack[1], slack[0] * ops[now]["t"])), key=lambda k: urgency[k])
+            if urgency[i][0] - urgency[now][0] < est[i] - t:
+                i = now
+            end[i] = free[e] = max(est[i], free.get(e, 0.0)) + ops[i]["t"]
+            ready[e].remove(i)
+            order.append(i)
+            for s, gap in after[i].items():
+                est[s] = max(est[s], end[i] + gap)
+                left[s] -= 1
+                if left[s] == 0:
+                    ready.setdefault(ops[s]["e"], []).append(s)
+        return order, end
+
+    tail, way, best = [o["lat"] for o in ops], [0.0] * n, None
     for j in range(n - 1, -1, -1):
-        pr[j] = ops[j]["t"] + max([gap(j, i) + pr[i] for i in succ[j]] + [ops[j]["lat"]])
-    left = [len(d) for d in deps]
-    est = [0.0] * n
-    ready = [i for i in range(n) if left[i] == 0]
-    free, order, end = {}, [], [0.0] * n
-    while ready:
-        best = {}
-        may = [i for i in ready if i not in after or after[i] in done]
-        for i in may:
-            e = ops[i]["e"]
-            best[e] = min(best.get(e, 1e9), max(est[i], free.get(e, 0.0)))
-        e = min(best, key=lambda k: best[k])
-        cand = [i for i in may if ops[i]["e"] == e and est[i] <= best[e] + SLACK]
-        i = max(cand, key=lambda k: (pr[k], -k))
-        done.add(i)
-        st = max(est[i], free.get(e, 0.0))
-        end[i] = free[e] = st + ops[i]["t"]
-        ready.remove(i)
-        order.append(i)
-        for s in succ[i]:
-            est[s] = max(est[s], end[i] + gap(i, s))
-            left[s] -= 1
-            if left[s] == 0:
-                ready.append(s)
-    return order, end
+        way[j] = ops[j]["t"] + max([tail[j]] + [gap + way[i] for i, gap in succ[j].items()])
+    for slack in LOOKS:
+        urgency = [(way[i], -i) for i in range(n)]
+        for _ in range(PASSES):
+            order, end = greedy(pred, succ, [0.0] * n, urgency, slack)
+            span = max(end[i] + tail[i] for i in range(n))
+            if best is None or span < best[0]:
+                best = (span, order, end)
+            back = greedy(succ, pred, tail, [(end[i], i) for i in range(n)], slack)[1]
+            urgency = [(back[i], -i) for i in range(n)]
+    return best[1], best[2]
 
 
 def rank_program(g, core, T, topo):
@@ -606,5 +656,5 @@ def rank_program(g, core, T, topo):
             ins.then_inc(T.sem["s" + o["e"]], 1)
         sent += o.get("sent", 0)
     g.wait_ge(T.sem.sent, sent)
-    for nm in ("yx", "yr", "y0", "y1"):
+    for nm in STORES:
         g.wait_ge(T.sem["d" + nm], 16)

@@ -6,12 +6,12 @@ B0 = C - LN * RO
 XW, RW, IW = 3280, 1408, 3088
 MAG = 12582912.0
 M30 = 1.5 * 2.0 ** 30
-MID, EPS = 0.25, 1.0 / 256
+UP, EPS = 64.0, 1.0 / 32
 HN = 1536.0
 BIG = 2.0 ** 70
-PEF = 0.525
+PEF = 0.51
 VVS = (96, 128)
-VUS = (32, 0)
+VUS = (64, 0)
 SV, SU, VH = L - min(VVS), L - min(VUS), max(a + b for a, b in zip(VVS, VUS))
 CUT = 96
 IS = 1536
@@ -24,8 +24,9 @@ SB = dict(
     YR=(NV, f32), Y1=(NV - YV, f32), DM=(NV, f32), RS=(256, f32),
     IO=(IW, f32), RTI=(12, i32), FNI=(8, i32), SNI=(8, i32), FN16=(8, u16), SN16=(8, u16),
     W0=(L, bf), W1=(L, bf), W2=(L, bf), W3=(L, bf), SEND0=(LN, bf), SEND1=(LN, bf), SEND2=(LN, bf),
-    GONE=(LN, bf), WT=(256, bf), NF0=(LN, f16), NL=(384, f16), NB=(384, bf),
-    O16=(384, u16), RVU=(384, f32), NM=(288, f16), HI=(L, bf), TL=(L, f16), DG=(LN, f32), TT=(384, f32), EB=(L, bf),
+    WT=(256, bf), NF0=(LN, f16), NL=(384, f16), NB=(384, bf),
+    O16=(384, u16), RVU=(384, f32), NM=(384, f16), FR=(L, bf), NEW=(384, f32),
+    I2=(128, bf), N2=(128, bf), IM=(128, bf), IC=(128, bf), HI=(L, bf), TL=(L, f16), DG=(LN, f32), TT=(384, f32), EB=(L, bf),
     RDC=(L, bf),
     ZV=(16 * SV, bf), ZU=(16 * SU, bf), AB=(3072, bf), MXV=(16 * SV, bf), MNV=(16 * SV, bf), MXU=(16 * SU, bf), MNU=(16 * SU, bf),
     ZH=(16 * VH, f16), MXH=(8 * VH, f16), MNH=(8 * VH, f16), OFS=(512, bf), OFL=(L, bf), MAGT=(L, bf),
@@ -38,7 +39,7 @@ SB = dict(
     OF0=(24, u16), OF1=(24, u16), OF2=(24, u16), PN0=(L, bf), PN1=(L, bf), PN2=(L, bf), H1=(12, f32), H2=(12, f32),
     KG=(384, f16), KL=(48, f32), MID0=(24, f32), MID1=(24, f32), HH0=(24, f32), HH1=(24, f32), OO=(24, f32),
     KM=(24, f32), SBL=(12, f32),
-    PI=(4, i32), COL=(16, f32), IF=(128, f32), NIF=(128, f32), IA=(128, f32), IB=(128, bf), NI=(128, bf), IH=(128, bf),
+    PI=(4, i32), COL=(16, f32), IF=(128, f32), NIF=(128, f32), IA=(128, f32), IB=(128, bf), NI=(128, bf), IH=(128, f16), NO=(128, f16),
     IK=(256, bf), IN=(128, bf), IL=(128, bf), IQ=(128, bf), TP=(128, bf), TN=(128, bf),
     WD=(144, bf), WM=(144, bf), WH=(144, bf), G2=(16, bf),
     JB=(128, bf), BOP=(128, bf), BON=(128, bf), BOD=(128, bf), BOO=(128, bf), LM=(208, bf), CD=(L, bf), CDR=(L, bf),
@@ -53,6 +54,8 @@ for _k, _v in SB.items():
     else:
         PLACE[_k] = (_k, 0, _v[0], _v[1])
         SCRATCH[_k] = ("sbuf", [128, _v[0]], _v[1])
+for _k in ("E", "EA"):
+    SCRATCH[_k] = ("sbuf", [128, 12, L], bf)
 SCRATCH["SMALL"] = ("sbuf", [128, _at], f32)
 for _b in range(8):
     SCRATCH["P%d" % _b] = ("psum", [128, 512], "float32")
@@ -61,7 +64,7 @@ LOADS = ["ring", "x", "rt", "xl", "fn", "k0", "k1", "k2", "k3", "snd"]
 STORES = ["yx", "yr0", "yr1", "y0", "y1"]
 SEMAPHORES = ["sV", "sS", "sP", "sG", "sent", "arr0", "arr1", "arr2"] + ["d" + n for n in LOADS + STORES]
 CYC = 0.83e-3
-FAC, GAT, SCA = 1.05, 1.56, 3.8
+FAC, GAT, SCA = 1.02, 1.59, 3.9
 
 
 def build(T, topo, rank):
@@ -132,7 +135,9 @@ def build(T, topo, rank):
             fn = lambda g: g.scalar.activation(out["v"], a["v"], func, bias=val(bias), scale=val(scale))
         else:
             fn = lambda g: g.scalar.activation(out["v"], a["v"], func, bias=val(bias), scale=val(scale), accum_out=accum["v"])
-        cost = (0, a["n"], 0, 80, 0) if "ind" in a else (max(64, a["n"]) + (25 if accum else 0), 0, 0, 0, 0)
+        if "ind" in out:
+            fn = lambda g: g.scalar.activation(out["v"], a["v"], func)
+        cost = (0, 0, a["n"], 80, 0) if "ind" in out else (0, a["n"], 0, 80, 0) if "ind" in a else (max(64, a["n"]) + (25 if accum else 0), 0, 0, 0, 0)
         add("S", fn, [a, bias, scale], [out] + ([accum] if accum else []), cost)
 
     def mm(out, lhsT, rhs, start, stop):
@@ -188,9 +193,12 @@ def build(T, topo, rank):
     tt(col(4), col(0), col(1), A.subtract)
     ts(col(5), col(4), 15.0, A.add)
     ts(ap("IF"), ap("IO", 0, 128), col(0), A.is_equal)
-    for name, a, sc in (("IB", 0, 1.0), ("NI", 0, -1.0), ("IH", 0, 0.5), ("IK", 0, -64.0), ("IK", 128, 1.0), ("NIF", 0, -1.0),
+    for name, a, sc in (("IB", 0, 1.0), ("NI", 0, -1.0), ("IK", 0, -64.0), ("IK", 128, 1.0), ("NIF", 0, -1.0),
+                        ("I2", 0, 2.0), ("N2", 0, -2.0), ("IM", 0, EPS), ("IC", 0, -2 * (HN + UP)),
                         ("IN", 0, -16384.0), ("IL", 0, 1344.0), ("IQ", 0, -2.0 ** 20), ("IA", 0, 32768.0)):
         act(ap(name, a, a + 128), ap("IF"), F.Identity, scale=sc)
+    ts(ap("IH"), ap("IF"), 0.5 - 2.0 ** -11, A.mult)
+    ts(ap("NO"), ap("IF"), 2.0 ** -10 - 1, A.mult)
     act(ap("MAGT"), ap("IO", 0, L), F.Identity, scale=0.0, bias=MAG)
     act(ap("HALF"), ap("IO", 0, L), F.Identity, scale=0.0, bias=-0.5)
     ts(ap("WD"), ap("IO", 0, 144), col(5), A.is_equal)
@@ -223,8 +231,8 @@ def build(T, topo, rank):
     ts(ap("DN", 0, 24, 2), ap("IO", 0, L, 16), col(1), A.add, float(C + 1), A.add)
     ts(ap("DVU"), ap("IO", 0, 384, 16), col(1), A.add, float(NV), A.add)
     ts(ap("NL"), ap("NB"), B0 + 192 - HN, A.add)
-    ts(ap("R", 0, 512), dict(ap("RI", 0, 512), r=kin), MID - EPS, A.add)
-    ts(ap("R", 512, NV), dict(ap("RI", 512, NV), r=kin), MID + EPS, A.add)
+    ts(ap("R", 0, 512), dict(ap("RI", 0, 512), r=kin), UP - EPS, A.add)
+    ts(ap("R", 512, NV), dict(ap("RI", 512, NV), r=kin), UP + EPS, A.add)
     copy(ap("FN16", 0, 6), ap("FNI", 0, 6))
     copy(ap("SN16", 0, 6), ap("SNI", 0, 6))
 
@@ -234,10 +242,13 @@ def build(T, topo, rank):
             if m == parts[0] or m == 0:
                 e = parts[0] if m < parts[0] else 12
                 copy(ap(rep, 16 * m, 16 * e), ind("IO", 0, top, ap(key16[0], key16[1] + m, key16[1] + e)))
-            ts(ap(E, m * L + 16 * m, m * L + L), ap(rep, 16 * m, L), keys(m), A.is_equal)
-            items.append((ap(bank, 16 * m, 16 * m + 16), ap("BOD"), ap(E, m * L + 16 * m, m * L + 16 * m + 16)))
+            row = lambda a, b: dict(v=T[E][:, m, a:b], n=b - a, r=[(E, m * L + a, m * L + b)], dt=bf, ps=False)
+            ts(row(0, L - 16 * m), ap(rep, 16 * m, L), keys(m), A.is_equal)
             if m < 11:
-                items.append((ap(bank, 16 * m + 16, L), ap("BOO"), ap(E, m * L + 16 * m + 16, m * L + L)))
+                items.append((ap(bank, 16 * m + 16, L), ap("BOO"), row(16, L - 16 * m)))
+            if m % 6 == 5:
+                own = dict(v=T[E][:, m - 5:m + 1, 0:16], n=96, r=[(E, (m - 5) * L, (m + 1) * L)], dt=bf, ps=False)
+                items.append((ap(bank, 16 * m - 80, 16 * m + 16), ap("BOD"), own))
         group(items)
 
     def to_list(out, src, n):
@@ -292,11 +303,14 @@ def build(T, topo, rank):
         k = (t & 1) if l == 0 else 2
         U, OF, PN, W = "U%d" % k, "OF%d" % k, "PN%d" % k, "W%d" % t
         nameF = ap("NF0") if t == 0 else ap("NL", LN * t - LN, LN * t)
-        thr = 2.0 ** t / 128
+        stamp = (t + 2) * EPS
         begin, last = t == 0 and l == 0, t == RO - 1 and l == 1
         VV, VU = VVS[l], VUS[l]
         SV, SU = L - VV, L - VU
-        copy(ap("O16", 0, L), dict(ind("RI", 0, NV, ap(U, 0, 12)), r=kin) if begin else ind("R", 0, RW, ap(U, 0, 12)))
+        if begin:
+            copy(ap("O16", 0, L), dict(ind("RI", 0, NV, ap(U, 0, 12)), r=kin))
+        else:
+            ts(ap("O16", 0, L), ind("R", 0, RW, ap(U, 0, 12)), 0.25 - UP, A.add)
         X = lambda a, b: ind("X", 0, XW, ap("O16", a, b))
 
         def stepped(o0, h0, n):
@@ -317,15 +331,15 @@ def build(T, topo, rank):
                 scan(ap(mx, 16 * a, 16 * b), ap("MXR", 0, 16 * (b - a)), ap(z, 16 * a, 16 * b), A.add, A.max)
                 scan(ap(mn, 16 * a, 16 * b), ap("MNR", 0, 16 * (b - a)), ap(z, 16 * a, 16 * b), A.add, A.min)
 
-        def midrange(c0, own, a, b, rounded):
-            o = lambda a, b: ap("P4", c0 + a, c0 + b)
+        def midrange(c0, own, a, b, rounded, bank="P4"):
+            o = lambda a, b: ap(bank, c0 + a, c0 + b)
             mx, mn = ("MXV", "MNV") if own else ("MXU", "MNU")
             (h0, h1, hz), (s0, s1) = ((SV, L, 0), (0, SV)) if own else ((0, VU, VV), (VU, L))
-            items = [(o(a, b), ap("IH"), ap("HALF", a, b)), (o(a, b), ap("NI"), ap(W, a, b))]
+            items = [(o(a, b), ap("NI"), ap(W, a, b))]
             x, y = max(a, h0), min(b, h1)
             if x < y:
                 z0, z1 = 8 * (hz + x - h0), 8 * (hz + y - h0)
-                items += [(o(x, y), ap("NI"), ap("OFL", 0, y - x)), (o(x, y), ap("IH"), ap("MXH", z0 + 7, z1, 8)),
+                items += [(o(x, y), ap("NO"), ap("OFL", 0, y - x)), (o(x, y), ap("IH"), ap("MXH", z0 + 7, z1, 8)),
                           (o(x, y), ap("IH"), ap("MNH", z0, z1, 8))]
             x, y = max(a, s0), min(b, s1)
             if x < y:
@@ -337,9 +351,9 @@ def build(T, topo, rank):
         stepped(SV, 0, VV)
         plain("ZV", "MXV", "MNV", 0, SV)
         act(ap("RVU"), ind("R", 0, RW, ap(U, 0, 24)), F.Identity)
-        copy(ap("O16", L, 384), ap("RVU", L, 384))
+        ts(ap("O16", L, 384), ap("RVU", L, 384), 0.25 - UP, A.add)
         ts(ap("HI"), ap("O16", 0, L), 1.0 / 64, A.mult, 128.0, A.add)
-        ts(ap("NM"), ap("O16", 0, 288), -HN, A.add)
+        ts(ap("NM"), ap("O16"), -HN, A.add)
         for i, c in enumerate(sorted(range(6), key=lambda c: (c < 3, 32 * c < SV, c))):
             o, q = ap(YB[i]), (32 * (c % 3), 32 * (c % 3) + 32)
             items = [(o, ap("WT", 128 * (c // 3), 128 * (c // 3) + 128, p=q), ap("EX", p=q))]
@@ -364,33 +378,37 @@ def build(T, topo, rank):
             scan(ap("CS", 48 * h, 48 * h + 48), ap("RS8"), ap(bk, 256, 304), A.add, A.min)
             copy(ap("C16", 6 * h, 6 * h + 6), ap("CS", 48 * h + 7, 48 * h + 48, 8))
         nb = ap("NB", LN * t, LN * t + LN)
-        group([(ap("P5", 0, 96), ap("IB"), ap("NM", 0, 96)), (ap("P5", 0, 96), ap("NI"), nb),
-               (ap("P5", 96, L), ap("IB"), ap("NM", L, 288)), (ap("P5", 96, L), ap("NI"), nb)])
-        tt(ap("TL"), ap("P5", 0, L), ap("LM", t, t + L), A.mult)
-        d = ap("P5", L, 288)
+        group([(ap("P7", 0, 96), ap("IB"), ap("NM", 0, 96)), (ap("P7", 0, 96), ap("NI"), nb),
+               (ap("P7", 96, L), ap("IB"), ap("NM", L, 288)), (ap("P7", 96, L), ap("NI"), nb)])
+        tt(ap("TL"), ap("P7", 0, L), ap("LM", t, t + L), A.mult)
+        d, o = ap("P5", L, 288), ap("P5", 288, 480)
+        group([(o, ap("IF"), ap("RVU", 0, L)), (o, ap("NI"), ap("NM", 0, L)), (o, ap("IM"), ap("MAGT"))])
+        act(ap("FR"), o, F.Identity, bias=-HN - UP - MAG * EPS)
         if l == 0:
-            group([(ap("P5", 288, 480), ap("IF"), ap("RVU", 0, L)), (ap("P5", 288, 480), ap("NI"), ap("NM", 0, L))])
-            act(ap("SG", 0, L), ap("P5", 288, 480), F.Sign, bias=-HN - MID)
+            act(ap("SG", 0, L), o, F.Sign, bias=-HN - UP - MAG * EPS)
             group([(d, ap("IB"), ap("NM", 96, L)), (d, ap("NI"), nameF)])
             act(ap("A2"), d, F.Abs)
-            act(ap("TP"), ap("IF"), F.Identity, scale=thr)
-            act(ap("TN"), ap("IF"), F.Identity, scale=-thr)
+            act(ap("TP"), ap("IF"), F.Identity, scale=stamp)
+            act(ap("TN"), ap("IF"), F.Identity, scale=-stamp)
         else:
-            group([(d, ap("IF"), ap("RVU", 96, L)), (d, ap("NI"), nameF)])
-            act(ap("A1"), d, F.Abs, bias=-HN - MID)
-            act(ap("A2"), ap("A1"), F.Relu, bias=-thr)
+            group([(d, ap("IB"), ap("NM", 96, L)), (d, ap("NI"), nameF), (d, ap("IB"), ap("FR", 96, L))])
+            act(ap("A1"), d, F.Abs)
+            act(ap("A2"), ap("A1"), F.Relu, bias=EPS / 2 - stamp)
         group([(d, ap("IQ"), ap("A2")), (d, ap("NI"), nameF)])
         act(ap("DG"), d, F.Relu, bias=C - HN)
         bv, bu = ap("P7", 0, L), ap("P7", L, 384)
-        group([(bu, ap("IF"), ap("RVU", 0, L)), (bu, ap("NIF"), ap("RVU", L, 384))] + ([(bu, ap("TP"), ap("SG", 0, L))] if l == 0 else []))
-        group([(ap("P5", 0, L), ap("IF"), ap("RVU", 0, L)), (ap("P5", 0, 96), ap("NI"), ap("TL", 0, 96)),
-               (ap("P5", 0, 96), ap("IL"), ap("LM", t, t + 96)), (ap("P5", 96, L), ap("IF"), ap("DG"))])
-        act(ap("RVU", 0, L), ap("P5", 0, L), F.Identity)
-        group([(bv, ap("IF"), ap("RVU", L, 384)), (bv, ap("NIF"), ap("RVU", 0, L)), (ap("P7", 0, 96), ap("NI"), ap("TL", 96, L)),
-               (ap("P7", 0, 96), ap("IL"), ap("LM", t, t + 96))] + ([(bv, ap("TN"), ap("SG", 0, L))] if l == 0 else []))
+        cv, cu = ap("P5", 0, L), ap("P5", L, 384)
+        group([(bu, ap("IB"), ap("NM", 0, L)), (bu, ap("NI"), ap("NM", L, 384)), (bu, ap("I2" if l else "IB"), ap("FR"))]
+              + ([(bu, ap("TP"), ap("SG", 0, L))] if l == 0 else []))
+        group([(bv, ap("NI"), ap("NM", 0, L)), (bv, ap("IB"), ap("NM", L, 384)), (bv, ap("N2" if l else "NI"), ap("FR")),
+               (ap("P7", 0, 96), ap("NI"), ap("TL", 96, L)), (ap("P7", 0, 96), ap("IB"), ap("TL", 0, 96)), (ap("P7", 96, L), ap("NIF"), ap("DG"))]
+              + ([(bv, ap("TN"), ap("SG", 0, L))] if l == 0 else []))
+        group([(ap("P5", 0, 384), ap("IB"), ap("NM")), (cv, ap("IC"), ap("HALF")), (cu, ap("IC"), ap("HALF")), (cv, ap("IB"), ap("FR")),
+               (cu, ap("NI"), ap("FR")), (ap("P5", 0, 96), ap("NI"), ap("TL", 0, 96)), (ap("P5", 0, 96), ap("IL"), ap("LM", t, t + 96)),
+               (ap("P5", 96, L), ap("IF"), ap("DG"))])
         if l == 0:
-            midrange(L, True, 0, L, False)
-            act(ap("SG", L, 384), ap("P4", L, 384), F.Sign, scale=-1.0, bias=0.5)
+            midrange(L, True, 0, L, False, "P6")
+            act(ap("SG", L, 384), ap("P6", L, 384), F.Sign, scale=-1.0, bias=0.625)
         midrange(0, True, 0, L, True)
         act(ap("HA", 0, L), ap("P4", 0, L), F.Abs, bias=-MAG)
         if l == 0:
@@ -415,7 +433,7 @@ def build(T, topo, rank):
         scan(ap("XO"), ap("SD", 7, L, 8), ap("DN"), A.min, A.max)
         copy(ap("XO16"), ap("XO", 1, 24, 2))
         o = ap("P6", 0, L)
-        group([(o, ap("IH"), ap(x)) for x in ("HALF", W, "XC")] + [(o, ap("IB"), ap("MAGT"))])
+        group([(o, ap("IH"), ap(x)) for x in (W, "XC")] + [(o, ap("IB"), ap("MAGT"))])
         act(ap("VAL"), o, F.Identity, bias=-MAG)
         copy(ind("X", 0, XW, ap("XO16")), ap("VAL"))
         if last:
@@ -433,7 +451,8 @@ def build(T, topo, rank):
             ts(ap("EB", a, b), o, 8192.0, A.is_gt)
             for c in (0, L):
                 tt(ap("TT", c + a, c + b), ap("P7", c + a, c + b), ap("EB", a, b), A.mult)
-                tt(ind("R", 0, RW, ap(OF, (c + a) // 16, (c + b) // 16)), ap("RVU", c + a, c + b), ap("TT", c + a, c + b), A.add)
+                tt(ap("NEW", c + a, c + b), ap("P5", c + a, c + b), ap("TT", c + a, c + b), A.add)
+                act(ind("R", 0, RW, ap(OF, (c + a) // 16, (c + b) // 16)), ap("NEW", c + a, c + b), F.Silu)
         if not last:
             act(ap("JUNK"), ap("EB"), F.Identity, accum=ap("SUM", 0, 1))
             act(ap("DP"), ap("IA"), F.Identity, scale=ap("SUM", 0, 1))
@@ -457,10 +476,10 @@ def build(T, topo, rank):
         snd, land = "SEND%d" % t, "W%d" % (t + 1)
         p0 = B0 + LN * t
         if t == 0:
-            copy(ap("GONE"), ind("X", 0, XW, ap("FN16", 0, 6)))
-            copy(ap(snd), ind("GONE", 0, LN, ap("SN16", 0, 6)))
+            act(ap("SEND1"), ind("X", 0, XW, ap("FN16", 0, 6)), F.Identity)
+            act(ap(snd), ind("SEND1", 0, LN, ap("SN16", 0, 6)), F.Identity)
         else:
-            copy(ap(snd), ind("X", p0 - LN, p0, ap("SN16", 0, 6)))
+            act(ap(snd), ind("X", p0 - LN, p0, ap("SN16", 0, 6)), F.Identity)
         mine = shares(rank)
 
         def send(g):
@@ -501,16 +520,16 @@ def build(T, topo, rank):
             copy(ap("LV1", 6, 12), ap("RTI", 0, 6))
             nodes(1)
             acting(1, "P4")
-    ts(ap("YR", 0, YV), ap("R", 0, YV), MAG, A.add, MAG, A.subtract)
+    ts(ap("YR", 0, YV), ap("R", 0, YV), MAG, A.add, MAG + UP, A.subtract)
     dma("Y", "yr0", T.yr[:, 0:YV], T.YR[:, 0:YV], [ap("YR", 0, YV)], [], 2.5)
     act(ap("Y1"), ap("R", YV, NV), F.Identity, bias=MAG)
-    act(ap("YR", YV, NV), ap("Y1"), F.Identity, bias=-MAG)
+    act(ap("YR", YV, NV), ap("Y1"), F.Identity, bias=-MAG - UP)
     dma("S", "yr1", T.yr[:, YV:NV], T.YR[:, YV:NV], [ap("YR", YV, NV)], [], 2.5)
     o = ap("P2", 0, 64)
     group([(o, ap("DM", 128 * a, 128 * a + 128), ap("R", 64 * a, 64 * a + 64)) for a in range(8)])
     ts(ap("RS", 0, 64), o, MAG, A.add, MAG, A.subtract)
     tt(ap("RS", 64, 128), o, ap("RS", 0, 64), A.subtract)
-    ts(o, ap("RS", 64, 128), MID, A.is_gt)
+    ts(o, ap("RS", 64, 128), 0.0, A.is_gt)
     tt(o, o, ap("KD"), A.mult)
     tt(ap("YK", 0, 64), o, ap("KS", 0, 64), A.add)
     tt(ap("YK", 64, 128), ap("KS", 64, 128), o, A.subtract)
@@ -549,7 +568,7 @@ def edges(ops):
     return deps
 
 
-HOP, SELF, PASSES = 0.3, 0.12, 6
+HOP, SELF, PASSES = 0.23, 0.23, 6
 LOOKS = ((0.0, 0.0), (0.5, 0.3), (0.3, 0.1), (0.7, 0.7))
 
 

@@ -6,82 +6,105 @@ B0 = C - LN * RO
 XW, RW, IW = 3280, 1408, 3088
 MAG = 12582912.0
 M30 = 1.5 * 2.0 ** 30
-UP, EPS = 64.0, 1.0 / 32
+UP, EPS = 64.0, 1.0 / 16
 HN = 1536.0
 BIG = 2.0 ** 70
+TOP = 1792.0
 PEF = 0.51
-VVS = (96, 128)
-VUS = (64, 0)
-SV, SU, VH = L - min(VVS), L - min(VUS), max(a + b for a, b in zip(VVS, VUS))
-CUT = 96
-IS = 1536
-YB = ("P2", "P3", "P4", "P0", "P3", "P4")
+SVS = (96, 96)
+VUS = (0, 0)
+VSC = (0, 0, 0, 1)
+DVS, DUS = (3, 3), (0, 0)
+GIS, GLAT = 1200, 2.2
+SV = max(SVS)
+OW = 512 if max(VUS) else 256
+IS = 1024
+VBX = (L - min(SVS)) // 16
+YB = ("P3", "P4", "P3")
 YV = 640
 
 bf, f32, i32, u16, f16 = "bfloat16", "float32", "int32", "uint16", "float16"
 SB = dict(
     X=(XW, bf), R=(RW, f32), RI=(NV, i32), K2=(128, i32), KS=(128, f32), KD=(64, f32), YK=(128, f32),
-    YR=(NV, f32), Y1=(NV - YV, f32), DM=(NV, f32), RS=(256, f32),
+    YR=(NV, f32), Y1=(NV - YV, f32), DM=(NV, f32), RS=(64, f32),
     IO=(IW, f32), RTI=(12, i32), FNI=(8, i32), SNI=(8, i32), FN16=(8, u16), SN16=(8, u16),
     W0=(L, bf), W1=(L, bf), W2=(L, bf), W3=(L, bf), SEND0=(LN, bf), SEND1=(LN, bf), SEND2=(LN, bf),
-    WT=(256, bf), NF0=(LN, f16), NL=(384, f16), NB=(384, bf),
-    O16=(384, u16), RVU=(384, f32), NM=(384, f16), FR=(L, bf), NEW=(384, f32),
-    I2=(128, bf), N2=(128, bf), IM=(128, bf), IC=(128, bf), HI=(L, bf), TL=(L, f16), DG=(LN, f32), TT=(384, f32), EB=(L, bf),
-    RDC=(L, bf),
-    ZV=(16 * SV, bf), ZU=(16 * SU, bf), AB=(3072, bf), MXV=(16 * SV, bf), MNV=(16 * SV, bf), MXU=(16 * SU, bf), MNU=(16 * SU, bf),
-    ZH=(16 * VH, f16), MXH=(8 * VH, f16), MNH=(8 * VH, f16), OFS=(512, bf), OFL=(L, bf), MAGT=(L, bf),
-    DN=(24, f32), XO=(24, f32), JUNK=(L, bf),
-    ST=(512, f32), RR=(32, f32), DIG=(32, bf), CS=(96, f32), C16=(12, u16), REP=(L, u16), REPA=(L, u16),
-    E=(12 * L, bf), EA=(12 * L, bf), SD=(L, f32), T1=(12, f32), T2=(12, f32), XO16=(12, u16),
-    T3=(24, f32), T4=(24, f32), XC=(L, bf), VAL=(L, bf),
-    HA=(384, bf), SG=(384, bf), A1=(LN, f32), A2=(LN, bf), SUM=(4, f32), DP=(128, bf),
-    LV0=(36, f32), LV1=(36, f32), LV2=(36, f32), U0=(36, u16), U1=(36, u16), U2=(36, u16),
+    WT=(128, bf), WS=(17 * VBX, f16), NF0=(LN, f16), NL=(384, f16), NB=(384, bf),
+    O16=(384, u16), RV=(L, f32), NM=((24, 17), f16), FR=(L, bf), NEW=(384, f32),
+    HI=((12, 17), bf), TL=(L, f16), DG=(LN, f32), TT=(384, f32), EB=(L, bf),
+    ZV=(16 * SV, f16), MXV=(16 * SV, bf), MNV=(16 * SV, bf),
+    ZH=(272 * VBX, f16), MW=(272 * 12, f16), ZU=(2048, f16), ZS=(3072, f16), MXS=(3072, bf), MNS=(3072, bf),
+    MXH=(1536, f16), MNH=(1536, f16), MXU=(1536, f16), MNU=(1536, f16), DG16=(LN, f16), OFH=(512, f16),
+    OFS=(OW, bf), OFL=(L, bf), O17=(17 * VBX, bf), ONE=(384, bf),
+    ST=(512, f32), RR=(32, f32), DIG=(32, bf), CS=(96, f32), C16=(12, u16), REP=(L, f16), REPA=(288, f16),
+    E=((144, 17), bf), EA=((12, L), bf), SD=(204, f32), RDA=(204, f32), EF=(12, bf), T1=(12, f32), T2=(12, f32), XO16=(12, u16),
+    T3=((2, 12), f32), T4=(24, f32), XC=(L, bf), VAL=(L, bf),
+    HA=(384, bf), SG=(384, bf), A1=(LN, bf), SUM=(4, f32), THR=(4, f32),
+    LV0=((3, 12), f32), LV1=((3, 12), f32), LV2=((3, 12), f32), U0=(36, u16), U1=(36, u16), U2=(36, u16),
     OF0=(24, u16), OF1=(24, u16), OF2=(24, u16), PN0=(L, bf), PN1=(L, bf), PN2=(L, bf), H1=(12, f32), H2=(12, f32),
-    KG=(384, f16), KL=(48, f32), MID0=(24, f32), MID1=(24, f32), HH0=(24, f32), HH1=(24, f32), OO=(24, f32),
-    KM=(24, f32), SBL=(12, f32),
-    PI=(4, i32), COL=(16, f32), IF=(128, f32), NIF=(128, f32), IA=(128, f32), IB=(128, bf), NI=(128, bf), IH=(128, f16), NO=(128, f16),
-    IK=(256, bf), IN=(128, bf), IL=(128, bf), IQ=(128, bf), TP=(128, bf), TN=(128, bf),
-    WD=(144, bf), WM=(144, bf), WH=(144, bf), G2=(16, bf),
-    JB=(128, bf), BOP=(128, bf), BON=(128, bf), BOD=(128, bf), BOO=(128, bf), LM=(208, bf), CD=(L, bf), CDR=(L, bf),
+    KG=(384, f16), KL=(48, f32), MH0=(48, f32), MH1=(48, f32), OO=(48, f32),
+    KM=(24, f32), EA0=((12, L), bf), TL32=(L, f32), LMB=(208, bf),
+    PI=(4, i32), COL=(16, f32), IF=(128, f32), NIF=(128, f32), IB=(128, bf), NI=(128, bf), IH=(128, f16), NO=(128, f16),
+    N64=(128, bf), IN=(128, bf), IL=(128, bf), IQ=(128, bf), HP=(128, bf), HM=(128, bf), EP=(128, bf), EM=(128, bf), E3=(128, bf), E3P=(128, bf),
+    IMAG=(128, bf), IME=(128, bf), IK0=(128, bf),
+    WD=(144, bf), WM=(144, bf), WH=(144, bf), G4=(16, bf), GN=(16, bf),
+    JB=(128, bf), BOP=(128, bf), BON=(128, bf), BOD=(128, bf), BOO=(128, bf), BN2=(128, bf), LM=(208, bf), CD=(204, bf), CDR=(L, bf),
     EX=(512, bf), LM1=(768, bf), LM64=(768, bf), PEN8=(48, bf), RS8=(48, bf), RT=(256, bf), MXR=(512, bf),
-    MNR=(512, bf), HALF=(L, bf), DVU=(24, f32), PW=(16, f32),
+    MNR=(512, bf), DVU=(24, f32), PW=(16, f32),
 )
-SCRATCH, PLACE, _at = {}, {}, 0
-for _k, _v in SB.items():
-    if _v[1] == f32 and _v[0] <= 48:
-        PLACE[_k] = ("SMALL", _at, _v[0], f32)
-        _at += (_v[0] + 7) // 8 * 8
+SCRATCH, PLACE, _at = {}, {}, {f32: 0, bf: 0}
+for _k, (_w, _d) in SB.items():
+    if isinstance(_w, tuple):
+        PLACE[_k] = (_k, 0, _w[0] * _w[1], _d, _w[1])
+        SCRATCH[_k] = ("sbuf", [128, _w[0], _w[1]], _d)
+    elif (_d == f32 and _w <= 96) or (_d == bf and _w == 128):
+        PLACE[_k] = ("SMALL" + _d, _at[_d], _w, _d, 0)
+        _at[_d] += (_w + 7) // 8 * 8
     else:
-        PLACE[_k] = (_k, 0, _v[0], _v[1])
-        SCRATCH[_k] = ("sbuf", [128, _v[0]], _v[1])
-for _k in ("E", "EA"):
-    SCRATCH[_k] = ("sbuf", [128, 12, L], bf)
-SCRATCH["SMALL"] = ("sbuf", [128, _at], f32)
+        PLACE[_k] = (_k, 0, _w, _d, 0)
+        SCRATCH[_k] = ("sbuf", [128, _w], _d)
+for _d in _at:
+    SCRATCH["SMALL" + _d] = ("sbuf", [128, _at[_d]], _d)
 for _b in range(8):
     SCRATCH["P%d" % _b] = ("psum", [128, 512], "float32")
-    PLACE["P%d" % _b] = ("P%d" % _b, 0, 512, f32)
+    PLACE["P%d" % _b] = ("P%d" % _b, 0, 512, f32, 0)
 LOADS = ["ring", "x", "rt", "xl", "fn", "k0", "k1", "k2", "k3", "snd"]
 STORES = ["yx", "yr0", "yr1", "y0", "y1"]
 SEMAPHORES = ["sV", "sS", "sP", "sG", "sent", "arr0", "arr1", "arr2"] + ["d" + n for n in LOADS + STORES]
+SEMAPHORES += ["aZV%d" % i for i in range(max(DVS))] + ["aZS%d" % i for i in range(max(DUS))]
 CYC = 0.83e-3
 FAC, GAT, SCA = 1.02, 1.59, 3.9
 
 
 def build(T, topo, rank):
-    ops = []
+    ops, used = [], {}
+
+    def cut(a, b, s):
+        return slice(a, b) if s == 1 else slice(a, b, s) if s > 0 else slice(b - 1, a - 1 if a else None, s)
 
     def ap(name, a=0, b=None, s=1, p=None):
-        buf, at, width, dt = PLACE[name]
+        buf, at, width, dt, pitch = PLACE[name]
         if b is None:
             b = width
-        rows = slice(0, 128) if p is None else slice(p[0], p[1])
-        if s == 1:
-            v = T[buf][rows, at + a:at + b]
-        elif s > 0:
-            v = T[buf][rows, at + a:at + b:s]
-        else:
-            v = T[buf][rows, at + b - 1:(at + a - 1 if at + a else None):s]
-        return dict(v=v, n=len(range(a, b, abs(s))), r=[(name, a, b)], dt=dt, ps=is_bank(name))
+        if pitch:
+            if a // pitch == (b - 1) // pitch:
+                return rows(name, a // pitch, a // pitch + 1, a % pitch, b - a // pitch * pitch, s, p)
+            return rows(name, a // pitch, b // pitch, 0, pitch, s, p)
+        part = slice(0, 128) if p is None else slice(p[0], p[1])
+        return dict(v=T[buf][part, cut(at + a, at + b, s)], n=len(range(a, b, abs(s))), r=[(name, a, b)], dt=dt, ps=is_bank(name))
+
+    def rows(name, r0, r1, a, b, s=1, p=None):
+        buf, at, width, dt, pitch = PLACE[name]
+        part = slice(0, 128) if p is None else slice(p[0], p[1])
+        v = T[buf][part, r0 if r1 - r0 == 1 else cut(r0, r1, 1 if s > 0 else -1), cut(a, b, s)]
+        return dict(v=v, n=(r1 - r0) * len(range(a, b, abs(s))), r=[(name, pitch * r + a, pitch * r + b) for r in range(r0, r1)], dt=dt, ps=is_bank(name))
+
+    def lanes(name, a, b, r0=0):
+        return rows(name, r0 + a // 16, r0 + b // 16, 0, 16)
+
+    def slot(name, r0, r1, k):
+        x = ap(name, 272 * r0 + k, 272 * r1, 16)
+        return dict(x, r=[("MW%d" % k, r0, r1)]) if name == "MW" else x
 
     def ind(name, a, b, off):
         return dict(v=T[name][:, a:b].indirect(off["v"]), n=16 * off["n"], r=[(name, a, b)], o=off["r"], dt=SCRATCH[name][2], ps=False, ind=1)
@@ -156,6 +179,9 @@ def build(T, topo, rank):
         add("G", fn, [], [out], (157 + 2 * out["n"], 0, 0, 0, 0))
         ops[-1]["chain"] = "G"
 
+    def pick(out, a, pat, base):
+        add("G", lambda g: g.affine_select(out["v"], a["v"], pat, A.is_equal, 0.0, base, 0), [a], [out], (205 + 2 * out["n"], 0, 0, 0, 0))
+
     def dma(q, name, out, in_, rd, wr, us):
         eng = (lambda g: g.sync) if q == "Y" else (lambda g: g.scalar)
         add(q, lambda g: eng(g).dma_start(out, in_), rd, wr, (0, 0, 0, 80, 0), sem="d" + name, lat=us)
@@ -163,7 +189,7 @@ def build(T, topo, rank):
             ops[-1]["chain"] = q
 
     col = lambda j: ap("COL", j, j + 1)
-    P96 = (0, 96)
+    PK = (0, 102)
     kin = [("RI", 0, NV), ("RI1", 0, NV)]
     dma("Y", "ring", T.RI[:], T.ring[:], [], [ap("RI")], 3.0)
     dma("S", "rt", T.RTI[:], T.rt[:], [], [ap("RTI")], 2.0)
@@ -175,106 +201,132 @@ def build(T, topo, rank):
     dma("Y", "k3", T.K2[:, 64:128], T.kid[:, 512:NV], [], [ap("K2", 64, 128)], 2.5)
     iota(ap("PI", 0, 1), [[1, 1]], 0, 1)
     iota(ap("IO", 0, 256), [[1, 256]])
-    iota(ap("LM"), [[0, 13], [1, 16]])
     iota(ap("JB"), [[16, 8], [0, 16]])
-    iota(ap("OFS"), [[0, 2], [256, 16], [0, 16]], -2048)
-    iota(ap("EX", p=P96), [[1, 32], [0, 16]])
-    iota(ap("G2"), [[0, 2], [16, 8]])
-    iota(ap("OFL"), [[0, 12], [256, 16]], -2048)
+    iota(ap("LM"), [[0, 13], [1, 16]])
+    iota(ap("O17"), [[0, VBX], [-256, 17]], int(TOP))
+    iota(ap("OFS"), [[0, OW // 256], [-256, 16], [0, 16]], int(TOP))
+    iota(ap("EX", p=(0, SV)), [[1, 32], [0, 16]])
+    iota(ap("G4"), [[0, 2], [16, 8]])
+    iota(ap("OFL"), [[0, 12], [-256, 16]], int(TOP))
     iota(ap("NB"), [[1, 384]], -192)
+    iota(ap("LM64", p=PK), [[-17, 6], [0, 8], [-1, 16]], 0, 1)
     iota(ap("PEN8"), [[0, 6], [16, 8]])
-    iota(ap("LM64", p=P96), [[-16, 6], [0, 8], [-1, 16]], 0, 1)
-    for a, n in ((256, 256), (512, 512), (1024, IS - 1024)):
-        act(ap("IO", a, a + n), ap("IO", 0, n), F.Identity, bias=float(a))
+    iota(ap("CD"), [[0, 12], [1, 17]])
     iota(ap("IO", IS, IW), [[1, IW - IS]], IS)
-    for j, m in ((1, 15), (2, 31), (3, 7)):
+    mset(ap("O17", 16, 17 * VBX, 17), 2048.0)
+    for a in (0, 256):
+        copy(ap("OFH", a, a + 256), ap("OFS", 0, 256))
+    mset(ap("ONE"), 1.0)
+    act(ap("NEW"), ap("ONE"), F.Identity)
+    act(ap("R", NV, RW), ap("NEW"), F.Silu)
+    ops[-1]["t"] += 1.3
+    ops[-1]["tab"] = 1
+    for a, n in ((256, 256), (512, IS - 512)):
+        act(ap("IO", a, a + n), ap("IO", 0, n), F.Identity, bias=float(a))
+    for j, m in ((1, 15), (2, 31)):
         ts(ap("PI", j, j + 1), ap("PI", 0, 1), m, A.bitwise_and)
-    copy(ap("COL", 0, 4), ap("PI"))
+    copy(ap("COL", 0, 3), ap("PI", 0, 3))
     tt(col(4), col(0), col(1), A.subtract)
     ts(col(5), col(4), 15.0, A.add)
-    ts(ap("IF"), ap("IO", 0, 128), col(0), A.is_equal)
-    for name, a, sc in (("IB", 0, 1.0), ("NI", 0, -1.0), ("IK", 0, -64.0), ("IK", 128, 1.0), ("NIF", 0, -1.0),
-                        ("I2", 0, 2.0), ("N2", 0, -2.0), ("IM", 0, EPS), ("IC", 0, -2 * (HN + UP)),
-                        ("IN", 0, -16384.0), ("IL", 0, 1344.0), ("IQ", 0, -2.0 ** 20), ("IA", 0, 32768.0)):
-        act(ap(name, a, a + 128), ap("IF"), F.Identity, scale=sc)
-    ts(ap("IH"), ap("IF"), 0.5 - 2.0 ** -11, A.mult)
-    ts(ap("NO"), ap("IF"), 2.0 ** -10 - 1, A.mult)
-    act(ap("MAGT"), ap("IO", 0, L), F.Identity, scale=0.0, bias=MAG)
-    act(ap("HALF"), ap("IO", 0, L), F.Identity, scale=0.0, bias=-0.5)
+    ts(ap("IB"), ap("IO", 0, 128), col(0), A.is_equal)
+    for name, sc in (("NI", -1.0), ("N64", -64.0), ("HP", 0.5), ("HM", -0.5), ("EP", EPS / 2), ("EM", -EPS / 2), ("E3", -1.5 * EPS), ("E3P", 1.5 * EPS),
+                     ("IN", -16384.0), ("IL", 1344.0), ("IQ", -2.0 ** 19), ("IMAG", MAG), ("IME", MAG * EPS), ("IK0", HN + UP),
+                     ("IH", 0.5 - 2.0 ** -11), ("NO", 2.0 ** -10 - 1)):
+        ts(ap(name), ap("IB"), sc, A.mult)
+    act(ap("IF"), ap("IB"), F.Identity)
+    act(ap("NIF"), ap("IB"), F.Identity, scale=-1.0)
     ts(ap("WD"), ap("IO", 0, 144), col(5), A.is_equal)
-    ts(ap("G2"), ap("G2"), col(4), A.is_equal, 2048.0, A.mult)
+    ts(ap("GN"), ap("G4"), col(4), A.is_equal, -2048.0, A.mult)
+    ts(ap("G4"), ap("G4"), col(4), A.is_equal, 4096.0, A.mult)
     ts(ap("JB"), ap("JB"), col(4), A.is_equal)
     ts(ap("LM"), ap("LM"), col(1), A.is_equal)
     mset(ap("MXR"), 0.0)
     mset(ap("MXR", s=16), -1024.0)
-    act(ap("CD"), ap("MXR", 0, L), F.Identity, scale=-2.0 ** 19)
-    act(ap("RDC"), ap("MXR", 0, L), F.Identity, scale=0.0, bias=0.5)
-    scan(ap("EB"), ap("RDC"), ap("CD"), A.mult, A.max)
-    tt(ap("PW"), ap("EB", 0, 16), ap("LM", 0, 16), A.mult)
-    add("V", lambda g: g.vector.tensor_reduce(col(6)["v"], ap("PW")["v"], AxisListType.X, A.add), [ap("PW")], [col(6)], (64, 0, 0, 0, 0))
-    act(ap("CDR"), ap("EB"), F.Identity, scale=-1.0)
-    act(ap("EB"), ap("LM", 0, L), F.Identity, scale=BIG, bias=-BIG)
-    group([(ap("P3", 0, L), ap("IB"), ap("CDR")), (ap("P3", 0, L), ap("IB"), ap("EB"))])
-    act(ap("CD"), ap("P3", 0, L), F.Identity)
-    ts(col(6), col(6), 0.5, A.mult)
-    for name, sc in (("BOO", 2.0 ** 40), ("BOD", col(6)), ("BOP", 16384.0), ("BON", -16384.0)):
+    ts(ap("EB"), ap("MXR", 0, L), 2.0 ** 19, A.mult)
+    mset(ap("XC"), 0.5)
+    scan(ap("CDR"), ap("XC"), ap("EB"), A.mult, A.min)
+    tt(ap("PW"), ap("CDR", 0, 16), ap("LM", 0, 16), A.mult)
+    add("V", lambda g: g.vector.tensor_reduce(col(10)["v"], ap("PW")["v"], AxisListType.X, A.add), [ap("PW")], [col(10)], (64, 0, 0, 0, 0))
+    ts(col(6), col(10), -0.5, A.mult)
+    ts(ap("CD"), ap("CD"), col(1), A.not_equal, -BIG, A.mult)
+    ts(ap("CD"), ap("CD"), col(10), A.min)
+    mset(ap("CD", 16, 204, 17), HN)
+    for name, sc in (("BOO", 2.0 ** 40), ("BOD", col(6)), ("BOP", 16384.0), ("BON", -16384.0), ("BN2", -2048.0)):
         act(ap(name), ap("JB"), F.Identity, scale=sc)
-    ts(ap("EX", p=P96), ap("EX", p=P96), ap("COL", 2, 3, p=P96), A.is_equal, -1.0, A.mult)
-    ts(ap("LM1", p=P96), ap("LM64", p=P96), 0.0, A.is_equal)
-    ts(ap("LM64", p=P96), ap("LM64", p=P96), 0.0, A.is_equal, 64.0, A.mult)
+    ts(ap("EX", p=(0, SV)), ap("EX", p=(0, SV)), ap("COL", 2, 3, p=(0, SV)), A.is_equal, -1.0, A.mult)
+    ts(ap("LM1", p=PK), ap("LM64", p=PK), 0.0, A.is_equal)
+    ts(ap("LM64", p=PK), ap("LM64", p=PK), 0.0, A.is_equal, 64.0, A.mult)
     ts(ap("PEN8"), ap("PEN8"), col(4), A.not_equal, 2.0 ** 20, A.mult)
-    for name, n, st, sc, b in (("RS8", 48, 2, -1024.0, 0.0), ("RT", 256, 1, -2.0 ** 20, -128.0), ("MNR", 512, 1, -1.0, 0.0),
-                               ("RDC", L, 1, BIG / 128, 0.0)):
+    ts(ap("PEN8"), ap("PEN8"), -HN, A.add)
+    for name, n, st, sc, b in (("RS8", 48, 2, -4096.0, 0.0), ("RT", 256, 1, -2.0 ** 20, -128.0), ("MNR", 512, 1, -1.0, 0.0)):
         act(ap(name), ap("MXR", 0, n * st, st), F.Identity, scale=sc, bias=b)
     mset(ap("X", C, XW), 0.0)
-    act(ap("R", NV, RW), ap("IO", 0, RW - NV), F.Identity)
-    ts(ap("DN", 0, 24, 2), ap("IO", 0, L, 16), col(1), A.add, float(C + 1), A.add)
+    for b in range(12):
+        if b < VBX:
+            mset(ap("ZH", 272 * b + 256, 272 * b + 272), 0.0)
+        if b >= (L - SV) // 16:
+            act(dict(ap("MW", 272 * b + 256, 272 * b + 272), r=[("MW%d" % k, b, b + 1) for k in range(16)]), ap("ONE", 0, 16), F.Identity)
+    mset(rows("E", 0, 144, 16, 17), 0.0)
+    mset(rows("NM", 0, 12, 16, 17), 0.0)
+    mset(rows("HI", 0, 12, 16, 17), 0.0)
+    mset(ap("RDA"), BIG)
+    mset(ap("RDA", 0, 204, 17), -4 * BIG)
+    ts(ap("RDA", 16, 204, 17), ap("IO", 0, L, 16), col(1), A.add, float(C + 1), A.add)
     ts(ap("DVU"), ap("IO", 0, 384, 16), col(1), A.add, float(NV), A.add)
     ts(ap("NL"), ap("NB"), B0 + 192 - HN, A.add)
-    ts(ap("R", 0, 512), dict(ap("RI", 0, 512), r=kin), UP - EPS, A.add)
+    act(ap("R", 0, 512), dict(ap("RI", 0, 512), r=kin), F.Identity, bias=UP - EPS)
     ts(ap("R", 512, NV), dict(ap("RI", 512, NV), r=kin), UP + EPS, A.add)
     copy(ap("FN16", 0, 6), ap("FNI", 0, 6))
     copy(ap("SN16", 0, 6), ap("SNI", 0, 6))
 
-    def matches(key16, keys, top, rep, E, bank, first, parts):
-        items = [(ap(bank, 0, L), ap("IB"), ap(first))]
-        for m in parts:
-            if m == parts[0] or m == 0:
-                e = parts[0] if m < parts[0] else 12
-                copy(ap(rep, 16 * m, 16 * e), ind("IO", 0, top, ap(key16[0], key16[1] + m, key16[1] + e)))
-            row = lambda a, b: dict(v=T[E][:, m, a:b], n=b - a, r=[(E, m * L + a, m * L + b)], dt=bf, ps=False)
-            ts(row(0, L - 16 * m), ap(rep, 16 * m, L), keys(m), A.is_equal)
-            if m < 11:
-                items.append((ap(bank, 16 * m + 16, L), ap("BOO"), row(16, L - 16 * m)))
-            if m % 6 == 5:
-                own = dict(v=T[E][:, m - 5:m + 1, 0:16], n=96, r=[(E, (m - 5) * L, (m + 1) * L)], dt=bf, ps=False)
-                items.append((ap(bank, 16 * m - 80, 16 * m + 16), ap("BOD"), own))
-        group(items)
-
     def to_list(out, src, n):
         group([(out, ap("WD", 15 - q, 143 - q), ap(src, q, n, 16)) for q in range(16)])
 
-    def nodes(k):
+    def nodes(k, v):
         lv, u = "LV%d" % k, "U%d" % k
-        ts(ap("H1"), ap(lv, 0, 12), 512.0, A.is_ge, -512.0, A.mult)
-        ts(ap("H2"), ap(lv, 0, 12), 512.0, A.is_lt, 512.0, A.mult)
-        tt(ap(lv, 24, 36), ap(lv, 0, 12), ap("H1"), A.add)
+        ts(ap("H1"), v, 512.0, A.is_ge, -512.0, A.mult)
+        ts(ap("H2"), v, 512.0, A.is_lt, 512.0, A.mult)
+        tt(ap(lv, 24, 36), v, ap("H1"), A.add)
         tt(ap(lv, 12, 24), ap(lv, 24, 36), ap("H2"), A.add)
-        copy(ap(u), ap(lv))
+        if k:
+            copy(ap(u, 0, 12), v)
+            copy(ap(u, 12, 36), ap(lv, 12, 36))
+        else:
+            copy(ap(u), ap(lv))
+
+    def pairs(k):
+        lv, u = "LV%d" % k, "U%d" % k
+        act(ap("REPA", 0, L), ind("IO", 0, 512, ap(u, 24, 36)), F.Identity)
+        if k == 0:
+            act(ap("REPA", L, 288), ap("REPA", 0, LN), F.Identity)
+        for m in range(12):
+            e = 288 if k == 0 and m >= 6 else L
+            ts(rows("EA" if k else "EA0", m, m + 1, 0, e - 16 * m), ap("REPA", 16 * m, e), ap(lv, 24 + m, 25 + m), A.is_equal)
 
     def acting(k, bank):
-        lv, u, of, pn = "LV%d" % k, "U%d" % k, "OF%d" % k, "PN%d" % k
-        matches((u, 24), lambda m: ap(lv, 24 + m, 25 + m), 512, "REPA", "EA", bank, "CDR", range(12))
+        lv, of, pn = "LV%d" % k, "OF%d" % k, "PN%d" % k
+        items, ea = [(ap(bank, 0, L), ap("IB"), ap("CDR"))], "EA" if k == 2 else "EA0"
+        for m in range(12):
+            h = m // 6
+            at, e = (LN - 2 * LN * h, LN + LN * h) if k == 1 else (0, L)
+            if 16 * m + 16 < e:
+                items.append((ap(bank, at + 16 * m + 16, at + e), ap("BOO"), rows(ea, m, m + 1, 16, e - 16 * m)))
+            if k == 1 and h:
+                items.append((ap(bank, LN, L), ap("BOO"), rows(ea, m, m + 1, L - 16 * m, 288 - 16 * m)))
+            if m % 6 == 5:
+                items.append((ap(bank, at + LN * h, at + LN * h + LN), ap("BOD"), rows(ea, m - 5, m + 1, 0, 16)))
+        group(items)
         act(ap(pn), ap(bank, 0, L), F.Relu)
         lose = ap(bank, L, L + 12)
         to_list(lose, pn, L)
-        tt(ap("T3", 0, 12), lose, ap(lv, 0, 12), A.max)
-        tt(ap("T3", 12, 24), lose, ap(lv, 12, 24), A.max)
+        tt(rows("T3", 0, 2, 0, 6), lose, ap("KL", 3, 48, 4) if k == 2 else ap(lv, 0, 12), A.max)
+        tt(rows("T3", 0, 2, 6, 12), lose, ap(lv, 12, 24), A.max)
         tt(ap("T4"), ap("T3"), ap("DVU"), A.min)
         copy(ap(of), ap("T4"))
 
     copy(ap("LV0", 0, 12), ap("RTI"))
-    nodes(0)
+    nodes(0, ap("LV0", 0, 12))
+    pairs(0)
     acting(0, "P7")
 
     def kids():
@@ -292,148 +344,171 @@ def build(T, topo, rank):
         ts(ap("T1"), ap("LV0", 0, 12), 512.0, A.is_ge, 2.0, A.mult)
         ts(ap("T2"), ap("T1"), -1.0, A.add)
         for j in range(2):
-            tt(ap("MID0", 12 * j, 12 * j + 12), ap("KL", 24 * j, 24 * j + 12), ap("KL", 24 * j + 12, 24 * j + 24), A.add)
+            tt(ap("MH0", 3 - j, 48, 4), ap("KL", 24 * j, 24 * j + 12), ap("KL", 24 * j + 12, 24 * j + 24), A.add)
             tt(ap("KM", 12 * j, 12 * j + 12), ap("KL", 24 * j, 24 * j + 12), ap("KL", 24 * j + 12, 24 * j + 24), A.subtract)
-            tt(ap("HH0", 12 * j, 12 * j + 12), ap("KM", 12 * j, 12 * j + 12), ap("T2"), A.mult)
-        for nm in ("MID", "HH"):
-            for j in range(4):
-                act(ap(nm + "1", 6 * j, 6 * j + 6), ap(nm + "0", 6 * (j ^ 1), 6 * (j ^ 1) + 6), F.Identity)
+            tt(ap("MH0", j, 48, 4), ap("KM", 12 * j, 12 * j + 12), ap("T2"), A.mult)
+        act(ap("MH1", 0, 24), ap("MH0", 24, 48), F.Identity)
+        act(ap("MH1", 24, 48), ap("MH0", 0, 24), F.Identity)
+        mset(ap("OO", 0, 48, 4), 0.0)
 
     def level(t, l):
         k = (t & 1) if l == 0 else 2
         U, OF, PN, W = "U%d" % k, "OF%d" % k, "PN%d" % k, "W%d" % t
         nameF = ap("NF0") if t == 0 else ap("NL", LN * t - LN, LN * t)
-        stamp = (t + 2) * EPS
         begin, last = t == 0 and l == 0, t == RO - 1 and l == 1
-        VV, VU = VVS[l], VUS[l]
-        SV, SU = L - VV, L - VU
-        if begin:
-            copy(ap("O16", 0, L), dict(ind("RI", 0, NV, ap(U, 0, 12)), r=kin))
-        else:
-            ts(ap("O16", 0, L), ind("R", 0, RW, ap(U, 0, 12)), 0.25 - UP, A.add)
+        SL, VU = SVS[l], VUS[l]
+        VV, VB = L - SL, (L - SL) // 16
+        NM = lambda a, b: lanes("NM", a, b)
+        for a in (0, 12):
+            if begin:
+                copy(ap("O16", 16 * a, 16 * a + L), dict(ind("RI", 0, NV, ap(U, a, a + 12)), r=kin))
+            else:
+                ts(ap("O16", 16 * a, 16 * a + L), ind("R", 0, RW, ap(U, a, a + 12)), 0.25 - UP, A.add)
         X = lambda a, b: ind("X", 0, XW, ap("O16", a, b))
 
-        def stepped(o0, h0, n):
-            for a in range(0, n, 32):
-                b = min(n, a + 32)
-                tt(ap("ZH", 16 * (h0 + a), 16 * (h0 + b)), X(o0 + a, o0 + b), ap("OFS", 0, 16 * (b - a)), A.add)
-            for a in range(h0, h0 + n, 16):
-                z0, z1 = 16 * a, 16 * a + 256
-                scan(ap("MXH", 8 * a, 8 * a + 128), ap("ZH", z0, z1, 2), ap("ZH", z0 + 1, z1, 2), A.max, A.max, -4096.0)
-                scan(ap("MNH", 8 * a, 8 * a + 128, -1), ap("ZH", z0, z1, -2), ap("ZH", z0, z1 - 1, -2), A.min, A.min, 4096.0)
+        def ends(z, n, mx, mn):
+            scan(mx, z(0, n, -2), z(0, n - 1, -2), A.max, A.max, -4096.0)
+            scan(mn, z(0, n, 2), z(1, n, 2), A.min, A.min, 4096.0)
 
-        def plain(z, mx, mn, o0, n):
-            for a in range(0, n, 32):
-                b = min(n, a + 32)
-                act(ap(z, 16 * a, 16 * b), X(o0 + a, o0 + b), F.Identity)
-            for a in range(0, n, 32):
-                b = min(n, a + 32)
-                scan(ap(mx, 16 * a, 16 * b), ap("MXR", 0, 16 * (b - a)), ap(z, 16 * a, 16 * b), A.add, A.max)
-                scan(ap(mn, 16 * a, 16 * b), ap("MNR", 0, 16 * (b - a)), ap(z, 16 * a, 16 * b), A.add, A.min)
+        def stepped(z, mx, mn, o0, blocks):
+            n = 1 if z == "ZH" else 2
+            for b in blocks:
+                tt(ap(z, 272 * b, 272 * b + 256) if n == 1 else ap(z, 256 * b, 256 * b + 512), X(o0 + 16 * b, o0 + 16 * (b + n)), ap("OFS", 0, 256 * n), A.add)
+                for j in range(b, b + n):
+                    a = 272 * j if n == 1 else 256 * j
+                    ends(lambda c, e, s: ap(z, a + c, a + e, s), 256, ap(mx, 128 * j, 128 * j + 128, -1), ap(mn, 128 * j, 128 * j + 128))
 
-        def midrange(c0, own, a, b, rounded, bank="P4"):
-            o = lambda a, b: ap(bank, c0 + a, c0 + b)
-            mx, mn = ("MXV", "MNV") if own else ("MXU", "MNU")
-            (h0, h1, hz), (s0, s1) = ((SV, L, 0), (0, SV)) if own else ((0, VU, VV), (VU, L))
-            items = [(o(a, b), ap("NI"), ap(W, a, b))]
-            x, y = max(a, h0), min(b, h1)
-            if x < y:
-                z0, z1 = 8 * (hz + x - h0), 8 * (hz + y - h0)
-                items += [(o(x, y), ap("NO"), ap("OFL", 0, y - x)), (o(x, y), ap("IH"), ap("MXH", z0 + 7, z1, 8)),
-                          (o(x, y), ap("IH"), ap("MNH", z0, z1, 8))]
-            x, y = max(a, s0), min(b, s1)
-            if x < y:
-                items += [(o(x, y), ap("IH"), ap(m, 16 * (x - s0) + 15, 16 * (y - s0), 16)) for m in (mx, mn)]
-            if rounded:
-                items.append((o(a, b), ap("IB"), ap("MAGT", a, b)))
-            group(items)
+        def gathered(z, a, o0):
+            act(ap(z, 16 * a, 16 * a + 512), X(o0, o0 + 32), F.Identity)
 
-        stepped(SV, 0, VV)
-        plain("ZV", "MXV", "MNV", 0, SV)
-        act(ap("RVU"), ind("R", 0, RW, ap(U, 0, 24)), F.Identity)
-        ts(ap("O16", L, 384), ap("RVU", L, 384), 0.25 - UP, A.add)
-        ts(ap("HI"), ap("O16", 0, L), 1.0 / 64, A.mult, 128.0, A.add)
-        ts(ap("NM"), ap("O16"), -HN, A.add)
-        for i, c in enumerate(sorted(range(6), key=lambda c: (c < 3, 32 * c < SV, c))):
-            o, q = ap(YB[i]), (32 * (c % 3), 32 * (c % 3) + 32)
-            items = [(o, ap("WT", 128 * (c // 3), 128 * (c // 3) + 128, p=q), ap("EX", p=q))]
-            if 32 * c < SV:
-                items.append((o, ap("IB"), ap("ZV", 512 * c, 512 * c + 512)))
+        def extremes(z, a, w0, n, mx, mn, px, pn):
+            at = lambda name: ap(name, 16 * a, 16 * a + 512)
+            if w0 < n:
+                sem = "a%s%d" % (z, a // 32)
+                used[sem] = used.get(sem, 0) + 16
+                add("G", lambda g: g.dma_start(at(z)["v"], ap("OFH")["v"], accum_op=A.add), [at(z), ap("OFH")], [at(z)], (0, 0, 0, GIS, 0), sem=sem, lat=GLAT)
+                ops[-1]["cnt"] = used[sem]
+                for j in (0, 1):
+                    c, e = 16 * a + 256 * j, 8 * w0 + 128 * j
+                    ends(lambda x, y, s: ap(z, c + x, c + y, s), 256, ap(mx, e, e + 128, -1), ap(mn, e, e + 128))
             else:
-                items += [(o, ap("NI"), ap("OFS")), (o, ap("IB"), ap("ZH", 512 * c - 16 * SV, 512 * c - 16 * SV + 512))]
+                scan(at(px), ap("MXR"), at(z), A.add, A.max)
+                scan(at(pn), ap("MNR"), at(z), A.add, A.min)
+
+        NV_, NU_ = VV + 32 * DVS[l], VU + 32 * DUS[l]
+
+        def midrange(bank, c0, own, rounded, a=0, b=L):
+            o = lambda a, b: ap(bank, c0 + a, c0 + b)
+            items = [(o(a, b), ap("NI"), ap(W, a, b))]
+            n, n0, mx, mn, px, pn = (NV_, VV, "MXH", "MNH", "MXV", "MNV") if own else (NU_, VU, "MXU", "MNU", "MXS", "MNS")
+            e = min(n, b)
+            if a < e:
+                items += [(o(a, e), ap("NO"), ap("OFL", a, e)), (o(a, e), ap("IH"), ap(mx, 8 * a, 8 * e, 8)), (o(a, e), ap("IH"), ap(mn, 8 * a + 7, 8 * e, 8))]
+            e = max(n, a)
+            if e < b:
+                items += [(o(e, b), ap("IH"), ap(m, 16 * (e - n0) + 15, 16 * (b - n0), 16)) for m in (px, pn)]
+            if rounded:
+                items.append((o(a, b), ap("IMAG"), ap("ONE", a, b)))
             group(items)
-            act(ap("AB", 512 * c, 512 * c + 512), o, F.Abs)
+
+        stepped("ZH", "MXH", "MNH", 0, sorted(range(VB), key=lambda b: b < 6))
+        for a in range(0, SL, 32):
+            gathered("ZV", a, VV + a)
+        act(ap("RV"), ind("R", 0, RW, ap(U, 0, 12)), F.Identity)
+        ts(lanes("HI", 0, L), ap("O16", 0, L), 1.0 / 64, A.mult, 128.0, A.add)
+        ts(NM(0, 384), ap("O16"), -HN, A.add)
+        for c in range(SL // 32):
+            o, q, b = ap(YB[c]), (SV - SL + 32 * c, SV - SL + 32 * c + 32), VB + 2 * c
+            group([(o, ap("WT", p=q), ap("EX", p=q)), (o, ap("IB"), ap("ZV", 512 * c, 512 * c + 512))])
+            for j in (0, 1):
+                act(dict(ap("MW", 272 * (b + j), 272 * (b + j) + 256), r=[("MW%d" % s, b + j, b + j + 1) for s in range(16)]),
+                    ap(YB[c], 256 * j, 256 * j + 256), F.Abs, scale=0.5)
+            extremes("ZV", 32 * c, VV + 32 * c, NV_, "MXH", "MNH", "MXV", "MNV")
+        for s in range(16):
+            scan(slot("MW", 0, VB, s), slot("ZH", 0, VB, s), ap("WS", 0, 17 * VB), A.min, A.max, 4096.0)
         for h in (1, 0):
-            bk = "P%d" % h
-            keys = [(ap(bk, 0, 256, p=P96), ap("HI", 96 * h, 96 * h + 96), ap("IK")),
-                    (ap(bk, 0, 128, p=P96), ap("NM", 96 * h, 96 * h + 96), ap("IB"))]
-            keys += [(ap(bk, s, 256, 16, p=P96), ap("AB", 1536 * h + s, 1536 * h + 1536, 16), ap("G2")) for s in range(16)]
+            bk, b0, b1 = "P%d" % h, 6 * h, min(6 * h + 6, VB)
+            keys, pz = [], (0, 17 * (b1 - b0))
+            if b0 < b1:
+                keys += [(ap(bk, a, a + 128, p=pz), ap("WS", 17 * b0, 17 * b1), ap("BN2")) for a in (0, 128)]
+                keys += [(ap(bk, s, 256, 16, p=pz), slot("ZH", b0, b1, s), ap("GN")) for s in range(16)]
+            keys += [(ap(bk, s, 256, 16, p=PK), slot("MW", b0, b0 + 6, s), ap("G4")) for s in range(16)]
+            hi = rows("HI", b0, b0 + 6, 0, 17)
+            keys += [(ap(bk, 0, 128, p=PK), hi, ap("N64")), (ap(bk, 128, 256, p=PK), hi, ap("IB")),
+                     (ap(bk, 0, 128, p=PK), rows("NM", b0, b0 + 6, 0, 17), ap("IB"))]
             group(keys)
-            scan(ap("ST", 256 * h, 256 * h + 256, p=P96), ap("RT", p=P96), ap(bk, 0, 256, p=P96), A.add, A.min)
-            ts(ap("RR", 16 * h, 16 * h + 16, p=P96), ap("ST", 256 * h + 15, 256 * h + 256, 16, p=P96), M30, A.add, M30, A.subtract)
-            tt(ap("DIG", 16 * h, 16 * h + 16, p=P96), ap("ST", 256 * h + 15, 256 * h + 256, 16, p=P96), ap("RR", 16 * h, 16 * h + 16, p=P96), A.subtract)
+            scan(ap("ST", 256 * h, 256 * h + 256, p=PK), ap("RT", p=PK), ap(bk, 0, 256, p=PK), A.add, A.min)
+            ts(ap("RR", 16 * h, 16 * h + 16, p=PK), ap("ST", 256 * h + 15, 256 * h + 256, 16, p=PK), M30, A.add, M30, A.subtract)
+            tt(ap("DIG", 16 * h, 16 * h + 16, p=PK), ap("ST", 256 * h + 15, 256 * h + 256, 16, p=PK), ap("RR", 16 * h, 16 * h + 16, p=PK), A.subtract)
             group([(ap(bk, 256, 304), ap("IB"), ap("PEN8"))]
-                  + [(ap(bk, 256 + 8 * m, 264 + 8 * m), ap("LM64" if ab else "LM1", 128 * m, 128 * m + 128, p=P96),
-                      ap("DIG", 16 * h + 8 * ab, 16 * h + 8 * ab + 8, p=P96)) for m in range(6) for ab in range(2)])
+                  + [(ap(bk, 256 + 8 * m, 264 + 8 * m), ap("LM64" if ab else "LM1", 128 * m, 128 * m + 128, p=PK),
+                      ap("DIG", 16 * h + 8 * ab, 16 * h + 8 * ab + 8, p=PK)) for m in range(6) for ab in range(2)])
             scan(ap("CS", 48 * h, 48 * h + 48), ap("RS8"), ap(bk, 256, 304), A.add, A.min)
-            copy(ap("C16", 6 * h, 6 * h + 6), ap("CS", 48 * h + 7, 48 * h + 48, 8))
+            ts(ap("C16", 6 * h, 6 * h + 6), ap("CS", 48 * h + 7, 48 * h + 48, 8), HN, A.add)
         nb = ap("NB", LN * t, LN * t + LN)
-        group([(ap("P7", 0, 96), ap("IB"), ap("NM", 0, 96)), (ap("P7", 0, 96), ap("NI"), nb),
-               (ap("P7", 96, L), ap("IB"), ap("NM", L, 288)), (ap("P7", 96, L), ap("NI"), nb)])
-        tt(ap("TL"), ap("P7", 0, L), ap("LM", t, t + L), A.mult)
-        d, o = ap("P5", L, 288), ap("P5", 288, 480)
-        group([(o, ap("IF"), ap("RVU", 0, L)), (o, ap("NI"), ap("NM", 0, L)), (o, ap("IM"), ap("MAGT"))])
-        act(ap("FR"), o, F.Identity, bias=-HN - UP - MAG * EPS)
+        group([(ap("P2", 0, 96), ap("IB"), NM(0, 96)), (ap("P2", 0, 96), ap("NI"), nb),
+               (ap("P2", 96, L), ap("IB"), NM(L, 288)), (ap("P2", 96, L), ap("NI"), nb)])
+        tt(ap("TL"), ap("P2", 0, L), ap("LM", t, t + L), A.mult)
+        d, o = ap("P2", L, 288), ap("P2", 288, 480)
+        dg, pos, neg = (ap("DG16"), ap("IB"), ap("NI")) if t else (ap("DG"), ap("IF"), ap("NIF"))
         if l == 0:
-            act(ap("SG", 0, L), o, F.Sign, bias=-HN - UP - MAG * EPS)
-            group([(d, ap("IB"), ap("NM", 96, L)), (d, ap("NI"), nameF)])
-            act(ap("A2"), d, F.Abs)
-            act(ap("TP"), ap("IF"), F.Identity, scale=stamp)
-            act(ap("TN"), ap("IF"), F.Identity, scale=-stamp)
+            group([(o, ap("IF"), ap("RV")), (o, ap("NI"), NM(0, L))])
+            act(ap("SG", 0, L), o, F.Sign, bias=-HN - UP)
+            group([(d, ap("IB"), NM(96, L)), (d, ap("NI"), nameF)])
         else:
-            group([(d, ap("IB"), ap("NM", 96, L)), (d, ap("NI"), nameF), (d, ap("IB"), ap("FR", 96, L))])
-            act(ap("A1"), d, F.Abs)
-            act(ap("A2"), ap("A1"), F.Relu, bias=EPS / 2 - stamp)
-        group([(d, ap("IQ"), ap("A2")), (d, ap("NI"), nameF)])
-        act(ap("DG"), d, F.Relu, bias=C - HN)
-        bv, bu = ap("P7", 0, L), ap("P7", L, 384)
-        cv, cu = ap("P5", 0, L), ap("P5", L, 384)
-        group([(bu, ap("IB"), ap("NM", 0, L)), (bu, ap("NI"), ap("NM", L, 384)), (bu, ap("I2" if l else "IB"), ap("FR"))]
-              + ([(bu, ap("TP"), ap("SG", 0, L))] if l == 0 else []))
-        group([(bv, ap("NI"), ap("NM", 0, L)), (bv, ap("IB"), ap("NM", L, 384)), (bv, ap("N2" if l else "NI"), ap("FR")),
-               (ap("P7", 0, 96), ap("NI"), ap("TL", 96, L)), (ap("P7", 0, 96), ap("IB"), ap("TL", 0, 96)), (ap("P7", 96, L), ap("NIF"), ap("DG"))]
-              + ([(bv, ap("TN"), ap("SG", 0, L))] if l == 0 else []))
-        group([(ap("P5", 0, 384), ap("IB"), ap("NM")), (cv, ap("IC"), ap("HALF")), (cu, ap("IC"), ap("HALF")), (cv, ap("IB"), ap("FR")),
-               (cu, ap("NI"), ap("FR")), (ap("P5", 0, 96), ap("NI"), ap("TL", 0, 96)), (ap("P5", 0, 96), ap("IL"), ap("LM", t, t + 96)),
-               (ap("P5", 96, L), ap("IF"), ap("DG"))])
+            group([(o, ap("IF"), ap("RV")), (o, ap("NI"), NM(0, L)), (o, ap("IME"), ap("ONE", 0, L))])
+            act(ap("FR"), o, F.Identity, bias=-HN - UP - MAG * EPS)
+            group([(d, ap("IB"), NM(96, L)), (d, ap("NI"), nameF), (d, ap("IB"), ap("FR", 96, L))])
+        act(ap("A1"), d, F.Abs)
+        group([(d, ap("IQ"), ap("A1")), (d, ap("HM"), nameF)])
+        act(dg, d, F.Relu, bias=(C - HN) / 2 + l * 2.0 ** 19 * EPS)
+        hd, mid = (lambda j, n=1: ap("P7", LN * j, LN * (j + n))), (lambda j, n=1: ap("P5", LN * j, LN * (j + n)))
+        own, riv = (lambda j: NM(LN * (j // 2), LN * (j // 2 + 1))), (lambda j: NM(L + LN * (j // 2), L + LN * (j // 2 + 1)))
+        mk = lambda j: ap("FR" if l else "SG", LN * (j // 2), LN * (j // 2 + 1))
+        group([(hd(j), ap("HP" if j % 2 else "HM"), own(j)) for j in range(4)] + [(hd(j), ap("HM" if j % 2 else "HP"), riv(j)) for j in range(4)]
+              + [(hd(j), ap((("E3", "E3P"), ("NI", "IB"))[l][j % 2]), mk(j)) for j in range(4)]
+              + [(hd(0), ap("HP"), ap("TL", 0, 96)), (hd(0), ap("HM"), ap("TL", 96, L)), (hd(2), neg, dg)])
+        group([(mid(j), ap("HP"), x(j)) for x in (own, riv) for j in range(4)]
+              + [(mid(0, 4), ap("IK0"), ap("ONE")), (mid(0), ap("IL"), ap("LM", t, t + 96))]
+              + [(mid(j), ap("EP" if j % 2 else "EM"), mk(j)) for j in range(4) if l == 0]
+              + [(mid(0), ap("HM"), ap("TL", 0, 96)), (mid(0), ap("HM"), ap("TL", 96, L)), (mid(2), pos, dg)])
         if l == 0:
-            midrange(L, True, 0, L, False, "P6")
+            midrange("P6", L, True, False)
             act(ap("SG", L, 384), ap("P6", L, 384), F.Sign, scale=-1.0, bias=0.625)
-        midrange(0, True, 0, L, True)
+        midrange("P4", 0, True, True)
         act(ap("HA", 0, L), ap("P4", 0, L), F.Abs, bias=-MAG)
         if l == 0:
             if t == 0:
                 kids()
             to_list(ap("P6", 0, 24), "SG", 384)
-            act(ap("OO", 0, 12), ap("P6", 0, 12), F.Sign)
-            act(ap("OO", 12, 24), ap("P6", 0, 12), F.Sign)
-            act(ap("SBL"), ap("P6", 12, 24), F.Sign, bias=-1.0)
-            tt(ap("T4"), ap("OO"), ap("HH%d" % k), A.mult)
-            tt(ap("KM"), ap("T4"), ap("MID%d" % k), A.add)
-            tt(ap("H1"), ap("SBL"), ap("KM", 12, 24), A.mult)
-            tt(ap("LV2", 0, 12), ap("H1"), ap("KM", 0, 12), A.add)
-            nodes(2)
-        stepped(L, VV, VU)
-        plain("ZU", "MXU", "MNU", L + VU, SU)
-        act(ap("RDC", 15, L, 16), ap("CS", 7, 96, 8), F.Relu, scale=4 * BIG, bias=-(C - 0.5) * 4 * BIG)
+            for j, a, c in ((2, 0, 0.0), (1, 12, -1.0), (3, 12, -1.0)):
+                act(dict(ap("OO", j, 48, 4), r=[("OO%d" % j, 0, 1)]), ap("P6", a, a + 12), F.Sign, bias=c)
+            scan(ap("KL"), dict(ap("OO"), r=[("OO", 0, 48)] + [("OO%d" % j, 0, 1) for j in (1, 2, 3)]), ap("MH%d" % k), A.mult, A.add)
+            nodes(2, ap("KL", 3, 48, 4))
+        stepped("ZU", "MXU", "MNU", L, range(0, VU // 16, 2))
+        for a in range(0, L - VU, 32):
+            gathered("ZS", a, L + VU + a)
+            extremes("ZS", a, VU + a, NU_, "MXU", "MNU", "MXS", "MNS")
+        names = ap("CS", 7, 96, 8)
+        act(ap("EF"), names, F.Relu, scale=4 * BIG, bias=-(C - HN - 0.5) * 4 * BIG)
         act(ap("XC"), ind("X", 0, XW, ap("C16")), F.Identity)
-        matches(("C16", 0), lambda m: ap("CS", 8 * m + 7, 8 * m + 8), IW, "REP", "E", "P2", "CD", [6, 7, 8, 9, 10, 11, 0, 1, 2, 3, 4, 5])
-        copy(ap("DN", 1, 24, 2), ap("CS", 7, 96, 8))
-        scan(ap("SD"), ap("RDC"), ap("P2", 0, L), A.add, A.max)
-        scan(ap("XO"), ap("SD", 7, L, 8), ap("DN"), A.min, A.max)
-        copy(ap("XO16"), ap("XO", 1, 24, 2))
+        items = [(ap("P2", 0, 204), ap("IB"), ap("CD"))]
+        for m in (6, 7, 8, 9, 10, 11, 0, 1, 2, 3, 4, 5):
+            if m % 6 == 0:
+                act(ap("REP", 16 * m, 16 * m + 96), ind("IO", 0, IW, ap("C16", m, m + 6)), F.Identity, bias=-HN)
+            ts(rows("E", 12 * m, 11 * m + 12, 0, 16), ap("REP", 16 * m, L), ap("CS", 8 * m + 7, 8 * m + 8), A.is_equal)
+            if m < 11:
+                items.append((ap("P2", 17 * m + 17, 204), ap("BOO"), rows("E", 12 * m + 1, 11 * m + 12, 0, 17)))
+            if m % 6 == 5:
+                own = dict(rows("E", 0, 6, 0, 17), v=T.E[:, 12 * m - 60:12 * m + 1:12, :], r=[("E", 204 * j, 204 * j + 17) for j in range(m - 5, m + 1)])
+                items.append((ap("P2", 17 * m - 85, 17 * m + 17), ap("BOD"), own))
+            if m == 0:
+                items += [(ap("P2", 16, 204, 17), ap("IF"), names), (ap("P2", 0, 204, 17), ap("IB"), ap("EF"))]
+        group(items)
+        scan(ap("SD"), ap("RDA"), ap("P2", 0, 204), A.min, A.max)
+        copy(ap("XO16"), ap("SD", 16, 204, 17))
         o = ap("P6", 0, L)
-        group([(o, ap("IH"), ap(x)) for x in (W, "XC")] + [(o, ap("IB"), ap("MAGT"))])
+        group([(o, ap("IH"), ap(x)) for x in (W, "XC")] + [(o, ap("IMAG"), ap("ONE", 0, L))])
         act(ap("VAL"), o, F.Identity, bias=-MAG)
         copy(ind("X", 0, XW, ap("XO16")), ap("VAL"))
         if last:
@@ -441,21 +516,26 @@ def build(T, topo, rank):
         elif l == 1:
             hand_on(t)
         if l == 0:
+            pairs(2)
             acting(2, "P6")
-        for i, (a, b) in enumerate(((0, CUT), (CUT, L))):
-            midrange(0, False, a, b, True)
-            act(ap("HA", L + a, L + b), ap("P4", a, b), F.Abs, bias=-MAG)
-            o = ap("P1", a, b)
-            group(([] if begin else [(o, ap("DP"), ap("HALF", a, b))])
-                  + [(o, ap("IN"), ap(PN, a, b)), (o, ap("BOP"), ap("HA", a, b)), (o, ap("BON"), ap("HA", L + a, L + b))])
-            ts(ap("EB", a, b), o, 8192.0, A.is_gt)
-            for c in (0, L):
-                tt(ap("TT", c + a, c + b), ap("P7", c + a, c + b), ap("EB", a, b), A.mult)
-                tt(ap("NEW", c + a, c + b), ap("P5", c + a, c + b), ap("TT", c + a, c + b), A.add)
-                act(ind("R", 0, RW, ap(OF, (c + a) // 16, (c + b) // 16)), ap("NEW", c + a, c + b), F.Silu)
-        if not last:
-            act(ap("JUNK"), ap("EB"), F.Identity, accum=ap("SUM", 0, 1))
-            act(ap("DP"), ap("IA"), F.Identity, scale=ap("SUM", 0, 1))
+        for i in range(2):
+            a, b = LN * i, LN * i + LN
+            midrange("P3", 0, False, True, a, b)
+            act(ap("HA", L + a, L + b), ap("P3", a, b), F.Abs, bias=-MAG)
+            o = ap("P4", L + a, L + b)
+            group([(o, ap("IN"), ap(PN, a, b)), (o, ap("BOP"), ap("HA", a, b)), (o, ap("BON"), ap("HA", L + a, L + b))])
+            act(ap("EB", a, b), o, F.Sign, bias=-8192.0 if begin else ap("THR", 1, 2), accum=None if last else ap("SUM", i, i + 1))
+            for j in (2 * i, 2 * i + 1):
+                tt(ap("TT", LN * j, LN * j + LN), hd(j), ap("EB", a, b), A.mult)
+            new, to = ap("NEW", 2 * a, 2 * b), ind("R", 0, RW, ap(OF, 12 * i, 12 * i + 12))
+            if VSC[2 * l + i]:
+                act(new, mid(2 * i, 2), F.Identity)
+                tt(to, new, ap("TT", 2 * a, 2 * b), A.add)
+            else:
+                tt(new, mid(2 * i, 2), ap("TT", 2 * a, 2 * b), A.add)
+                act(to, new, F.Silu)
+        for i in range(0 if last else 2):
+            act(ap("THR", i, i + 1), ap("SUM", i, i + 1), F.Identity, scale=-8192.0, bias=ap("THR", 0, 1) if i else -8192.0 * (L + 1))
 
     def shares(r):
         me = T.cores[r]
@@ -496,6 +576,8 @@ def build(T, topo, rank):
         ops.append(dict(e="X", fn=None, rd=[("wire", t, t + 1)], wr=[(land, 16, LN)], t=0.0, c=(0, 0, 0, 0, 0), acc=False, lat=0.0, sem="arr%d" % t,
                         cnt=sum(len(shares((rank - d) % N)[d]) for d in range(1, N))))
 
+    for a in range(8):
+        pick(ap("DM", 128 * a, 128 * a + 128), ap("IF"), [[0, 16], [1, 8]], -a)
     for t in range(RO):
         p0, W = B0 + LN * t, "W%d" % t
         if t > 0:
@@ -503,23 +585,23 @@ def build(T, topo, rank):
         act(ap("X", p0, p0 + LN), ap(W, 0, LN), F.Identity)
         if t == 0:
             act(ap(W, LN, L), ind("X", 0, XW, ap("FN16", 0, 6)), F.Identity)
-            ts(ap("NF0"), ind("IO", 0, IW, ap("FN16", 0, 6)), -HN, A.add)
-        for h in (1, 0):
-            for q in range(3):
-                mm(ap("P6", 0, 128, p=(32 * q, 32 * q + 32)), ap(W, 96 * h + 32 * q, 96 * h + 32 * q + 32), ap("IB"), True, True)
-            act(ap("WT", 128 * h, 128 * h + 128, p=P96), ap("P6", 0, 128, p=P96), F.Identity)
+            act(ap("NF0"), ind("IO", 0, IW, ap("FN16", 0, 6)), F.Identity, bias=-HN)
+        for q in range(SV // 32):
+            mm(ap("P6", 0, 128, p=(32 * q, 32 * q + 32)), ap(W, L - SV + 32 * q, L - SV + 32 * q + 32), ap("IB"), True, True)
+        act(ap("WT", p=(0, SV)), ap("P6", 0, 128, p=(0, SV)), F.Identity)
+        o = ap("P6", 128, 128 + 17 * VBX)
+        group([(o, ap("IB"), ap("O17"))] + [(ap("P6", 128 + 17 * b, 144 + 17 * b), ap("IB"), ap(W, 16 * b, 16 * b + 16)) for b in range(VBX)])
+        act(ap("WS"), o, F.Identity)
         level(t, 0)
         if t == 1:
-            ts(col(10), col(3), 128.0, A.mult, col(0), A.add)
-            ts(ap("DM"), ap("IO", 0, NV), col(10), A.is_equal)
             copy(ap("KS"), ap("K2"))
             tt(ap("KD"), ap("KS", 64, 128), ap("KS", 0, 64), A.subtract)
         level(t, 1)
         if t == 0:
-            copy(ap("LV1", 0, 6), ap("RTI", 6, 12))
-            copy(ap("LV1", 6, 12), ap("RTI", 0, 6))
-            nodes(1)
-            acting(1, "P4")
+            copy(rows("LV1", 0, 3, 0, 6), rows("LV0", 0, 3, 6, 12))
+            copy(rows("LV1", 0, 3, 6, 12), rows("LV0", 0, 3, 0, 6))
+            copy(ap("U1"), ap("LV1"))
+            acting(1, "P1")
     ts(ap("YR", 0, YV), ap("R", 0, YV), MAG, A.add, MAG + UP, A.subtract)
     dma("Y", "yr0", T.yr[:, 0:YV], T.YR[:, 0:YV], [ap("YR", 0, YV)], [], 2.5)
     act(ap("Y1"), ap("R", YV, NV), F.Identity, bias=MAG)
@@ -527,9 +609,8 @@ def build(T, topo, rank):
     dma("S", "yr1", T.yr[:, YV:NV], T.YR[:, YV:NV], [ap("YR", YV, NV)], [], 2.5)
     o = ap("P2", 0, 64)
     group([(o, ap("DM", 128 * a, 128 * a + 128), ap("R", 64 * a, 64 * a + 64)) for a in range(8)])
-    ts(ap("RS", 0, 64), o, MAG, A.add, MAG, A.subtract)
-    tt(ap("RS", 64, 128), o, ap("RS", 0, 64), A.subtract)
-    ts(o, ap("RS", 64, 128), 0.0, A.is_gt)
+    ts(ap("RS"), o, MAG, A.add, MAG, A.subtract)
+    tt(o, o, ap("RS"), A.is_gt)
     tt(o, o, ap("KD"), A.mult)
     tt(ap("YK", 0, 64), o, ap("KS", 0, 64), A.add)
     tt(ap("YK", 64, 128), ap("KS", 64, 128), o, A.subtract)

from concourse.bass import DstId, RemoteDMATransfer
from concourse.mybir import AluOpType as A, ActivationFunctionType as F, AxisListType

C, NV, LN, RO, L, N = 3072, 1024, 96, 4, 192, 6
B0 = C - LN * RO
XW, RW, IW = 3280, 1408, 3088
MAG = 12582912.0
M30 = 1.5 * 2.0 ** 30
UP, EPS = 64.0, 1.0 / 16
HN = 1536.0
BIG = 2.0 ** 70
TOP = 1792.0
PEF = 0.51
SVS = (96, 96)
VUS = (0, 0)
VSC = (0, 0, 0, 1)
DVS, DUS = (3, 3), (0, 0)
GIS, GLAT = 1200, 2.2
SV = max(SVS)
OW = 512 if max(VUS) else 256
IS = 1024
VBX = (L - min(SVS)) // 16
YB = ("P3", "P4", "P3")
YV = 640

bf, f32, i32, u16, f16 = "bfloat16", "float32", "int32", "uint16", "float16"
SB = dict(
    X=(XW, bf), R=(RW, f32), RI=(NV, i32), K2=(128, i32), KS=(128, f32), KD=(64, f32), YK=(128, f32),
    YR=(NV, f32), Y1=(NV - YV, f32), DM=(NV, f32), RS=(64, f32),
    IO=(IW, f32), RTI=(12, i32), FNI=(8, i32), SNI=(8, i32), FN16=(8, u16), SN16=(8, u16),
    W0=(L, bf), W1=(L, bf), W2=(L, bf), W3=(L, bf), SEND0=(LN, bf), SEND1=(LN, bf), SEND2=(LN, bf),
    WT=(128, bf), WS=(17 * VBX, f16), NF0=(LN, f16), NL=(384, f16), NB=(384, bf),
    O16=(384, u16), RV=(L, f32), NM=((24, 17), f16), FR=(L, bf), NEW=(384, f32),
    HI=((12, 17), bf), TL=(L, f16), DG=(LN, f32), TT=(384, f32), EB=(L, bf),
    ZV=(16 * SV, f16), MXV=(16 * SV, bf), MNV=(16 * SV, bf),
    ZH=(272 * VBX, f16), MW=(272 * 12, f16), ZU=(2048, f16), ZS=(3072, f16), MXS=(3072, bf), MNS=(3072, bf),
    MXH=(1536, f16), MNH=(1536, f16), MXU=(1536, f16), MNU=(1536, f16), DG16=(LN, f16), OFH=(512, f16),
    OFS=(OW, bf), OFL=(L, bf), O17=(17 * VBX, bf), ONE=(384, bf),
    ST=(512, f32), RR=(32, f32), DIG=(32, bf), CS=(96, f32), C16=(12, u16), REP=(L, f16), REPA=(288, f16),
    E=((144, 17), bf), EA=((12, L), bf), SD=(204, f32), RDA=(204, f32), EF=(12, bf), T1=(12, f32), T2=(12, f32), XO16=(12, u16),
    T3=((2, 12), f32), T4=(24, f32), XC=(L, bf), VAL=(L, bf),
    HA=(384, bf), SG=(384, bf), A1=(LN, bf), SUM=(4, f32), THR=(4, f32),
    LV0=((3, 12), f32), LV1=((3, 12), f32), LV2=((3, 12), f32), U0=(36, u16), U1=(36, u16), U2=(36, u16),
    OF0=(24, u16), OF1=(24, u16), OF2=(24, u16), PN0=(L, bf), PN1=(L, bf), PN2=(L, bf), H1=(12, f32), H2=(12, f32),
    KG=(384, f16), KL=(48, f32), MH0=(48, f32), MH1=(48, f32), OO=(48, f32),
    KM=(24, f32), EA0=((12, L), bf), TL32=(L, f32), LMB=(208, bf),
    PI=(4, i32), COL=(16, f32), IF=(128, f32), NIF=(128, f32), IB=(128, bf), NI=(128, bf), IH=(128, f16), NO=(128, f16),
    N64=(128, bf), IN=(128, bf), IL=(128, bf), IQ=(128, bf), HP=(128, bf), HM=(128, bf), EP=(128, bf), EM=(128, bf), E3=(128, bf), E3P=(128, bf),
    IMAG=(128, bf), IME=(128, bf), IK0=(128, bf),
    WD=(144, bf), WM=(144, bf), WH=(144, bf), G4=(16, bf), GN=(16, bf),
    JB=(128, bf), BOP=(128, bf), BON=(128, bf), BOD=(128, bf), BOO=(128, bf), BN2=(128, bf), LM=(208, bf), CD=(204, bf), CDR=(L, bf),
    EX=(512, bf), LM1=(768, bf), LM64=(768, bf), PEN8=(48, bf), RS8=(48, bf), RT=(256, bf), MXR=(512, bf),
    MNR=(512, bf), DVU=(24, f32), PW=(16, f32),
)
SCRATCH, PLACE, _at = {}, {}, {f32: 0, bf: 0}
for _k, (_w, _d) in SB.items():
    if isinstance(_w, tuple):
        PLACE[_k] = (_k, 0, _w[0] * _w[1], _d, _w[1])
        SCRATCH[_k] = ("sbuf", [128, _w[0], _w[1]], _d)
    elif (_d == f32 and _w <= 96) or (_d == bf and _w == 128):
        PLACE[_k] = ("SMALL" + _d, _at[_d], _w, _d, 0)
        _at[_d] += (_w + 7) // 8 * 8
    else:
        PLACE[_k] = (_k, 0, _w, _d, 0)
        SCRATCH[_k] = ("sbuf", [128, _w], _d)
for _d in _at:
    SCRATCH["SMALL" + _d] = ("sbuf", [128, _at[_d]], _d)
for _b in range(8):
    SCRATCH["P%d" % _b] = ("psum", [128, 512], "float32")
    PLACE["P%d" % _b] = ("P%d" % _b, 0, 512, f32, 0)
LOADS = ["ring", "x", "rt", "xl", "fn", "k0", "k1", "k2", "k3", "snd"]
STORES = ["yx", "yr0", "yr1", "y0", "y1"]
SEMAPHORES = ["sV", "sS", "sP", "sG", "sent", "arr0", "arr1", "arr2"] + ["d" + n for n in LOADS + STORES]
SEMAPHORES += ["aZV%d" % i for i in range(max(DVS))] + ["aZS%d" % i for i in range(max(DUS))]
CYC = 0.83e-3
FAC, GAT, SCA = 1.02, 1.59, 3.9


def build(T, topo, rank):
    ops, used = [], {}

    def cut(a, b, s):
        return slice(a, b) if s == 1 else slice(a, b, s) if s > 0 else slice(b - 1, a - 1 if a else None, s)

    def ap(name, a=0, b=None, s=1, p=None):
        buf, at, width, dt, pitch = PLACE[name]
        if b is None:
            b = width
        if pitch:
            if a // pitch == (b - 1) // pitch:
                return rows(name, a // pitch, a // pitch + 1, a % pitch, b - a // pitch * pitch, s, p)
            return rows(name, a // pitch, b // pitch, 0, pitch, s, p)
        part = slice(0, 128) if p is None else slice(p[0], p[1])
        return dict(v=T[buf][part, cut(at + a, at + b, s)], n=len(range(a, b, abs(s))), r=[(name, a, b)], dt=dt, ps=is_bank(name))

    def rows(name, r0, r1, a, b, s=1, p=None):
        buf, at, width, dt, pitch = PLACE[name]
        part = slice(0, 128) if p is None else slice(p[0], p[1])
        v = T[buf][part, r0 if r1 - r0 == 1 else cut(r0, r1, 1 if s > 0 else -1), cut(a, b, s)]
        return dict(v=v, n=(r1 - r0) * len(range(a, b, abs(s))), r=[(name, pitch * r + a, pitch * r + b) for r in range(r0, r1)], dt=dt, ps=is_bank(name))

    def lanes(name, a, b, r0=0):
        return rows(name, r0 + a // 16, r0 + b // 16, 0, 16)

    def slot(name, r0, r1, k):
        x = ap(name, 272 * r0 + k, 272 * r1, 16)
        return dict(x, r=[("MW%d" % k, r0, r1)]) if name == "MW" else x

    def ind(name, a, b, off):
        return dict(v=T[name][:, a:b].indirect(off["v"]), n=16 * off["n"], r=[(name, a, b)], o=off["r"], dt=SCRATCH[name][2], ps=False, ind=1)

    def val(x):
        return x["v"] if isinstance(x, dict) else x

    def add(eng, fn, ins, outs, cost, acc=False, sem=None, lat=0.0):
        rd, wr = [], []
        for x in ins:
            if isinstance(x, dict):
                rd += x["r"] + x.get("o", [])
        for x in outs:
            wr += x["r"]
            rd += x.get("o", [])
        t = (cost[0] * FAC + cost[1] * GAT + cost[2] * SCA + cost[3] + cost[4] * PEF) * CYC
        ops.append(dict(e=eng, fn=fn, rd=rd, wr=wr, t=t, c=cost, acc=acc, sem=sem, lat=lat))

    def vcost(out, ins, rate=None):
        n = ins[0]["n"] if ins else out["n"]
        if "ind" in out:
            return (0, 0, n, 60, 0)
        if ins and "ind" in ins[0]:
            return (0, n, 0, 60, 0)
        if rate is None:
            rate = 0.5 if all(x["dt"] in (bf, u16, f16) for x in ins + [out]) else 1.0
        return (max(64, n * rate), 0, 0, 0, 0)

    def copy(out, a):
        add("V", lambda g: g.vector.tensor_copy(out["v"], a["v"]), [a], [out], vcost(out, [a]))

    def tt(out, a, b, op):
        add("V", lambda g: g.vector.tensor_tensor(out["v"], a["v"], b["v"], op), [a, b], [out],
            vcost(out, [a, b], 1.0 if a["ps"] or b["ps"] else 2.0))

    def ts(out, a, s1, op0, s2=None, op1=None):
        if op1 is None:
            fn = lambda g: g.vector.tensor_scalar(out["v"], a["v"], val(s1), None, op0)
        else:
            fn = lambda g: g.vector.tensor_scalar(out["v"], a["v"], val(s1), val(s2), op0, op1)
        add("V", fn, [a, s1, s2], [out], vcost(out, [a]))

    def scan(out, d0, d1, op0, op1, init=0.0):
        add("V", lambda g: g.vector.tensor_tensor_scan(out["v"], d0["v"], d1["v"], init, op0, op1), [d0, d1], [out], vcost(out, [d0, d1]))

    def mset(out, c):
        add("V", lambda g: g.vector.memset(out["v"], c), [], [out], vcost(out, []))

    def act(out, a, func, bias=0.0, scale=1.0, accum=None):
        if accum is None:
            fn = lambda g: g.scalar.activation(out["v"], a["v"], func, bias=val(bias), scale=val(scale))
        else:
            fn = lambda g: g.scalar.activation(out["v"], a["v"], func, bias=val(bias), scale=val(scale), accum_out=accum["v"])
        if "ind" in out:
            fn = lambda g: g.scalar.activation(out["v"], a["v"], func)
        cost = (0, 0, a["n"], 80, 0) if "ind" in out else (0, a["n"], 0, 80, 0) if "ind" in a else (max(64, a["n"]) + (25 if accum else 0), 0, 0, 0, 0)
        add("S", fn, [a, bias, scale], [out] + ([accum] if accum else []), cost)

    def mm(out, lhsT, rhs, start, stop):
        cyc = max(min(64, lhsT["n"]), rhs["n"]) * (4 if rhs["dt"] == f32 else 1)
        add("P", lambda g: g.tensor.matmul(out["v"], lhsT["v"], rhs["v"], start, stop), [lhsT, rhs], [out], (0, 0, 0, 0, cyc), acc=True)

    def group(items):
        for i, (o, l, r) in enumerate(items):
            mm(o, l, r, i == 0, i == len(items) - 1)

    def iota(out, pat, base=0, cm=0):
        if out["dt"] == i32:
            fn = lambda g: g.iota(out["v"], pat, base, cm)
        else:
            fn = lambda g: g.iota(out["v"], pat, base, cm, allow_small_or_imprecise_dtypes=True)
        add("G", fn, [], [out], (157 + 2 * out["n"], 0, 0, 0, 0))
        ops[-1]["chain"] = "G"

    def pick(out, a, pat, base):
        add("G", lambda g: g.affine_select(out["v"], a["v"], pat, A.is_equal, 0.0, base, 0), [a], [out], (205 + 2 * out["n"], 0, 0, 0, 0))

    def dma(q, name, out, in_, rd, wr, us):
        eng = (lambda g: g.sync) if q == "Y" else (lambda g: g.scalar)
        add(q, lambda g: eng(g).dma_start(out, in_), rd, wr, (0, 0, 0, 80, 0), sem="d" + name, lat=us)
        if wr:
            ops[-1]["chain"] = q

    col = lambda j: ap("COL", j, j + 1)
    PK = (0, 102)
    kin = [("RI", 0, NV), ("RI1", 0, NV)]
    dma("Y", "ring", T.RI[:], T.ring[:], [], [ap("RI")], 3.0)
    dma("S", "rt", T.RTI[:], T.rt[:], [], [ap("RTI")], 2.0)
    dma("Y", "x", T.X[:, 0:C], T.x[:], [], [ap("X", 0, C)], 5.0)
    dma("S", "xl", T.W0[:, 0:LN], T.xl[:], [], [ap("W0", 0, LN)], 2.2)
    dma("S", "fn", T.FNI[:, 0:6], T.fn[:], [], [ap("FNI")], 2.2)
    dma("Y", "snd", T.SNI[:, 0:6], T.snd[:], [], [ap("SNI")], 2.2)
    dma("Y", "k2", T.K2[:, 0:64], T.kid[:, 0:512], [], [ap("K2", 0, 64)], 2.5)
    dma("Y", "k3", T.K2[:, 64:128], T.kid[:, 512:NV], [], [ap("K2", 64, 128)], 2.5)
    iota(ap("PI", 0, 1), [[1, 1]], 0, 1)
    iota(ap("IO", 0, 256), [[1, 256]])
    iota(ap("JB"), [[16, 8], [0, 16]])
    iota(ap("LM"), [[0, 13], [1, 16]])
    iota(ap("O17"), [[0, VBX], [-256, 17]], int(TOP))
    iota(ap("OFS"), [[0, OW // 256], [-256, 16], [0, 16]], int(TOP))
    iota(ap("EX", p=(0, SV)), [[1, 32], [0, 16]])
    iota(ap("G4"), [[0, 2], [16, 8]])
    iota(ap("OFL"), [[0, 12], [-256, 16]], int(TOP))
    iota(ap("NB"), [[1, 384]], -192)
    iota(ap("LM64", p=PK), [[-17, 6], [0, 8], [-1, 16]], 0, 1)
    iota(ap("PEN8"), [[0, 6], [16, 8]])
    iota(ap("CD"), [[0, 12], [1, 17]])
    iota(ap("IO", IS, IW), [[1, IW - IS]], IS)
    mset(ap("O17", 16, 17 * VBX, 17), 2048.0)
    for a in (0, 256):
        copy(ap("OFH", a, a + 256), ap("OFS", 0, 256))
    mset(ap("ONE"), 1.0)
    act(ap("NEW"), ap("ONE"), F.Identity)
    act(ap("R", NV, RW), ap("NEW"), F.Silu)
    ops[-1]["t"] += 1.3
    ops[-1]["tab"] = 1
    for a, n in ((256, 256), (512, IS - 512)):
        act(ap("IO", a, a + n), ap("IO", 0, n), F.Identity, bias=float(a))
    for j, m in ((1, 15), (2, 31)):
        ts(ap("PI", j, j + 1), ap("PI", 0, 1), m, A.bitwise_and)
    copy(ap("COL", 0, 3), ap("PI", 0, 3))
    tt(col(4), col(0), col(1), A.subtract)
    ts(col(5), col(4), 15.0, A.add)
    ts(ap("IB"), ap("IO", 0, 128), col(0), A.is_equal)
    for name, sc in (("NI", -1.0), ("N64", -64.0), ("HP", 0.5), ("HM", -0.5), ("EP", EPS / 2), ("EM", -EPS / 2), ("E3", -1.5 * EPS), ("E3P", 1.5 * EPS),
                     ("IN", -16384.0), ("IL", 1344.0), ("IQ", -2.0 ** 19), ("IMAG", MAG), ("IME", MAG * EPS), ("IK0", HN + UP),
                     ("IH", 0.5 - 2.0 ** -11), ("NO", 2.0 ** -10 - 1)):
        ts(ap(name), ap("IB"), sc, A.mult)
    act(ap("IF"), ap("IB"), F.Identity)
    act(ap("NIF"), ap("IB"), F.Identity, scale=-1.0)
    ts(ap("WD"), ap("IO", 0, 144), col(5), A.is_equal)
    ts(ap("GN"), ap("G4"), col(4), A.is_equal, -2048.0, A.mult)
    ts(ap("G4"), ap("G4"), col(4), A.is_equal, 4096.0, A.mult)
    ts(ap("JB"), ap("JB"), col(4), A.is_equal)
    ts(ap("LM"), ap("LM"), col(1), A.is_equal)
    mset(ap("MXR"), 0.0)
    mset(ap("MXR", s=16), -1024.0)
    ts(ap("EB"), ap("MXR", 0, L), 2.0 ** 19, A.mult)
    mset(ap("XC"), 0.5)
    scan(ap("CDR"), ap("XC"), ap("EB"), A.mult, A.min)
    tt(ap("PW"), ap("CDR", 0, 16), ap("LM", 0, 16), A.mult)
    add("V", lambda g: g.vector.tensor_reduce(col(10)["v"], ap("PW")["v"], AxisListType.X, A.add), [ap("PW")], [col(10)], (64, 0, 0, 0, 0))
    ts(col(6), col(10), -0.5, A.mult)
    ts(ap("CD"), ap("CD"), col(1), A.not_equal, -BIG, A.mult)
    ts(ap("CD"), ap("CD"), col(10), A.min)
    mset(ap("CD", 16, 204, 17), HN)
    for name, sc in (("BOO", 2.0 ** 40), ("BOD", col(6)), ("BOP", 16384.0), ("BON", -16384.0), ("BN2", -2048.0)):
        act(ap(name), ap("JB"), F.Identity, scale=sc)
    ts(ap("EX", p=(0, SV)), ap("EX", p=(0, SV)), ap("COL", 2, 3, p=(0, SV)), A.is_equal, -1.0, A.mult)
    ts(ap("LM1", p=PK), ap("LM64", p=PK), 0.0, A.is_equal)
    ts(ap("LM64", p=PK), ap("LM64", p=PK), 0.0, A.is_equal, 64.0, A.mult)
    ts(ap("PEN8"), ap("PEN8"), col(4), A.not_equal, 2.0 ** 20, A.mult)
    ts(ap("PEN8"), ap("PEN8"), -HN, A.add)
    for name, n, st, sc, b in (("RS8", 48, 2, -4096.0, 0.0), ("RT", 256, 1, -2.0 ** 20, -128.0), ("MNR", 512, 1, -1.0, 0.0)):
        act(ap(name), ap("MXR", 0, n * st, st), F.Identity, scale=sc, bias=b)
    mset(ap("X", C, XW), 0.0)
    for b in range(12):
        if b < VBX:
            mset(ap("ZH", 272 * b + 256, 272 * b + 272), 0.0)
        if b >= (L - SV) // 16:
            act(dict(ap("MW", 272 * b + 256, 272 * b + 272), r=[("MW%d" % k, b, b + 1) for k in range(16)]), ap("ONE", 0, 16), F.Identity)
    mset(rows("E", 0, 144, 16, 17), 0.0)
    mset(rows("NM", 0, 12, 16, 17), 0.0)
    mset(rows("HI", 0, 12, 16, 17), 0.0)
    mset(ap("RDA"), BIG)
    mset(ap("RDA", 0, 204, 17), -4 * BIG)
    ts(ap("RDA", 16, 204, 17), ap("IO", 0, L, 16), col(1), A.add, float(C + 1), A.add)
    ts(ap("DVU"), ap("IO", 0, 384, 16), col(1), A.add, float(NV), A.add)
    ts(ap("NL"), ap("NB"), B0 + 192 - HN, A.add)
    act(ap("R", 0, 512), dict(ap("RI", 0, 512), r=kin), F.Identity, bias=UP - EPS)
    ts(ap("R", 512, NV), dict(ap("RI", 512, NV), r=kin), UP + EPS, A.add)
    copy(ap("FN16", 0, 6), ap("FNI", 0, 6))
    copy(ap("SN16", 0, 6), ap("SNI", 0, 6))

    def to_list(out, src, n):
        group([(out, ap("WD", 15 - q, 143 - q), ap(src, q, n, 16)) for q in range(16)])

    def nodes(k, v):
        lv, u = "LV%d" % k, "U%d" % k
        ts(ap("H1"), v, 512.0, A.is_ge, -512.0, A.mult)
        ts(ap("H2"), v, 512.0, A.is_lt, 512.0, A.mult)
        tt(ap(lv, 24, 36), v, ap("H1"), A.add)
        tt(ap(lv, 12, 24), ap(lv, 24, 36), ap("H2"), A.add)
        if k:
            copy(ap(u, 0, 12), v)
            copy(ap(u, 12, 36), ap(lv, 12, 36))
        else:
            copy(ap(u), ap(lv))

    def pairs(k):
        lv, u = "LV%d" % k, "U%d" % k
        act(ap("REPA", 0, L), ind("IO", 0, 512, ap(u, 24, 36)), F.Identity)
        if k == 0:
            act(ap("REPA", L, 288), ap("REPA", 0, LN), F.Identity)
        for m in range(12):
            e = 288 if k == 0 and m >= 6 else L
            ts(rows("EA" if k else "EA0", m, m + 1, 0, e - 16 * m), ap("REPA", 16 * m, e), ap(lv, 24 + m, 25 + m), A.is_equal)

    def acting(k, bank):
        lv, of, pn = "LV%d" % k, "OF%d" % k, "PN%d" % k
        items, ea = [(ap(bank, 0, L), ap("IB"), ap("CDR"))], "EA" if k == 2 else "EA0"
        for m in range(12):
            h = m // 6
            at, e = (LN - 2 * LN * h, LN + LN * h) if k == 1 else (0, L)
            if 16 * m + 16 < e:
                items.append((ap(bank, at + 16 * m + 16, at + e), ap("BOO"), rows(ea, m, m + 1, 16, e - 16 * m)))
            if k == 1 and h:
                items.append((ap(bank, LN, L), ap("BOO"), rows(ea, m, m + 1, L - 16 * m, 288 - 16 * m)))
            if m % 6 == 5:
                items.append((ap(bank, at + LN * h, at + LN * h + LN), ap("BOD"), rows(ea, m - 5, m + 1, 0, 16)))
        group(items)
        act(ap(pn), ap(bank, 0, L), F.Relu)
        lose = ap(bank, L, L + 12)
        to_list(lose, pn, L)
        tt(rows("T3", 0, 2, 0, 6), lose, ap("KL", 3, 48, 4) if k == 2 else ap(lv, 0, 12), A.max)
        tt(rows("T3", 0, 2, 6, 12), lose, ap(lv, 12, 24), A.max)
        tt(ap("T4"), ap("T3"), ap("DVU"), A.min)
        copy(ap(of), ap("T4"))

    copy(ap("LV0", 0, 12), ap("RTI"))
    nodes(0, ap("LV0", 0, 12))
    pairs(0)
    acting(0, "P7")

    def kids():
        dma("Y", "k0", T.RI[0:128:16, :], T.kid[0:16:2, :], [], [ap("RI")], 2.5)
        dma("Y", "k1", T.RI[1:128:16, :], T.kid[1:16:2, :], [], [dict(r=kin[1:])], 2.5)
        copy(ap("KG"), dict(ind("RI", 0, NV, ap("U0", 0, 24)), r=kin))
        ts(col(7), col(1), 2.0, A.is_lt, 0.25, A.mult)
        ts(col(8), col(1), 0.5, A.mult, -0.25, A.add)
        tt(col(9), col(8), col(7), A.mult)
        act(ap("WM"), ap("WD"), F.Identity, scale=col(7))
        ts(ap("WH"), ap("WD"), col(9), A.mult, 4.0, A.mult)
        for j, w in enumerate(("WM", "WH")):
            group([(ap("P6", 24 * j, 24 * j + 24), ap(w, 15 - q, 143 - q), ap("KG", q, 384, 16)) for q in range(16)])
        act(ap("KL"), ap("P6", 0, 48), F.Identity)
        ts(ap("T1"), ap("LV0", 0, 12), 512.0, A.is_ge, 2.0, A.mult)
        ts(ap("T2"), ap("T1"), -1.0, A.add)
        for j in range(2):
            tt(ap("MH0", 3 - j, 48, 4), ap("KL", 24 * j, 24 * j + 12), ap("KL", 24 * j + 12, 24 * j + 24), A.add)
            tt(ap("KM", 12 * j, 12 * j + 12), ap("KL", 24 * j, 24 * j + 12), ap("KL", 24 * j + 12, 24 * j + 24), A.subtract)
            tt(ap("MH0", j, 48, 4), ap("KM", 12 * j, 12 * j + 12), ap("T2"), A.mult)
        act(ap("MH1", 0, 24), ap("MH0", 24, 48), F.Identity)
        act(ap("MH1", 24, 48), ap("MH0", 0, 24), F.Identity)
        mset(ap("OO", 0, 48, 4), 0.0)

    def level(t, l):
        k = (t & 1) if l == 0 else 2
        U, OF, PN, W = "U%d" % k, "OF%d" % k, "PN%d" % k, "W%d" % t
        nameF = ap("NF0") if t == 0 else ap("NL", LN * t - LN, LN * t)
        begin, last = t == 0 and l == 0, t == RO - 1 and l == 1
        SL, VU = SVS[l], VUS[l]
        VV, VB = L - SL, (L - SL) // 16
        NM = lambda a, b: lanes("NM", a, b)
        for a in (0, 12):
            if begin:
                copy(ap("O16", 16 * a, 16 * a + L), dict(ind("RI", 0, NV, ap(U, a, a + 12)), r=kin))
            else:
                ts(ap("O16", 16 * a, 16 * a + L), ind("R", 0, RW, ap(U, a, a + 12)), 0.25 - UP, A.add)
        X = lambda a, b: ind("X", 0, XW, ap("O16", a, b))

        def ends(z, n, mx, mn):
            scan(mx, z(0, n, -2), z(0, n - 1, -2), A.max, A.max, -4096.0)
            scan(mn, z(0, n, 2), z(1, n, 2), A.min, A.min, 4096.0)

        def stepped(z, mx, mn, o0, blocks):
            n = 1 if z == "ZH" else 2
            for b in blocks:
                tt(ap(z, 272 * b, 272 * b + 256) if n == 1 else ap(z, 256 * b, 256 * b + 512), X(o0 + 16 * b, o0 + 16 * (b + n)), ap("OFS", 0, 256 * n), A.add)
                for j in range(b, b + n):
                    a = 272 * j if n == 1 else 256 * j
                    ends(lambda c, e, s: ap(z, a + c, a + e, s), 256, ap(mx, 128 * j, 128 * j + 128, -1), ap(mn, 128 * j, 128 * j + 128))

        def gathered(z, a, o0):
            act(ap(z, 16 * a, 16 * a + 512), X(o0, o0 + 32), F.Identity)

        def extremes(z, a, w0, n, mx, mn, px, pn):
            at = lambda name: ap(name, 16 * a, 16 * a + 512)
            if w0 < n:
                sem = "a%s%d" % (z, a // 32)
                used[sem] = used.get(sem, 0) + 16
                add("G", lambda g: g.dma_start(at(z)["v"], ap("OFH")["v"], accum_op=A.add), [at(z), ap("OFH")], [at(z)], (0, 0, 0, GIS, 0), sem=sem, lat=GLAT)
                ops[-1]["cnt"] = used[sem]
                for j in (0, 1):
                    c, e = 16 * a + 256 * j, 8 * w0 + 128 * j
                    ends(lambda x, y, s: ap(z, c + x, c + y, s), 256, ap(mx, e, e + 128, -1), ap(mn, e, e + 128))
            else:
                scan(at(px), ap("MXR"), at(z), A.add, A.max)
                scan(at(pn), ap("MNR"), at(z), A.add, A.min)

        NV_, NU_ = VV + 32 * DVS[l], VU + 32 * DUS[l]

        def midrange(bank, c0, own, rounded, a=0, b=L):
            o = lambda a, b: ap(bank, c0 + a, c0 + b)
            items = [(o(a, b), ap("NI"), ap(W, a, b))]
            n, n0, mx, mn, px, pn = (NV_, VV, "MXH", "MNH", "MXV", "MNV") if own else (NU_, VU, "MXU", "MNU", "MXS", "MNS")
            e = min(n, b)
            if a < e:
                items += [(o(a, e), ap("NO"), ap("OFL", a, e)), (o(a, e), ap("IH"), ap(mx, 8 * a, 8 * e, 8)), (o(a, e), ap("IH"), ap(mn, 8 * a + 7, 8 * e, 8))]
            e = max(n, a)
            if e < b:
                items += [(o(e, b), ap("IH"), ap(m, 16 * (e - n0) + 15, 16 * (b - n0), 16)) for m in (px, pn)]
            if rounded:
                items.append((o(a, b), ap("IMAG"), ap("ONE", a, b)))
            group(items)

        stepped("ZH", "MXH", "MNH", 0, sorted(range(VB), key=lambda b: b < 6))
        for a in range(0, SL, 32):
            gathered("ZV", a, VV + a)
        act(ap("RV"), ind("R", 0, RW, ap(U, 0, 12)), F.Identity)
        ts(lanes("HI", 0, L), ap("O16", 0, L), 1.0 / 64, A.mult, 128.0, A.add)
        ts(NM(0, 384), ap("O16"), -HN, A.add)
        for c in range(SL // 32):
            o, q, b = ap(YB[c]), (SV - SL + 32 * c, SV - SL + 32 * c + 32), VB + 2 * c
            group([(o, ap("WT", p=q), ap("EX", p=q)), (o, ap("IB"), ap("ZV", 512 * c, 512 * c + 512))])
            for j in (0, 1):
                act(dict(ap("MW", 272 * (b + j), 272 * (b + j) + 256), r=[("MW%d" % s, b + j, b + j + 1) for s in range(16)]),
                    ap(YB[c], 256 * j, 256 * j + 256), F.Abs, scale=0.5)
            extremes("ZV", 32 * c, VV + 32 * c, NV_, "MXH", "MNH", "MXV", "MNV")
        for s in range(16):
            scan(slot("MW", 0, VB, s), slot("ZH", 0, VB, s), ap("WS", 0, 17 * VB), A.min, A.max, 4096.0)
        for h in (1, 0):
            bk, b0, b1 = "P%d" % h, 6 * h, min(6 * h + 6, VB)
            keys, pz = [], (0, 17 * (b1 - b0))
            if b0 < b1:
                keys += [(ap(bk, a, a + 128, p=pz), ap("WS", 17 * b0, 17 * b1), ap("BN2")) for a in (0, 128)]
                keys += [(ap(bk, s, 256, 16, p=pz), slot("ZH", b0, b1, s), ap("GN")) for s in range(16)]
            keys += [(ap(bk, s, 256, 16, p=PK), slot("MW", b0, b0 + 6, s), ap("G4")) for s in range(16)]
            hi = rows("HI", b0, b0 + 6, 0, 17)
            keys += [(ap(bk, 0, 128, p=PK), hi, ap("N64")), (ap(bk, 128, 256, p=PK), hi, ap("IB")),
                     (ap(bk, 0, 128, p=PK), rows("NM", b0, b0 + 6, 0, 17), ap("IB"))]
            group(keys)
            scan(ap("ST", 256 * h, 256 * h + 256, p=PK), ap("RT", p=PK), ap(bk, 0, 256, p=PK), A.add, A.min)
            ts(ap("RR", 16 * h, 16 * h + 16, p=PK), ap("ST", 256 * h + 15, 256 * h + 256, 16, p=PK), M30, A.add, M30, A.subtract)
            tt(ap("DIG", 16 * h, 16 * h + 16, p=PK), ap("ST", 256 * h + 15, 256 * h + 256, 16, p=PK), ap("RR", 16 * h, 16 * h + 16, p=PK), A.subtract)
            group([(ap(bk, 256, 304), ap("IB"), ap("PEN8"))]
                  + [(ap(bk, 256 + 8 * m, 264 + 8 * m), ap("LM64" if ab else "LM1", 128 * m, 128 * m + 128, p=PK),
                      ap("DIG", 16 * h + 8 * ab, 16 * h + 8 * ab + 8, p=PK)) for m in range(6) for ab in range(2)])
            scan(ap("CS", 48 * h, 48 * h + 48), ap("RS8"), ap(bk, 256, 304), A.add, A.min)
            ts(ap("C16", 6 * h, 6 * h + 6), ap("CS", 48 * h + 7, 48 * h + 48, 8), HN, A.add)
        nb = ap("NB", LN * t, LN * t + LN)
        group([(ap("P2", 0, 96), ap("IB"), NM(0, 96)), (ap("P2", 0, 96), ap("NI"), nb),
               (ap("P2", 96, L), ap("IB"), NM(L, 288)), (ap("P2", 96, L), ap("NI"), nb)])
        tt(ap("TL"), ap("P2", 0, L), ap("LM", t, t + L), A.mult)
        d, o = ap("P2", L, 288), ap("P2", 288, 480)
        dg, pos, neg = (ap("DG16"), ap("IB"), ap("NI")) if t else (ap("DG"), ap("IF"), ap("NIF"))
        if l == 0:
            group([(o, ap("IF"), ap("RV")), (o, ap("NI"), NM(0, L))])
            act(ap("SG", 0, L), o, F.Sign, bias=-HN - UP)
            group([(d, ap("IB"), NM(96, L)), (d, ap("NI"), nameF)])
        else:
            group([(o, ap("IF"), ap("RV")), (o, ap("NI"), NM(0, L)), (o, ap("IME"), ap("ONE", 0, L))])
            act(ap("FR"), o, F.Identity, bias=-HN - UP - MAG * EPS)
            group([(d, ap("IB"), NM(96, L)), (d, ap("NI"), nameF), (d, ap("IB"), ap("FR", 96, L))])
        act(ap("A1"), d, F.Abs)
        group([(d, ap("IQ"), ap("A1")), (d, ap("HM"), nameF)])
        act(dg, d, F.Relu, bias=(C - HN) / 2 + l * 2.0 ** 19 * EPS)
        hd, mid = (lambda j, n=1: ap("P7", LN * j, LN * (j + n))), (lambda j, n=1: ap("P5", LN * j, LN * (j + n)))
        own, riv = (lambda j: NM(LN * (j // 2), LN * (j // 2 + 1))), (lambda j: NM(L + LN * (j // 2), L + LN * (j // 2 + 1)))
        mk = lambda j: ap("FR" if l else "SG", LN * (j // 2), LN * (j // 2 + 1))
        group([(hd(j), ap("HP" if j % 2 else "HM"), own(j)) for j in range(4)] + [(hd(j), ap("HM" if j % 2 else "HP"), riv(j)) for j in range(4)]
              + [(hd(j), ap((("E3", "E3P"), ("NI", "IB"))[l][j % 2]), mk(j)) for j in range(4)]
              + [(hd(0), ap("HP"), ap("TL", 0, 96)), (hd(0), ap("HM"), ap("TL", 96, L)), (hd(2), neg, dg)])
        group([(mid(j), ap("HP"), x(j)) for x in (own, riv) for j in range(4)]
              + [(mid(0, 4), ap("IK0"), ap("ONE")), (mid(0), ap("IL"), ap("LM", t, t + 96))]
              + [(mid(j), ap("EP" if j % 2 else "EM"), mk(j)) for j in range(4) if l == 0]
              + [(mid(0), ap("HM"), ap("TL", 0, 96)), (mid(0), ap("HM"), ap("TL", 96, L)), (mid(2), pos, dg)])
        if l == 0:
            midrange("P6", L, True, False)
            act(ap("SG", L, 384), ap("P6", L, 384), F.Sign, scale=-1.0, bias=0.625)
        midrange("P4", 0, True, True)
        act(ap("HA", 0, L), ap("P4", 0, L), F.Abs, bias=-MAG)
        if l == 0:
            if t == 0:
                kids()
            to_list(ap("P6", 0, 24), "SG", 384)
            for j, a, c in ((2, 0, 0.0), (1, 12, -1.0), (3, 12, -1.0)):
                act(dict(ap("OO", j, 48, 4), r=[("OO%d" % j, 0, 1)]), ap("P6", a, a + 12), F.Sign, bias=c)
            scan(ap("KL"), dict(ap("OO"), r=[("OO", 0, 48)] + [("OO%d" % j, 0, 1) for j in (1, 2, 3)]), ap("MH%d" % k), A.mult, A.add)
            nodes(2, ap("KL", 3, 48, 4))
        stepped("ZU", "MXU", "MNU", L, range(0, VU // 16, 2))
        for a in range(0, L - VU, 32):
            gathered("ZS", a, L + VU + a)
            extremes("ZS", a, VU + a, NU_, "MXU", "MNU", "MXS", "MNS")
        names = ap("CS", 7, 96, 8)
        act(ap("EF"), names, F.Relu, scale=4 * BIG, bias=-(C - HN - 0.5) * 4 * BIG)
        act(ap("XC"), ind("X", 0, XW, ap("C16")), F.Identity)
        items = [(ap("P2", 0, 204), ap("IB"), ap("CD"))]
        for m in (6, 7, 8, 9, 10, 11, 0, 1, 2, 3, 4, 5):
            if m % 6 == 0:
                act(ap("REP", 16 * m, 16 * m + 96), ind("IO", 0, IW, ap("C16", m, m + 6)), F.Identity, bias=-HN)
            ts(rows("E", 12 * m, 11 * m + 12, 0, 16), ap("REP", 16 * m, L), ap("CS", 8 * m + 7, 8 * m + 8), A.is_equal)
            if m < 11:
                items.append((ap("P2", 17 * m + 17, 204), ap("BOO"), rows("E", 12 * m + 1, 11 * m + 12, 0, 17)))
            if m % 6 == 5:
                own = dict(rows("E", 0, 6, 0, 17), v=T.E[:, 12 * m - 60:12 * m + 1:12, :], r=[("E", 204 * j, 204 * j + 17) for j in range(m - 5, m + 1)])
                items.append((ap("P2", 17 * m - 85, 17 * m + 17), ap("BOD"), own))
            if m == 0:
                items += [(ap("P2", 16, 204, 17), ap("IF"), names), (ap("P2", 0, 204, 17), ap("IB"), ap("EF"))]
        group(items)
        scan(ap("SD"), ap("RDA"), ap("P2", 0, 204), A.min, A.max)
        copy(ap("XO16"), ap("SD", 16, 204, 17))
        o = ap("P6", 0, L)
        group([(o, ap("IH"), ap(x)) for x in (W, "XC")] + [(o, ap("IMAG"), ap("ONE", 0, L))])
        act(ap("VAL"), o, F.Identity, bias=-MAG)
        copy(ind("X", 0, XW, ap("XO16")), ap("VAL"))
        if last:
            dma("Y", "yx", T.yx[:], T.X[:, 0:C], [ap("X", 0, C)], [], 4.0)
        elif l == 1:
            hand_on(t)
        if l == 0:
            pairs(2)
            acting(2, "P6")
        for i in range(2):
            a, b = LN * i, LN * i + LN
            midrange("P3", 0, False, True, a, b)
            act(ap("HA", L + a, L + b), ap("P3", a, b), F.Abs, bias=-MAG)
            o = ap("P4", L + a, L + b)
            group([(o, ap("IN"), ap(PN, a, b)), (o, ap("BOP"), ap("HA", a, b)), (o, ap("BON"), ap("HA", L + a, L + b))])
            act(ap("EB", a, b), o, F.Sign, bias=-8192.0 if begin else ap("THR", 1, 2), accum=None if last else ap("SUM", i, i + 1))
            for j in (2 * i, 2 * i + 1):
                tt(ap("TT", LN * j, LN * j + LN), hd(j), ap("EB", a, b), A.mult)
            new, to = ap("NEW", 2 * a, 2 * b), ind("R", 0, RW, ap(OF, 12 * i, 12 * i + 12))
            if VSC[2 * l + i]:
                act(new, mid(2 * i, 2), F.Identity)
                tt(to, new, ap("TT", 2 * a, 2 * b), A.add)
            else:
                tt(new, mid(2 * i, 2), ap("TT", 2 * a, 2 * b), A.add)
                act(to, new, F.Silu)
        for i in range(0 if last else 2):
            act(ap("THR", i, i + 1), ap("SUM", i, i + 1), F.Identity, scale=-8192.0, bias=ap("THR", 0, 1) if i else -8192.0 * (L + 1))

    def shares(r):
        me = T.cores[r]
        ds = sorted(range(1, N), key=lambda d: len(topo.engines(me, T.cores[(r + d) % N])))
        used, res = set(), {}
        for i, d in enumerate(ds):
            allowed = topo.engines(me, T.cores[(r + d) % N])
            free = [e for e in allowed if e not in used]
            rivals = sum(1 for d2 in ds[i:] if topo.engines(me, T.cores[(r + d2) % N]) == allowed)
            n = 1
            while 2 * n * rivals <= len(free):
                n *= 2
            res[d] = free[:n]
            used.update(res[d])
        return res

    def hand_on(t):
        snd, land = "SEND%d" % t, "W%d" % (t + 1)
        p0 = B0 + LN * t
        if t == 0:
            act(ap("SEND1"), ind("X", 0, XW, ap("FN16", 0, 6)), F.Identity)
            act(ap(snd), ind("SEND1", 0, LN, ap("SN16", 0, 6)), F.Identity)
        else:
            act(ap(snd), ind("X", p0 - LN, p0, ap("SN16", 0, 6)), F.Identity)
        mine = shares(rank)

        def send(g):
            tr = []
            for d in range(1, N):
                rid, pid, _ = topo.addr(T.cores[(rank + d) % N])
                tr.append(RemoteDMATransfer(dst_ids=[DstId(rid=rid, pnc=pid)], dma_engine_mask=sum(1 << e for e in mine[d]),
                                            remote_sem=T.sem["arr%d" % t], src=T[snd][:, 16 * d:16 * d + 16], dst=T[land][:, 16 * d:16 * d + 16]))
            g.remote_dma_fused(tr, local_sem=T.sem.sent)
            return None
        add("G", send, [ap(snd)], [dict(r=[("wire", t, t + 1)])], (0, 0, 0, 600, 0), sem="", lat=2.5)
        ops[-1]["sent"] = sum(len(v) for v in mine.values())
        act(ap(land, 0, 16), ap(snd, 0, 16), F.Identity)
        ops.append(dict(e="X", fn=None, rd=[("wire", t, t + 1)], wr=[(land, 16, LN)], t=0.0, c=(0, 0, 0, 0, 0), acc=False, lat=0.0, sem="arr%d" % t,
                        cnt=sum(len(shares((rank - d) % N)[d]) for d in range(1, N))))

    for a in range(8):
        pick(ap("DM", 128 * a, 128 * a + 128), ap("IF"), [[0, 16], [1, 8]], -a)
    for t in range(RO):
        p0, W = B0 + LN * t, "W%d" % t
        if t > 0:
            act(ap(W, LN, L), ap("X", p0 - LN, p0), F.Identity)
        act(ap("X", p0, p0 + LN), ap(W, 0, LN), F.Identity)
        if t == 0:
            act(ap(W, LN, L), ind("X", 0, XW, ap("FN16", 0, 6)), F.Identity)
            act(ap("NF0"), ind("IO", 0, IW, ap("FN16", 0, 6)), F.Identity, bias=-HN)
        for q in range(SV // 32):
            mm(ap("P6", 0, 128, p=(32 * q, 32 * q + 32)), ap(W, L - SV + 32 * q, L - SV + 32 * q + 32), ap("IB"), True, True)
        act(ap("WT", p=(0, SV)), ap("P6", 0, 128, p=(0, SV)), F.Identity)
        o = ap("P6", 128, 128 + 17 * VBX)
        group([(o, ap("IB"), ap("O17"))] + [(ap("P6", 128 + 17 * b, 144 + 17 * b), ap("IB"), ap(W, 16 * b, 16 * b + 16)) for b in range(VBX)])
        act(ap("WS"), o, F.Identity)
        level(t, 0)
        if t == 1:
            copy(ap("KS"), ap("K2"))
            tt(ap("KD"), ap("KS", 64, 128), ap("KS", 0, 64), A.subtract)
        level(t, 1)
        if t == 0:
            copy(rows("LV1", 0, 3, 0, 6), rows("LV0", 0, 3, 6, 12))
            copy(rows("LV1", 0, 3, 6, 12), rows("LV0", 0, 3, 0, 6))
            copy(ap("U1"), ap("LV1"))
            acting(1, "P1")
    ts(ap("YR", 0, YV), ap("R", 0, YV), MAG, A.add, MAG + UP, A.subtract)
    dma("Y", "yr0", T.yr[:, 0:YV], T.YR[:, 0:YV], [ap("YR", 0, YV)], [], 2.5)
    act(ap("Y1"), ap("R", YV, NV), F.Identity, bias=MAG)
    act(ap("YR", YV, NV), ap("Y1"), F.Identity, bias=-MAG - UP)
    dma("S", "yr1", T.yr[:, YV:NV], T.YR[:, YV:NV], [ap("YR", YV, NV)], [], 2.5)
    o = ap("P2", 0, 64)
    group([(o, ap("DM", 128 * a, 128 * a + 128), ap("R", 64 * a, 64 * a + 64)) for a in range(8)])
    ts(ap("RS"), o, MAG, A.add, MAG, A.subtract)
    tt(o, o, ap("RS"), A.is_gt)
    tt(o, o, ap("KD"), A.mult)
    tt(ap("YK", 0, 64), o, ap("KS", 0, 64), A.add)
    tt(ap("YK", 64, 128), ap("KS", 64, 128), o, A.subtract)
    dma("Y", "y0", T.yk[:, 0:512], T.YK[:, 0:64], [ap("YK", 0, 64)], [], 2.0)
    dma("S", "y1", T.yk[:, 512:NV], T.YK[:, 64:128], [ap("YK", 64, 128)], [], 2.0)
    return ops


def is_bank(name):
    return name[0] == "P" and name[1:].isdigit()


def edges(ops):
    hist, deps = {}, []
    for i, o in enumerate(ops):
        d = {}
        for kind, regs in (("r", o["rd"]), ("w", o["wr"])):
            for (nm, a, b) in regs:
                h = hist.setdefault(nm, [])
                bank = is_bank(nm)
                for (j, k2, a2, b2) in h:
                    if j == i:
                        continue
                    hit = (a < b2 and a2 < b) or (a, b) == (a2, b2)
                    if hit and (k2 == "w" or kind == "w"):
                        d[j] = d.get(j, False) or not (o["acc"] and ops[j]["acc"])
                if bank and h:
                    d.setdefault(h[-1][0], False)
        for kind, regs in (("r", o["rd"]), ("w", o["wr"])):
            for (nm, a, b) in regs:
                h = hist[nm]
                if kind == "w":
                    h[:] = [x for x in h if not (a <= x[2] and x[3] <= b and x[3] > x[2])]
                h.append((i, kind, a, b))
        deps.append(d)
    return deps


HOP, SELF, PASSES = 0.23, 0.23, 6
LOOKS = ((0.0, 0.0), (0.5, 0.3), (0.3, 0.1), (0.7, 0.7))


def schedule(ops, deps):
    n = len(ops)
    pred, succ, prev = [{} for _ in range(n)], [{} for _ in range(n)], {}
    for i, o in enumerate(ops):
        for j, hard in deps[i].items():
            far = ops[j]["e"] != o["e"] or ops[j]["sem"] is not None
            pred[i][j] = HOP + ops[j]["lat"] if far else SELF if hard else 0.0
        if "chain" in o:
            if o["chain"] in prev:
                pred[i].setdefault(prev[o["chain"]], 0.0)
            prev[o["chain"]] = i
        for j, gap in pred[i].items():
            succ[j][i] = gap

    def greedy(before, after, head, urgency, slack):
        left, est, ready, free, end, order = [len(p) for p in before], list(head), {}, {}, [0.0] * n, []
        for i in range(n):
            if left[i] == 0:
                ready.setdefault(ops[i]["e"], []).append(i)
        while len(order) < n:
            t, e = min((max(free.get(e, 0.0), min(est[i] for i in r)), e) for e, r in ready.items() if r)
            now = max((k for k in ready[e] if est[k] <= t + 1e-9), key=lambda k: urgency[k])
            i = max((k for k in ready[e] if est[k] <= t + 1e-9 + min(slack[1], slack[0] * ops[now]["t"])), key=lambda k: urgency[k])
            if urgency[i][0] - urgency[now][0] < est[i] - t:
                i = now
            end[i] = free[e] = max(est[i], free.get(e, 0.0)) + ops[i]["t"]
            ready[e].remove(i)
            order.append(i)
            for s, gap in after[i].items():
                est[s] = max(est[s], end[i] + gap)
                left[s] -= 1
                if left[s] == 0:
                    ready.setdefault(ops[s]["e"], []).append(s)
        return order, end

    tail, way, best = [o["lat"] for o in ops], [0.0] * n, None
    for j in range(n - 1, -1, -1):
        way[j] = ops[j]["t"] + max([tail[j]] + [gap + way[i] for i, gap in succ[j].items()])
    for slack in LOOKS:
        urgency = [(way[i], -i) for i in range(n)]
        for _ in range(PASSES):
            order, end = greedy(pred, succ, [0.0] * n, urgency, slack)
            span = max(end[i] + tail[i] for i in range(n))
            if best is None or span < best[0]:
                best = (span, order, end)
            back = greedy(succ, pred, tail, [(end[i], i) for i in range(n)], slack)[1]
            urgency = [(back[i], -i) for i in range(n)]
    return best[1], best[2]


def rank_program(g, core, T, topo):
    rank = T.rank_of(core)
    if rank is None:
        return
    ops = build(T, topo, rank)
    deps = edges(ops)
    order, _ = schedule(ops, deps)
    queue = {"V": g.vector, "S": g.scalar, "P": g.tensor, "G": g, "Y": g.sync}
    pos, cnt = {}, {}
    for i in order:
        pos[i] = cnt.get(ops[i]["e"], 0)
        cnt[ops[i]["e"]] = pos[i] + 1
    seen, waits, needed = {}, {}, set()
    for i in order:
        e = ops[i]["e"]
        if e == "X":
            continue
        w = {}
        for j, hard in deps[i].items():
            oj = ops[j]
            if oj["sem"] is not None:
                if (e, "dma", j) not in seen:
                    seen[(e, "dma", j)] = 1
                    w[("dma", j)] = j
            elif (oj["e"] != e or hard) and pos[j] > seen.get((e, oj["e"]), -1):
                if oj["e"] not in w or pos[j] > pos[w[oj["e"]]]:
                    w[oj["e"]] = j
        for k, j in w.items():
            if ops[j]["sem"] is None:
                seen[(e, k)] = pos[j]
                needed.add(j)
        waits[i] = list(w.values())
    count, tick, sent = {}, {}, 0
    for i in order:
        if i in needed:
            count[ops[i]["e"]] = tick[i] = count.get(ops[i]["e"], 0) + 1
    for i in order:
        o = ops[i]
        if o["e"] == "X":
            continue
        for j in waits[i]:
            oj = ops[j]
            if oj["sem"] is None:
                queue[o["e"]].wait_ge(T.sem["s" + oj["e"]], tick[j])
            else:
                queue[o["e"]].wait_ge(T.sem[oj["sem"]], oj.get("cnt", 16))
        ins = o["fn"](g)
        if o["sem"]:
            ins.then_inc(T.sem[o["sem"]], 16)
        elif i in needed:
            ins.then_inc(T.sem["s" + o["e"]], 1)
        sent += o.get("sent", 0)
    g.wait_ge(T.sem.sent, sent)
    for nm in STORES:
        g.wait_ge(T.sem["d" + nm], 16)
